import numpy as np, ml_dtypes
CORES = [5,29,101,125,133,157,229,253]
N = 8
import mx_ref
BF = ml_dtypes.bfloat16
def cols(t, e):
    v = np.concatenate([t.reshape(128, -1, 4), np.zeros((128, 1, 4), BF)], axis=1)
    return np.ascontiguousarray(v[:, e]).reshape(128, -1)
def pick(q, e):
    c = np.concatenate([q[0].reshape(128, -1, 4), np.zeros((128, 1, 4), np.uint8)], axis=1); s = np.concatenate([q[1], np.ones((16, 1), np.uint8)], axis=1)
    return (np.ascontiguousarray(c[:, e].reshape(128, -1)), np.ascontiguousarray(s[:, e]))
def join(*qs):
    return (np.concatenate([q[0] for q in qs], axis=1), np.concatenate([q[1] for q in qs], axis=1))
def put(q, e, v):
    c, s = q[0].reshape(128, -1, 4).copy(), q[1].copy(); c[:, e] = v[0].reshape(128, -1, 4); s[:, e] = v[1]
    return (c.reshape(128, -1), s)
def pk(c, s):
    return (np.ascontiguousarray(c), mx_ref.live(s))
def emit(q):
    return q[0], q[1]
def decode(q):
    o = []
    for b in range(4):
        e = np.zeros((128, 128, 4), np.float32); e[np.arange(128), np.arange(128), b] = 1
        o.append(mx_ref.matmul(mx_ref.quantize(e.reshape(128, 512).astype(BF)), q))
    return np.stack(o, axis=2).reshape(128, -1)
def f(rng, *shape):
    return mx_ref.flush((rng.standard_normal(shape, dtype=np.float32) * np.exp2(rng.integers(-2, 3, shape[:-1] + (1,)))).astype(BF))
def wide(rng, *shape, cols=0):
    v = rng.standard_normal(shape, dtype=np.float32) * np.exp2(rng.integers(-12, 13, shape)).astype(np.float32)
    if cols: v *= np.repeat(np.exp2(rng.integers(-cols, cols + 1, shape[:-2] + (1, shape[-1] // 4))) * (rng.random(shape[:-2] + (1, shape[-1] // 4)) > 0.0625), 4, axis=-1).astype(np.float32)
    return mx_ref.flush(v.astype(BF))
P, K, O = 96, 32, 1
def big(v):
    v = np.array(v.astype(np.float32))
    v[np.abs(v) < np.float32(2.0 ** -16)] = 0
    return v.astype(BF)
def sized(t, a):
    return big(t.astype(np.float32) * np.repeat(np.asarray(a, np.float32), 4, axis=-1))
def query(rng):
    v = np.zeros((N, 128, 512), BF)
    v[:, :, :4] = f(rng, 1, 128, 4)
    return v
def plain(rng):
    return {"lv": big(f(rng, N, 128, 4 * P)), "dm": big(f(rng, N, 128, 4 * P)), "nz": big(f(rng, N, 128, 4 * P)), "u": query(rng), "z": query(rng), "w": f(rng, N, 128, 512 * O)}
def positive(d):
    return {k: v if k == "w" else np.abs(v.astype(np.float32)).astype(BF) for k, v in d.items()}
def onto(t, e, rng):
    at, far = np.arange(N * P), e[e >= P]
    free = rng.permutation(np.setdiff1d(np.arange(P), e))[:far.size]
    at[free], at[far] = far, free
    return np.stack(np.split(cols(np.concatenate(t, axis=1), at), N, axis=1))
def setup_inputs(rng):
    return plain(rng)
def setup_inputs_ties(rng):
    d = plain(rng)
    for k in ("lv", "dm", "nz"):
        v = big((1 + rng.random((128, 48))) * 2.0 ** 27)
        d[k] = np.stack([big(cols(v, rng.permutation(np.arange(P) % 12)).astype(np.float32) * np.repeat(1 - 2 * rng.integers(0, 2, P), 4)) for r in range(N)])
    for k in ("u", "z"): d[k][:, :, :4] = big((1 + rng.random((1, 128, 4))) * 2.0 ** 29)
    return d
def setup_inputs_one(rng):
    d = positive(plain(rng))
    a, b = rng.permutation(N)[:2]
    g, h = np.ones((N, P)), np.ones((N, P))
    g[a, rng.permutation(P)[:K]] = 2.0 ** -8
    g[b, rng.permutation(P)[:K]] = 2.0 ** -4
    h[b, rng.permutation(P)[:K]] = 2.0 ** 8
    h[a, rng.permutation(P)[:K]] = 2.0 ** 4
    d["lv"], d["dm"] = sized(d["lv"], g[:, None]), sized(d["dm"], h[:, None])
    return d
def setup_inputs_again(rng):
    d = positive(plain(rng))
    n, top = K // N, (np.arange(128) < 64)[None, :, None]
    lt, lb, dt, db, nt = np.ones((5, N, P))
    for r in range(N):
        at, to = rng.permutation(P), rng.permutation(P)
        lt[r, at[:n]], lt[r, at[n:2 * n]] = 2.0 ** -6, 2.0 ** -3
        lb[r, at[:n:2]] = 2.0 ** 8
        nt[r, at[:n // 2]], nt[r, at[n // 2:n]] = 2.0 ** -8, 2.0 ** 4
        dt[r, to[:n]] = 2.0 ** -8
        db[r, to[:n]], db[r, to[n:2 * n]] = 2.0 ** 6, 2.0 ** 3
    d["lv"] = sized(d["lv"], np.where(top, lt[:, None], lb[:, None]))
    d["dm"] = sized(d["dm"], np.where(top, dt[:, None], db[:, None]))
    d["nz"] = sized(d["nz"], np.where(top, nt[:, None], 1.0))
    d["u"], d["z"] = big(d["u"].astype(np.float32) * top), big(d["z"].astype(np.float32) * ~top)
    return d
def setup_inputs_zero(rng):
    d = plain(rng)
    g, h, e = np.ones((3, N, P))
    for r in range(N):
        g[r, rng.permutation(P)[:3 * K // (2 * N)]] = 0
        h[r, rng.permutation(P)[K // (2 * N):]] = 0
        e[r, rng.permutation(P)[:P // 2]] = 0
    d["lv"], d["dm"], d["nz"] = sized(d["lv"], g[:, None]), sized(d["dm"], h[:, None]), sized(d["nz"], e[:, None])
    return d
def setup_inputs_spread(rng):
    d = plain(rng)
    d["lv"] = sized(wide(rng, N, 128, 4 * P), 32 * np.exp2(rng.integers(-6, 7, (N, 1, P))))
    for k in ("dm", "nz"): d[k] = sized(wide(rng, N, 128, 4 * P, cols=6), np.full((1, 1, P), 32.0))
    for k in ("u", "z"): d[k] = sized(d[k], np.full((1, 1, 128), 2.0 ** 24))
    low = np.concatenate([score(d["u"][r], mx_ref.quantize(np.ascontiguousarray(d["lv"][r]))) for r in range(N)])
    high = np.concatenate([score(d["z"][r], mx_ref.quantize(np.ascontiguousarray(d["dm"][r]))) for r in range(N)])
    d["lv"] = onto(d["lv"], np.argsort(low, kind="stable")[:K], rng)
    d["dm"] = onto(d["dm"], np.argsort(-high, kind="stable")[:K], rng)
    return d
def check_inputs(d):
    b = []
    for k, lo, hi in (("lv", -16, 28), ("dm", -16, 28), ("nz", -16, 28), ("u", -30, 30), ("z", -30, 30), ("w", -30, 30)):
        v = np.abs(d[k].astype(np.float32))
        if not (np.isfinite(v).all() and ((v == 0) | (v >= 2.0 ** lo) & (v <= 2.0 ** hi)).all()): b.append("a value of " + k)
    for k in ("u", "z"):
        v = d[k].astype(np.float32)
        if (v[:, :, 4:] != 0).any(): b.append(k + " has numbers behind its column 0")
        if (v != v[:1]).any(): b.append(k + " isn't the same on all ranks")
    return b
def score(t, q):
    return np.abs(mx_ref.matmul(mx_ref.quantize(np.ascontiguousarray(t)), q)[0]) + np.float32(0)
def reference(lv, dm, nz, u, z, w):
    L = [mx_ref.quantize(np.ascontiguousarray(lv[r])) for r in range(N)]
    X = [mx_ref.quantize(np.ascontiguousarray(dm[r])) for r in range(N)]
    noise = join(*[mx_ref.quantize(np.ascontiguousarray(nz[r])) for r in range(N)])
    oc, osc = np.zeros((N, 128, 8 * P), np.uint8), np.zeros((N, 16, 2 * P), np.uint8)
    sw, lw, y = np.zeros((N, 2, K), np.float32), np.zeros((N, 2, K), np.float32), np.zeros((N, 128, O * P), np.float32)
    for t in range(2):
        low = np.argsort(np.concatenate([score(u[r], L[r]) for r in range(N)]), kind="stable")[:K]
        high = np.argsort(-np.concatenate([score(z[r], X[r]) for r in range(N)]), kind="stable")[:K]
        lw[:, t], sw[:, t] = low, high
        gone, come = pick(join(*L), low), pick(join(*X), high)
        v = decode(come) * np.float32(0.5) + decode(pick(noise, low)) * np.float32(0.5)
        new = mx_ref.quantize(np.ascontiguousarray(v.astype(BF)))
        for r in range(N):
            a, b = np.flatnonzero(low // P == r), np.flatnonzero(high // P == r)
            L[r] = put(L[r], low[a] - P * r, pick(new, a))
            X[r] = put(X[r], high[b] - P * r, pick(gone, b))
    for r in range(N):
        oc[r], osc[r] = emit(join(L[r], X[r]))
        for o in range(O):
            y[r, :, P * o:P * o + P] = mx_ref.matmul(mx_ref.quantize(np.ascontiguousarray(w[r][:, 512 * o:512 * o + 512])), L[r])
    return {"oc": oc, "osc": osc, "sw": sw, "lw": lw, "y": y}

@@ -1,0 +1,848 @@
+import numpy as np
+from concourse.bass import DstId, RemoteDMATransfer
+from concourse.mybir import dt, AluOpType, AxisListType, ActivationFunctionType
+
+O = AluOpType
+AF = ActivationFunctionType
+P = 96
+F32, BF, I32, U16 = "float32", "bfloat16", "int32", "uint16"
+SCRATCH = {
+    "BT": ("sbuf", [128, 1152], BF), "WT": ("sbuf", [128, 512], BF), "UZ": ("sbuf", [128, 8], BF),
+    "UT": ("sbuf", [128, 512], BF), "ZT": ("sbuf", [128, 512], BF), "ONB": ("sbuf", [128, 128], BF),
+    "HAF": ("sbuf", [128, 128], BF), "DG": ("sbuf", [128, 128], BF), "ET": ("sbuf", [128, 2048], BF),
+    "NT0": ("sbuf", [128, 512], BF), "NT1": ("sbuf", [128, 512], BF),
+    "PI": ("sbuf", [128, 1], I32), "PJ": ("sbuf", [128, 4], I32), "MI": ("sbuf", [128, 3], I32),
+    "DPo": ("sbuf", [128, 2], U16), "LPo": ("sbuf", [128, 2], U16), "Mo": ("sbuf", [128, 6], U16),
+    "O1o": ("sbuf", [128, 2], U16), "UOo": ("sbuf", [128, 2], U16), "X2o": ("sbuf", [128, 6], U16), "B2o": ("sbuf", [128, 2], U16), "N2o": ("sbuf", [128, 2], U16),
+    "FLo": ("sbuf", [128, 8], U16), "FDo": ("sbuf", [128, 6], U16), "GI": ("sbuf", [128, 4], I32), "GJ": ("sbuf", [128, 4], I32),
+    "GK": ("sbuf", [128, 4], I32),
+}
+for _n, _w in {"QT": 544, "UQ": 128, "ZQ": 128, "EQ": 512, "WQ": 128, "SL1": 32, "LD1": 128, "MG1": 32, "UO": 36, "UD": 128, "SL2": 96,
+               "LD2": 128, "MG2": 16, "LD3": 32, "MG3": 16, "DW": 224, "NP1": 128, "BP2": 128, "NP2": 128, "LF": 128, "DF": 96}.items():
+    SCRATCH[_n] = ("sbuf", [128, _w], "float8_e4m3fn_x4")
+    SCRATCH[_n + "s"] = ("sbuf", [128, _w], "uint8")
+for _x, _n, _w in ((1, 16, 18), (2, 48, 16), (3, 16, 4)):
+    SCRATCH["RC%d" % _x] = ("sbuf", [128, _n], "float8_e4m3fn_x4")
+    SCRATCH["RC%ds" % _x] = ("sbuf", [128, _n], "uint8")
+    SCRATCH["RW%d" % _x] = ("sbuf", [128, _w], "float8_e4m3fn_x4")
+    SCRATCH["RW%ds" % _x] = ("sbuf", [128, _w], "uint8")
+_F = {"RS1": 1, "RS2": 1, "RS3": 1, "RS4": 1, "SD": 32, "NL": 32, "NM": 32, "DQ": 1, "GV": 2, "CX": 256, "CY": 256, "SWA": 8, "HN": 128, "HM": 128,
+      "T4": 4, "TS": 2, "G2": 2, "GA": 8, "NS2": 1, "NK": 32, "ON": 32, "ROW": 192, "R96": 96, "PC": 8, "LC": 1, "TL": 32, "CT": 416, "UZ": 8,
+      "FT": 96, "FK": 96, "JB": 6, "PT": 192, "K0": 192, "KK": 192, "TT": 192, "KF": 96, "TF": 96, "CL": 288, "RB": 4,
+      "EO": 32, "RO": 32, "CW": 256, "CV": 256, "NF": 4, "CN": 1, "CF": 1, "CTO": 64, "IDW": 32, "RP": 96,
+      "HL": 288, "HT": 288, "H1": 64, "H1t": 64, "OL": 2,
+      "VO": 2, "H2": 192, "H2t": 192, "OX": 6, "XO": 24, "XP": 18,
+      "OW": 4, "MM": 32, "MW": 384, "MV": 384, "OM": 6,
+      "SC": 32, "NS": 4, "FM": 12, "FH": 768, "FR": 24, "FL": 6, "FD": 6, "Y": 96, "G4": 8, "G4t": 64, "NB": 1,
+      "PR": 64, "PM": 64, "HP": 64, "HPt": 64, "DL": 2, "OE": 32, "OR": 32, "KM": 64, "OT": 64, "Q1": 2, "KC": 2, "QA": 2, "PA": 4,
+      "K4": 4, "KT": 4, "KE": 128, "KR": 128, "GR": 128, "GP": 4, "FF": 512, "WW": 512, "CC": 512, "N1": 4, "RB2": 4, "CO": 128, "AD": 4,
+      "HO": 256, "HQ": 256, "MO": 2,
+      "FT0": 192, "FT1": 192, "FT2": 192, "FT3": 192}
+for _n, _w in (("EP", 128), ("EQr", 128), ("MK", 128), ("MG", 192), ("MT", 512), ("MH", 640), ("ML", 16)):
+    _F[_n] = _F[_n + "b"] = _w
+_AT, _o = {}, 0
+for _n, _w in _F.items():
+    if _n in ("RS1", "RS2", "RS3", "RS4", "SD", "NL", "NM", "NK", "Y", "G4t"):
+        SCRATCH["f" + _n] = ("sbuf", [128, _w], F32)
+    else:
+        _AT["f" + _n] = (_o, _w)
+        _o += -(-_w // 32) * 32
+SCRATCH["fW"] = ("sbuf", [128, _o], F32)
+for _i in range(8):
+    SCRATCH["p%d" % _i] = ("psum", [128, 512], F32)
+SEMAPHORES = ["vs", "ac", "te", "gp", "ls"] + [_s + str(_k) for _k in (1, 2, 3, 4) for _s in ("sa", "sn", "sr")]
+for _x in (1, 2, 3):
+    SEMAPHORES += ["a%d" % _x, "b%d" % _x, "qc%d" % _x, "qs%d" % _x, "wc%d" % _x, "ws%d" % _x]
+SEMAPHORES += ["d%d" % _i for _i in range(60)]
+WAKE, PIPE, CYCLE, SLACK = 0.1, 0.06, 0.00083, 0.03
+LATE = {"n1": 2.53, "s1": 3.9, "a1": 4.9, "b1": 2.63, "n3": 1.9, "s3": 2.97, "n4": 1.9, "s4": 3.09, "n2": 2.14, "s2": 5.03, "a2": 4.51, "b2": 5.0,
+        "a3": 3.82, "b3": 2.45}
+NX = {1: 16, 2: 16, 3: 4}
+NY = {1: 18, 2: 16, 3: 4}
+LAND = {1: ("UO", 0), 2: ("DW", 96), 3: ("DW", 192)}
+
+
+def _layout(T, topo):
+    ranks = T.cores
+    a = [r for r in range(8) if r == 0 or topo.same_plane(ranks[0], ranks[r])]
+    b = [r for r in range(8) if r not in a]
+    return a, b
+
+
+def _owners(x, order):
+    return {1: [order[0], order[4]], 2: order[1:4] + order[5:8], 3: order}[x]
+
+
+def _helpers(home, far, topo):
+    h = [c for c in topo.cores_of(home) if c != home and topo.may_write(c, far)]
+    return sorted(h, key=lambda c: (topo.die(c) != topo.die(home), c))
+
+
+def _remote(g, T, topo, core, moves, sem):
+    tr = []
+    for src, dsts, eng, *own in moves:
+        ids = []
+        for c, _ in dsts:
+            rid, pid = topo.addr(c, core)
+            ids.append(DstId(rid=rid, pnc=pid))
+        m = 0
+        for e in eng:
+            m |= 1 << e
+        tr.append(RemoteDMATransfer(dst_ids=ids, dma_engine_mask=m, remote_sem=T.sem[own[0] if own else sem], srcs=[src], dsts=[d for _, d in dsts]))
+    g.remote_dma_fused(tr, local_sem=T.sem.ls)
+    return sum(len(mv[2]) for mv in moves)
+
+
+def _codes(T, name, a, b):
+    return T[name][:, a:b].bitcast(dt.uint8)
+
+
+def _hand_on(g, core, T, topo, rank, far):
+    home = T.cores[rank]
+    hs = _helpers(home, T.cores[far[0]], topo)
+    if core not in hs:
+        return
+    me, ls = hs.index(core), 0
+    eng = topo.engines(core, T.cores[far[0]])
+    n_on = len(topo.engines(home, core)) - len(eng)
+    a, b = _layout(T, topo)
+
+    def scores(k, w):
+        g.wait_ge(T.sem["sr%d" % k], n_on)
+        dst = ("fSD", "fNK", "fNL", "fNM")[k - 1]
+        to = far[:len(far) // 2] if me < 2 else far[len(far) // 2:]
+        return _remote(g, T, topo, core, [(T["fRS%d" % k][:], [(T.cores[r], T[dst][:, 4 * rank:4 * rank + w]) for r in to], eng)], "sa%d" % k)
+
+    def first(x, codes):
+        n = NX[x]
+        g.wait_ge(T.sem[("qc%d" if codes else "qs%d") % x], n_on)
+        mv = []
+        to = [r for r in _owners(x, a + b) if r in far]
+        for i, r in enumerate(to):
+            e = eng if x == 1 else eng[2 * i:2 * i + 2]
+            if codes:
+                mv.append((_codes(T, "RC%d" % x, n * i, n * i + n), [(T.cores[r], _codes(T, "LD%d" % x, n * rank, n * rank + n))], e))
+            else:
+                mv.append((T["RC%ds" % x][:, n * i:n * i + n], [(T.cores[r], T["LD%ds" % x][:, n * rank:n * rank + n])], e))
+        return _remote(g, T, topo, core, mv, "a%d" % x)
+
+    def second(x, codes):
+        own = _owners(x, a + b)
+        if rank not in own:
+            return 0
+        n = NY[x]
+        nm, base = LAND[x]
+        base += n * own.index(rank)
+        g.wait_ge(T.sem[("wc%d" if codes else "ws%d") % x], n_on)
+        if codes:
+            mv = [(_codes(T, "RW%d" % x, 0, n), [(T.cores[r], _codes(T, nm, base, base + n)) for r in far], eng)]
+        else:
+            mv = [(T["RW%ds" % x][:], [(T.cores[r], T[nm + "s"][:, base:base + n]) for r in far], eng)]
+        return _remote(g, T, topo, core, mv, "b%d" % x)
+
+    if me in (1, 2):
+        ls += scores(1, 1)
+        for x in (1, 3):
+            ls += first(x, me == 1)
+            ls += second(x, me == 1)
+    elif me in (0, 3):
+        ls += scores(3, 1)
+        ls += scores(4, 1)
+        ls += first(2, me == 0)
+        ls += scores(2, 1)
+        ls += second(2, me == 0)
+    g.wait_ge(T.sem.ls, ls)
+
+
+def rank_program(g, core, T, topo):
+    rank = T.rank_of(core)
+    pa, pb = _layout(T, topo)
+    if rank is None:
+        for r in range(8):
+            if core in topo.cores_of(T.cores[r]):
+                _hand_on(g, core, T, topo, r, pb if r in pa else pa)
+        return
+    far = pb if rank in pa else pa
+    near = [r for r in (pa if rank in pa else pb) if r != rank]
+    order = pa + pb
+    m = order.index(rank)
+    hs = _helpers(core, T.cores[far[0]], topo)
+    e_off = topo.engines(core, T.cores[near[0]])
+    e_on = [e for e in topo.engines(core, hs[0]) if e not in e_off]
+    me = rank
+
+    Q = {"v": g.vector, "a": g.scalar, "t": g.tensor, "g": g, "y": g.sync}
+    SEM = {"v": "vs", "a": "ac", "t": "te", "g": "gp"}
+    acc, waited, know, cnt = {}, {q: {} for q in Q}, {}, {}
+    nd, ls, sent = [0], [0], []
+
+    def X(name, c0=0, c1=None, r0=0, r1=128, st=1):
+        o, w = _AT[name] if name in _AT else (0, SCRATCH[name][1][1])
+        return ("fW" if name in _AT else name, o + c0, o + (w if c1 is None else c1), r0, r1, st)
+
+    def ap(v):
+        n, c0, c1, r0, r1, st = v
+        if (r0, r1) == (0, 128):
+            return T[n][:, c0:c1] if st == 1 else T[n][:, c0:c1:st]
+        return T[n][r0:r1, c0:c1] if st == 1 else T[n][r0:r1, c0:c1:st]
+
+    def width(v):
+        return -(-(v[2] - v[1]) // v[5])
+
+    def hit(a, b):
+        if a[4] <= b[3] or b[4] <= a[3] or a[2] <= b[1] or b[2] <= a[1]:
+            return False
+        return not (a[5] == b[5] > 1 and (a[1] - b[1]) % a[5])
+
+    def norm(v):
+        return (v[0], 0, 512, 0, 128, 1) if SCRATCH[v[0]][0] == "psum" else v
+
+    def enter(book, reads, writes, tag, q):
+        for v in writes:
+            nv = norm(v)
+            book[v[0]] = [e for e in book.get(v[0], []) if not (nv[1] <= e[0][1] and e[0][2] <= nv[2] and nv[3] <= e[0][3] and e[0][4] <= nv[4] and nv[5] == 1)]
+            book[v[0]].append((nv, True, tag, q))
+        for v in reads:
+            book.setdefault(v[0], []).append((norm(v), False, tag, q))
+
+    def pre(q, reads, writes):
+        need = {}
+        for vs, w in ((reads, False), (writes, True)):
+            for v in vs:
+                ps = SCRATCH[v[0]][0] == "psum"
+                for r, iw, ev, eq in acc.get(v[0], []):
+                    if (iw or w or (ps and eq != q)) and hit(r, norm(v)):
+                        if ps and q == "t" and eq == "t" and w:
+                            continue
+                        need[ev[0]] = max(need.get(ev[0], 0), ev[1])
+        for s in sorted(need, key=lambda s: (s in ("vs", "ac", "te"), s)):
+            if waited[q].get(s, 0) < need[s]:
+                Q[q].wait_ge(T.sem[s], need[s])
+                for s2, n2 in know.get((s, need[s]), {}).items():
+                    waited[q][s2] = max(waited[q].get(s2, 0), n2)
+                waited[q][s] = need[s]
+
+    def post(q, reads, writes, ev):
+        know[ev] = dict(waited[q])
+        enter(acc, reads, writes, ev, q)
+
+    nodes, seen = [], {}
+
+    def note(ways, reads, writes, after=(), late=0.0):
+        k = len(nodes)
+        pr = set(after)
+        q0 = list(ways)[0] if len(ways) == 1 else ""
+        for vs, w in ((reads, False), (writes, True)):
+            for v in vs:
+                ps = SCRATCH[v[0]][0] == "psum"
+                for r, iw, i, q in seen.get(v[0], []):
+                    if i != k and (iw or w or (ps and (q != q0 or not q))) and hit(r, norm(v)):
+                        pr.add(i)
+        enter(seen, reads, writes, k, q0)
+        nodes.append((ways, pr, late))
+        return k
+
+    def schedule():
+        n = len(nodes)
+        succ = [[] for _ in range(n)]
+        for k, (_, pr, _) in enumerate(nodes):
+            for p in pr:
+                succ[p].append(k)
+        dur = [min(c for _, c in w.values()) + late for w, _, late in nodes]
+        path = [0.0] * n
+        for k in range(n - 1, -1, -1):
+            path[k] = dur[k] + max([path[x] + WAKE for x in succ[k]], default=0.0)
+        left = [len(pr) for _, pr, _ in nodes]
+        at = [0.0] * n
+        free = {q: 0.0 for q in Q}
+        ready = {k for k in range(n) if not left[k]}
+        while ready:
+            opt = []
+            for k in ready:
+                q, t = min(((q, max(free.get(q, 0.0), at[k])) for q in nodes[k][0]), key=lambda x: x[1] + nodes[k][0][x[0]][1])
+                opt.append((t, k, q))
+            first = min(opt)[0]
+            t, k, q = max((o for o in opt if o[0] <= first + SLACK), key=lambda o: (path[o[1]], -o[1]))
+            ready.discard(k)
+            issue, c = nodes[k][0][q]
+            issue()
+            if q in free:
+                free[q] = t + c - (PIPE if q in SEM else 0.0)
+            for x in succ[k]:
+                at[x] = max(at[x], t + c + nodes[k][2] + WAKE)
+                left[x] -= 1
+                if not left[x]:
+                    ready.add(x)
+
+    def issue_op(q, call, reads, writes):
+        pre(q, reads, writes)
+        s = SEM[q]
+        if q == "g" and waited[q].get(s, 0) < cnt.get(s, 0):
+            g.wait_ge(T.sem[s], cnt[s])
+            waited[q][s] = cnt[s]
+        i = call()
+        cnt[s] = cnt.get(s, 0) + 1
+        i.then_inc(T.sem[s], 1)
+        post(q, reads, writes, (s, cnt[s]))
+
+    def el(n, f=1.0):
+        return PIPE + max(64, n * f) * CYCLE
+
+    def op(q, call, reads, writes, cost):
+        note({q: (lambda: issue_op(q, call, reads, writes), cost)}, reads, writes)
+
+    def either(v, a, reads, writes, n):
+        note({"v": (lambda: issue_op("v", v, reads, writes), el(n)), "a": (lambda: issue_op("a", a, reads, writes), el(n) + 0.02)}, reads, writes)
+
+    def dma(q, out, in_, reads=(), writes=()):
+        def issue():
+            pre(q, reads, writes)
+            s = "d%d" % nd[0]
+            nd[0] += 1
+            Q[q].dma_start(out, in_).then_inc(T.sem[s], 16)
+            cnt[s] = 16
+            post(q, reads, writes, (s, 16))
+        note({q: (issue, 0.06)}, reads, writes, (), 2.0)
+
+    def send(moves, sem, reads):
+        def issue():
+            pre("g", reads, [])
+            ls[0] += _remote(g, T, topo, core, moves, sem)
+        sent.append(note({"g": (issue, 0.4)}, reads, [], sent[-1:]))
+
+    def arrive(views, sem, total, late):
+        def issue():
+            cnt[sem] = total
+            for v in views:
+                acc.setdefault(v[0], []).append((v, True, (sem, total), "r"))
+        note({"r": (issue, 0.0)}, [], views, sent[-1:], late)
+
+    def dcol(q, dst, d0, src, s0, n):
+        dma(q, _codes(T, dst, d0, d0 + n), _codes(T, src, s0, s0 + n), [X(src, s0, s0 + n)], [X(dst, d0, d0 + n)])
+        dma(q, T[dst + "s"][:, d0:d0 + n], T[src + "s"][:, s0:s0 + n], [X(src + "s", s0, s0 + n)], [X(dst + "s", d0, d0 + n)])
+
+    def sc(s):
+        return (ap(s), [s]) if isinstance(s, tuple) else (s, [])
+
+    def ts(out, a, s1, op0, s2=None, op1=None):
+        p1, r1 = sc(s1)
+        p2, r2 = sc(s2)
+        if op1 is None:
+            op("v", lambda: g.vector.tensor_scalar(ap(out), ap(a), p1, None, op0), [a] + r1, [out], el(width(out)))
+        else:
+            op("v", lambda: g.vector.tensor_scalar(ap(out), ap(a), p1, p2, op0, op1), [a] + r1 + r2, [out], el(width(out)))
+
+    def tt(out, a, b, o):
+        op("v", lambda: g.vector.tensor_tensor(ap(out), ap(a), ap(b), o), [a, b], [out], el(width(out), 2.0))
+
+    def cp(out, a):
+        v = lambda: g.vector.tensor_copy(ap(out), ap(a))
+        if SCRATCH[out[0]][2] in (F32, BF) and SCRATCH[a[0]][2] in (F32, BF):
+            either(v, lambda: g.scalar.activation(ap(out), ap(a), AF.Copy), [a], [out], width(out))
+        else:
+            op("v", v, [a], [out], el(width(out)))
+
+    def times(out, a, col):
+        either(lambda: g.vector.tensor_scalar(ap(out), ap(a), ap(col), None, O.mult), lambda: g.scalar.activation(ap(out), ap(a), AF.Copy, scale=ap(col)), [a, col], [out], width(out))
+
+    def red(out, a, o=O.add, neg=False, ab=False):
+        op("v", lambda: g.vector.tensor_reduce(ap(out), ap(a), AxisListType.X, o, negate=neg, apply_absolute_value=ab), [a], [out], el(width(a)))
+
+    def total(out, a):
+        either(lambda: g.vector.tensor_reduce(ap(out), ap(a), AxisListType.X, O.add),
+               lambda: g.scalar.activation(ap(a), ap(a), AF.Copy, accum_out=ap(out)), [a], [a, out], width(a))
+
+    def tr(out, a):
+        op("v", lambda: g.vector.transpose(ap(out), ap(a)), [a], [out], el(width(a)))
+
+    def ms(out, c):
+        op("v", lambda: g.vector.memset(ap(out), c), [], [out], el(width(out)))
+
+    def act(out, a, func):
+        op("a", lambda: g.scalar.activation(ap(out), ap(a), func), [a], [out], el(width(out)) + 0.02)
+
+    def iota(out, pat, base, cm=0):
+        kw = {} if SCRATCH[out[0]][2] == I32 else {"allow_small_or_imprecise_dtypes": True}
+        op("g", lambda: g.iota(ap(out), pat, base, cm, **kw), [], [out], 0.13 + 2 * CYCLE * width(out))
+
+    def quant(dst, d0, d1, src, s0, s1):
+        op("v", lambda: g.vector.quantize_mx(T[dst][:, d0:d1], T[dst + "s"][:, d0:d1], T[src][:, s0:s1]), [X(src, s0, s1)], [X(dst, d0, d1), X(dst + "s", d0, d1)], 0.07 + 0.00022 * (s1 - s0))
+
+    def mm(bank, n, l, l0, r, r0, start=True, stop=True):
+        op("t", lambda: g.tensor.matmul_mx(T[bank][:, 0:n], T[l][:, l0:l0 + 128], T[l + "s"][:, l0:l0 + 128], T[r][:, r0:r0 + n], T[r + "s"][:, r0:r0 + n], start, stop),
+           [X(l, l0, l0 + 128), X(l + "s", l0, l0 + 128), X(r, r0, r0 + n), X(r + "s", r0, r0 + n)], [X(bank, 0, n)], PIPE + 0.001 * (n + 16))
+
+    def pick(dst, n, win, a, b, off):
+        ov = X(off[0], off[1], off[1] + n // 16)
+        op("a", lambda: g.scalar.activation(T[dst + "s"][:, 0:n], T[win + "s"][:, a:b].indirect(ap(ov)), AF.Copy), [X(win + "s", a, b), ov], [X(dst + "s", 0, n)], el(n, 1.5) + 0.02)
+        op("v", lambda: g.vector.tensor_copy(T[dst][:, 0:n].bitcast(dt.uint32), T[win][:, a:b].bitcast(dt.uint32).indirect(ap(ov))), [X(win, a, b), ov], [X(dst, 0, n)], el(n, 1.5))
+
+    def send1(x, src, s0, between=lambda: None):
+        n, own, ps = NX[x], _owners(x, order), src + "s"
+        fo = [r for r in own if r in far]
+        p, w = s0 + n * own.index(fo[0]), n * len(fo)
+        send([(_codes(T, src, p, p + w), [(hs[0 if x == 2 else 1], _codes(T, "RC%d" % x, 0, w))], e_on)], "qc%d" % x, [X(src, p, p + w)])
+        send([(T[ps][:, p:p + w], [(hs[3 if x == 2 else 2], T["RC%ds" % x][:])], e_on)], "qs%d" % x, [X(ps, p, p + w)])
+        mc, mp, rd, rp = [], [], [], []
+        for i, r in enumerate([r for r in near if r in own]):
+            c = s0 + n * own.index(r)
+            e = e_off if x == 1 else e_off[2 * i:2 * i + 2]
+            mc.append((_codes(T, src, c, c + n), [(T.cores[r], _codes(T, "LD%d" % x, n * me, n * me + n))], e))
+            mp.append((T[ps][:, c:c + n], [(T.cores[r], T["LD%ds" % x][:, n * me:n * me + n])], e))
+            rd.append(X(src, c, c + n))
+            rp.append(X(ps, c, c + n))
+        between()
+        if mc:
+            send(mc, "a%d" % x, rd)
+            send(mp, "a%d" % x, rp)
+        if me in own:
+            dcol("y", "LD%d" % x, n * me, src, s0 + n * own.index(me), n)
+            oth = [X(k, n * r, n * r + n) for k in ("LD%d" % x, "LD%ds" % x) for r in range(8) if r != me]
+            arrive(oth, "a%d" % x, 7 * 2 * (len(e_off) if x == 1 else 2), LATE["a%d" % x])
+
+    def send2(x):
+        n, own = NY[x], _owners(x, order)
+        nm, base = LAND[x]
+        src = "MG%d" % x
+        if me in own:
+            c = base + n * own.index(me)
+            for s, hc, h, k in ((src, "RW%d" % x, hs[0 if x == 2 else 1], "wc%d"), (src + "s", "RW%ds" % x, hs[3 if x == 2 else 2], "ws%d")):
+                code = s == src
+                sap = _codes(T, s, 0, n) if code else T[s][:, 0:n]
+                dap = _codes(T, nm, c, c + n) if code else T[nm + "s"][:, c:c + n]
+                hap = _codes(T, hc, 0, n) if code else T[hc][:]
+                send([(sap, [(h, hap)], e_on, k % x), (sap, [(T.cores[r], dap) for r in near], e_off, "b%d" % x)], None, [X(s, 0, n)])
+            dcol("y", nm, c, src, 0, n)
+        oth = [(base + n * i, r) for i, r in enumerate(own) if r != me]
+        arrive([X(k, c, c + n) for k in (nm, nm + "s") for c, r in oth], "b%d" % x, len(oth) * 2 * len(e_off), LATE["b%d" % x])
+
+    def send_scores(k, src, c0, w):
+        sap = T[src][:, c0:c0 + w]
+        rd = [X(src, c0, c0 + w)]
+        fm = (sap, [(h, T["fRS%d" % k][:]) for h in (hs[1:3] if k == 1 else (hs[0], hs[3]))], e_on, "sr%d" % k)
+        nm = (sap, [(T.cores[r], T[src][:, c0:c0 + w]) for r in near], e_off, "sn%d" % k)
+        for mv in ([fm], [nm]) if k == 1 else ([fm, nm],):
+            send(mv, None, rd)
+        arrive([X(src, 4 * r, 4 * r + w) for r in near], "sn%d" % k, len(near) * len(e_off), LATE["n%d" % k])
+        arrive([X(src, 4 * r, 4 * r + w) for r in far], "sa%d" % k, len(far) * len(e_off), LATE["s%d" % k])
+
+    def load(q, buf, c0, c1, ext):
+        dma(q, T[buf][:, c0:c1], ext, [], [X(buf, c0, c1)])
+
+    load("y", "UZ", 4, 8, T.z[:, 0:4])
+    load("a", "UZ", 0, 4, T.u[:, 0:4])
+    load("y", "BT", 384, 768, T.dm[:])
+    load("a", "BT", 0, 384, T.lv[:])
+    load("y", "BT", 768, 1152, T.nz[:])
+    load("a", "WT", 0, 512, T.w[:])
+    iota(X("PI"), [[1, 1]], 0, 1)
+    iota(X("fR96"), [[0, 3], [1, 32]], 0)
+    iota(X("fROW"), [[16, 6], [0, 2], [1, 16]], 0)
+    CT = lambda a, b, r0=0, r1=128: X("fCT", a, b, r0, r1)
+    iota(CT(96, 128), [[0, 8], [1, 4]], 4 * m)
+    iota(X("fJB"), [[16, 6]], 0)
+    e1 = _owners(1, order)
+    cl = [order.index(s) % 2 for s in range(8)]
+    a0, a1 = -cl[me] % 2, (1 - cl[me]) % 2
+    iota(X("fPR"), [[a1 - a0, 2], [0, 2], [2, 16]], a0)
+    if me in e1:
+        ow = e1.index(me)
+        pairs = [(order[2 * q + ow], order[2 * q + 1 - ow]) for q in range(4)]
+        for q, (s0, s1) in enumerate(pairs):
+            iota(X("fGR", 32 * q, 32 * q + 32), [[2, 16], [1 + 32 * (s1 - s0), 2]], 32 * s0)
+    ms(X("ONB"), 1.0)
+    ms(X("fON"), 1.0)
+    ms(X("HAF"), 0.5)
+    ms(CT(192, 320, 0, 64), -1000.0)
+    ms(CT(320, 384, 64, 128), -1000.0)
+    op("g", lambda: g.affine_select(T.DG[:], T.HAF[:], [[-1, 128]], O.is_equal, 0.0, 0, 1), [X("HAF")], [X("DG")], 0.4)
+    for i, k in enumerate((31, 15, 3, 1)):
+        op("v", lambda k=k, i=i: g.vector.tensor_scalar(T.PJ[:, i:i + 1], T.PI[:], k, None, O.bitwise_and), [X("PI")], [X("PJ", i, i + 1)], el(1))
+    cp(X("fPC", 0, 3), X("PJ", 0, 3))
+    cp(X("fPA", 0, 1), X("PJ", 3, 4))
+    P32, P16, P4 = X("fPC", 0, 1), X("fPC", 1, 2), X("fPC", 2, 3)
+    for a in range(4):
+        ts(X("fLC", 0, 1, 32 * a, 32 * a + 32), X("fPC", 0, 1, 32 * a, 32 * a + 32), 32.0 * (a % 2), O.add)
+    ts(X("fTL"), X("fR96", 0, 32), X("fLC"), O.add, P32, O.subtract)
+    step = 2.0 ** -24
+    ms(X("fFT", 0, 96, 64, 128), 1.0)
+    ms(X("fFK", 0, 96, 0, 64), 1.0)
+    for n, r0 in (("fFT", 0), ("fFK", 64)):
+        v = X(n, 0, 96, r0, r0 + 64)
+        ts(v, X("fR96", 0, 96, r0, r0 + 64), X("fPC", 0, 1, r0, r0 + 64), O.is_lt, -step, O.mult)
+        ts(v, v, 1.0, O.add)
+    for b in range(3):
+        ts(X("fPC", 3 + b, 4 + b), P32, 32.0 * b, O.add)
+    cp(X("fUZ"), X("UZ"))
+    for nm, c, q in (("ZT", 4, "ZQ"), ("UT", 0, "UQ")):
+        for t in range(4):
+            times(X(nm, t, 512, 0, 128, 4), X("ONB"), X("fUZ", c + t, c + t + 1))
+        quant(q, 0, 128, nm, 0, 512)
+    quant("QT", 0, 288, "BT", 0, 1152)
+    mm("p0", 192, "ZQ", 0, "QT", 0)
+    mm("p1", 128, "UQ", 0, "QT", 0)
+    act(X("fK0", 0, 96, 0, 64), X("p0", 96, 192, 0, 64), AF.Abs)
+    act(X("fK0", 0, 96, 64, 128), X("p1", 0, 96, 64, 128), AF.Abs)
+    act(X("fK0", 96, 192), X("p0", 0, 96), AF.Abs)
+    low = 2.0 ** -110
+    ts(X("fKK", 0, 96, 0, 64), X("fK0", 0, 96, 0, 64), low, O.max)
+    ts(X("fKK", 0, 96, 64, 128), X("fK0", 0, 96, 64, 128), -1.0, O.mult, -low, O.min)
+    ts(X("fKK", 96, 192), X("fK0", 96, 192), low, O.max)
+    tr(X("fTT"), X("fKK"))
+    tt(X("fKF"), X("fKK", 0, 96), X("fFK"), O.mult)
+    tt(X("fTF"), X("fTT", 0, 96), X("fFT"), O.mult)
+    for b in range(3):
+        s = X("fTT", 32 * b, 32 * b + 1)
+        if b:
+            ts(X("fCL", 96 * b, 96 * b + 32 * b), X("fKK", 0, 32 * b), s, O.is_ge)
+        if b < 2:
+            ts(X("fCL", 96 * b + 32 * b + 32, 96 * b + 96), X("fKK", 32 * b + 32, 96), s, O.is_gt)
+        tt(X("fCL", 128 * b, 128 * b + 32), X("fKF", 32 * b, 32 * b + 32), X("fTF", 32 * b, 32 * b + 32), O.is_gt)
+    for b in range(3):
+        total(X("fRB", b, b + 1), X("fCL", 96 * b, 96 * b + 96))
+    for i, val in enumerate((lambda b: X("fTT", 32 * b, 32 * b + 1), lambda b: X("fPC", 3 + b, 4 + b), lambda b: X("fTT", 96 + 32 * b, 97 + 32 * b))):
+        for b in range(3):
+            ts(X("fHL", 96 * i + 32 * b, 96 * i + 32 * b + 32), X("fTL"), X("fRB", b, b + 1), O.is_equal, val(b), O.mult)
+        tr(X("fHT", 96 * i, 96 * i + 96), X("fHL", 96 * i, 96 * i + 96))
+        total(X("fSD", 4 * me + i, 4 * me + i + 1), X("fHT", 96 * i, 96 * i + 96))
+    send_scores(1, "fSD", 4 * me, 1)
+
+    B0 = lambda n, c0=0, c1=None: X(n, c0, c1, 0, 32)
+    ts(B0("fPM"), B0("fPR"), B0("fPC", 0, 1), O.is_equal)
+    times(B0("fHP"), B0("fPM"), B0("fSD", 4 * me + 1, 4 * me + 2))
+    tr(B0("fHPt"), B0("fHP"))
+    total(B0("fDL", 0, 1), B0("fHPt", 0, 32))
+    total(B0("fDL", 1, 2), B0("fHPt", 32, 64))
+    for d in range(4):
+        cp(("DPo", 0, 2, 32 * d, 32 * d + 32, 1), ("fW",) + X("fDL")[1:3] + (0, 32, 1))
+    pick("SL1", 32, "QT", 96, 192, ("DPo", 0))
+    send1(1, "SL1", 0)
+
+    LCv = X("fLC")
+    ts(CT(0, 64), X("fROW", 0, 64), LCv, O.subtract)
+    ts(CT(64, 96), X("fR96", 0, 32), LCv, O.subtract)
+    ts(CT(128, 160), X("fR96", 0, 32), LCv, O.subtract, 32.0, O.add)
+    ts(CT(96, 128), CT(96, 128), P32, O.is_equal)
+    x2 = _owners(2, order)
+    if me in x2:
+        ts(X("fMM", 0, 32), X("fROW", 0, 32), 16.0 * (x2.index(me) % 2), O.add, P32, O.is_equal)
+    ts(X("fGV", 0, 1), X("fSD", 4 * me + 1, 4 * me + 2), 128.0 * me, O.add)
+    cp(X("fGV", 1, 2, 32, 64), X("fGV", 0, 1, 32, 64))
+    cp(X("fGV", 1, 2, 64, 128), X("fGV", 0, 1, 64, 128))
+    ts(B0("fNS2"), B0("fPA", 0, 1), float(cl[me]), O.not_equal, 1024.0, O.mult)
+    tt(B0("fGV", 1, 2), B0("fGV", 0, 1), B0("fNS2"), O.add)
+    ms(X("fNL", 4 * me, 4 * me + 1, 96, 128), 0.0)
+    for h in range(2):
+        ts(X("fKC", h, h + 1), P16, 16.0 * h, O.add)
+        ts(X("fKM", 32 * h, 32 * h + 32), X("fR96", 0, 32), X("fKC", h, h + 1), O.is_equal, 64.0, O.mult)
+        ts(X("fOT", 32 * h, 32 * h + 32), X("fR96", 0, 32), X("fKC", h, h + 1), O.is_lt)
+    tt(X("fKM"), X("fKM"), X("fOT"), O.add)
+    if me in e1:
+        par, npar = B0("fPA", 0, 1), B0("fPA", 1, 2)
+        ts(npar, par, -1.0, O.mult, 1.0, O.add)
+        ts(B0("fPA", 2, 3), B0("fPC", 0, 1), 0.5, O.mult)
+        for q, (s0, s1) in enumerate(pairs):
+            ts(B0("fAD", q, q + 1), par, 16.0 * (s1 - s0) - 0.5, O.mult, 16.0 * s0, O.add)
+            tt(B0("fAD", q, q + 1), B0("fAD", q, q + 1), B0("fPA", 2, 3), O.add)
+            ts(B0("fGP", q, q + 1), par, 32.0 * (s1 - s0), O.mult, B0("fPC", 0, 1), O.add)
+            ts(B0("fGP", q, q + 1), B0("fGP", q, q + 1), 32.0 * s0, O.add)
+            ff = B0("fFF", 128 * q, 128 * q + 128)
+            ts(ff, B0("fGR"), B0("fGP", q, q + 1), O.is_ge, -step, O.mult)
+            ts(ff, ff, 1.0, O.add)
+    ts(CT(192, 320, 64, 128), X("fROW", 0, 128, 64, 128), X("fLC", 0, 1, 64, 128), O.subtract)
+    ts(CT(320, 384, 0, 64), X("fROW", 0, 64, 0, 64), X("fLC", 0, 1, 0, 64), O.subtract, 32.0, O.add)
+    ts(X("fPT"), X("fROW"), 128.0 * me, O.add)
+    ts(X("fJB"), X("fJB"), P16, O.add)
+    ts(X("fRP", 0, 64), X("fROW", 0, 64), P32, O.subtract)
+    ts(X("fRP", 64, 96), X("fR96", 0, 32), P32, O.subtract)
+    ms(X("fVO", 0, 1, 0, 64), 96.0)
+    ms(X("fVO", 0, 1, 64, 128), 0.0)
+    for b in range(8):
+        ms(X("ET", 256 * b, 256 * b + 256), 0.0)
+    for b in range(4):
+        cp(X("ET", 513 * b, 512 * b + 512, 0, 128, 4), X("DG"))
+    for b in range(4):
+        quant("EQ", 128 * b, 128 * b + 128, "ET", 512 * b, 512 * b + 512)
+    quant("WQ", 0, 128, "WT", 0, 512)
+    ms(X("FLo", 6, 8), 0)
+    for d in ("UD", "NP1", "BP2", "NP2"):
+        dcol("y", d, 32, "QT", 0, 96)
+    dcol("y", "DW", 0, "QT", 96, 96)
+
+    def key(s):
+        return X("fSD", 4 * s, 4 * s + 1)
+
+    def rows4(v, a):
+        return (v[0], v[1], v[2], 32 * a, 32 * a + 32, v[5])
+
+    def to_all(out, src, a):
+        for d in range(4):
+            cp(rows4(out, d), rows4(src, a))
+
+    times(X("fEO"), X("fON"), key(me))
+    tr(X("fRO"), X("fEO"))
+    planes = (pa, pb) if rank in pa else (pb, pa)
+    for i, grp in enumerate((near, far)):
+        n, pl = 32 * len(grp), planes[i]
+        for a in range(4):
+            cp(X("fSWA", 4 * i, 4 * i + 4, 32 * a, 32 * a + 32), ("fSD", 4 * pl[0], 4 * pl[-1] + 1, 32 * (a ^ 1), 32 * (a ^ 1) + 32, 4 * (pl[1] - pl[0])))
+        for j, s in enumerate(grp):
+            o = O.is_le if s < me else O.is_lt
+            w = 4 * i + pl.index(s)
+            ts(X("fCW", 128 * i + 32 * j, 128 * i + 32 * j + 32), X("fRO"), key(s), o)
+            ts(X("fCX", 128 * i + 32 * j, 128 * i + 32 * j + 32), X("fRO"), X("fSWA", w, w + 1), o)
+        for k, (w, v) in enumerate((("fCW", "fCV"), ("fCX", "fCY"))):
+            tr(X(v, 128 * i, 128 * i + n), X(w, 128 * i, 128 * i + n))
+            total(X("fNF", 2 * k + i, 2 * k + i + 1), X(v, 128 * i, 128 * i + n))
+        if i == 0:
+            ts(X("fCTO"), CT(0, 64), X("fNF", 0, 1), O.subtract)
+            tt(X("fNF", 2, 3), X("fNF", 0, 1), X("fNF", 2, 3), O.add)
+    ts(X("fCN"), X("fNF", 0, 1), X("fNF", 1, 2), O.add)
+    ts(X("fCF"), X("fNF", 2, 3), X("fNF", 1, 2), O.add, X("fNF", 3, 4), O.add)
+    NL = lambda a, n="fNL": X(n, 4 * me, 4 * me + 1, 32 * a, 32 * a + 32)
+    T4 = lambda a, c: X("fT4", c, c + 1, 32 * a, 32 * a + 32)
+    TS = lambda a, c: X("fTS", c, c + 1, 32 * a, 32 * a + 32)
+    entries = lambda i, t, n, v: ts(X("fHN", 32 * i, 32 * i + 32), t, X(n), O.is_equal, v, O.mult)
+    entries(0, CT(64, 96), "fCN", X("fGV", 1, 2))
+    entries(1, CT(64, 96), "fCN", X("fSD", 4 * me + 2, 4 * me + 3))
+    tr(X("fHM", 0, 64), X("fHN", 0, 64))
+    for a in (0, 2):
+        total(NL(a), X("fHM", 0, 32, 32 * a, 32 * a + 32))
+    total(T4(2, 0), X("fHM", 32, 64, 64, 96))
+    cp(NL(1), T4(2, 0))
+    send_scores(3, "fNL", 4 * me, 1)
+
+    if me in e1:
+        nq = [2 * ow, 2 * ow + 1]
+        n0, f0 = 64 * ow, 64 - 64 * ow
+        for q in nq + [q for q in range(4) if q not in nq]:
+            k4 = B0("fK4", q, q + 1)
+            times(B0("fKT", q, q + 1), par, B0("fSD", 4 * pairs[q][1], 4 * pairs[q][1] + 1))
+            ts(k4, npar, B0("fSD", 4 * pairs[q][0], 4 * pairs[q][0] + 1), O.mult, B0("fKT", q, q + 1), O.add)
+            times(B0("fKE", 32 * q, 32 * q + 32), B0("fON"), k4)
+            if q % 2:
+                tr(B0("fKR", 32 * q - 32, 32 * q + 32), B0("fKE", 32 * q - 32, 32 * q + 32))
+
+        def ahead(q, c0, c1, out):
+            w, c = B0("fWW", 128 * q + c0, 128 * q + c1), B0("fCC", 128 * q + c0, 128 * q + c1)
+            tt(w, B0("fKR", c0, c1), B0("fFF", 128 * q + c0, 128 * q + c1), O.mult)
+            ts(c, w, B0("fK4", q, q + 1), O.is_ge)
+            total(out, c)
+
+        for i, q in enumerate(nq):
+            ahead(q, n0, n0 + 64, B0("fN1", q, q + 1))
+            ts(B0("fCO", 64 * i, 64 * i + 64), B0("fROW", 0, 64), B0("fN1", q, q + 1), O.subtract)
+        for q in range(4):
+            if q in nq:
+                ahead(q, f0, f0 + 64, B0("fRB2", q, q + 1))
+            else:
+                ahead(q, 0, 128, B0("fRB2", q, q + 1))
+            for h in range(2):
+                t = B0("fCO", 64 * nq.index(q) + 32 * h, 64 * nq.index(q) + 32 * h + 32) if q in nq else B0("fROW", 32 * h, 32 * h + 32)
+                ts(B0("fHO", 128 * h + 32 * q, 128 * h + 32 * q + 32), t, B0("fRB2", q, q + 1), O.is_equal, B0("fAD", q, q + 1), O.mult)
+        for h in range(2):
+            tr(B0("fHQ", 128 * h, 128 * h + 128), B0("fHO", 128 * h, 128 * h + 128))
+            total(B0("fMO", h, h + 1), B0("fHQ", 128 * h, 128 * h + 128))
+        for d in range(4):
+            cp(("O1o", 0, 2, 32 * d, 32 * d + 32, 1), B0("fMO"))
+        pick("MG1", 32, "LD1", 0, 128, ("O1o", 0))
+    send2(1)
+
+    entries(2, CT(128, 160), "fCF", X("fGV", 0, 1))
+    entries(3, CT(128, 160), "fCF", key(me))
+    tr(X("fHM", 64, 128), X("fHN", 64, 128))
+    for i in (2, 3):
+        total(X("fT4", i, i + 1), X("fHM", 32 * i, 32 * i + 32))
+    for a in range(4):
+        c = 2 if a % 2 else 3
+        cp(TS(a, c - 2), T4(a ^ 1, c))
+        tt(NL(a, "fNM"), T4(a, c), TS(a, c - 2), O.add)
+    send_scores(4, "fNM", 4 * me, 1)
+
+    ts(X("fH1"), X("fCTO"), X("fNF", 1, 2), O.is_equal, X("fSD", 4 * me + 1, 4 * me + 2), O.mult)
+    tr(X("fH1t"), X("fH1"))
+    total(X("fOL", 0, 1), X("fH1t", 0, 32))
+    total(X("fOL", 1, 2), X("fH1t", 32, 64))
+
+    def owners(parts, mul, add, i):
+        n = len(parts)
+        for j, (mask, col) in enumerate(parts):
+            ts(X("fMW", 128 * i + 32 * j, 128 * i + 32 * j + 32), mask, col, O.mult)
+        tr(X("fMV", 128 * i, 128 * i + 32 * n), X("fMW", 128 * i, 128 * i + 32 * n))
+        red(X("fOM", 2 * i, 2 * i + 1), X("fMV", 128 * i, 128 * i + 32 * n))
+        ts(X("fOM", 2 * i + 1, 2 * i + 2), X("fOM", 2 * i, 2 * i + 1), 63.5, O.subtract, 1.0 / 128, O.mult)
+        cp(X("MI", i, i + 1), X("fOM", 2 * i + 1, 2 * i + 2))
+        ts(X("Mo", 2 * i, 2 * i + 1), X("MI", i, i + 1), float(mul), O.mult, add, O.add)
+
+    tt(X("fVO", 1, 2), X("fVO", 0, 1), X("fSD", 4 * me + 1, 4 * me + 2), O.add)
+    ts(X("fH2"), CT(192, 384), X("fCF"), O.is_equal, X("fVO", 1, 2), O.mult)
+    tr(X("fH2t"), X("fH2"))
+    for c in range(6):
+        total(X("fOX", c, c + 1), X("fH2t", 32 * c, 32 * c + 32))
+    for a in range(4):
+        to_all(X("fXO", 6 * a, 6 * a + 6), X("fOX"), a)
+    tt(X("fXP", 0, 12), X("fXO", 0, 12), X("fXO", 12, 24), O.add)
+    tt(X("fXP", 12, 18), X("fXP", 0, 6), X("fXP", 6, 12), O.add)
+    cp(X("X2o"), X("fXP", 12, 18))
+    pick("SL2", 96, "QT", 0, 192, ("X2o", 0))
+    send1(2, "SL2", 0)
+
+    L1q, L2g, D1g, H2g = (X("fG4", i, i + 1) for i in range(4))
+    red(X("fG2", 0, 1), ("fNL", 0, 32, 0, 128, 4))
+    DQ = X("fDQ")
+    to_all(DQ, X("fG2", 0, 1), 0)
+    ts(X("fOE"), X("fON"), DQ, O.mult, 1024.0, O.is_ge)
+    tr(X("fOR"), X("fOE"))
+    for h in range(2):
+        tt(X("fOT", 32 * h, 32 * h + 32), X("fOR"), X("fKM", 32 * h, 32 * h + 32), O.mult)
+        total(X("fQ1", h, h + 1), X("fOT", 32 * h, 32 * h + 32))
+    tt(X("fQA"), X("fKC"), X("fQ1"), O.subtract)
+    for h in range(2):
+        ts(X("UOo", h, h + 1), X("fQ1", h, h + 1), 46.0, O.subtract, X("fQA", h, h + 1), O.max)
+    pick("UD", 32, "UO", 0, 36, ("UOo", 0))
+    red(X("fG2", 1, 2), ("fNM", 0, 32, 0, 128, 4))
+    for a in range(4):
+        to_all(X("fGA", 2 * a, 2 * a + 2), X("fG2"), a)
+    _, c2k, z1, c2g, L1g, o2k, _, o2g = (X("fGA", i, i + 1) for i in range(8))
+    ts(D1g, DQ, 1024.0, O.is_ge, -1024.0, O.mult)
+    tt(D1g, D1g, DQ, O.add)
+
+    to_all(X("LPo"), X("fOL"), 2)
+    pick("NP1", 32, "QT", 192, 288, ("LPo", 0))
+    for b in range(4):
+        mm("p%d" % (2 + b), 128, "EQ", 128 * b, "NP1", 0, True, False)
+    ts(X("fOW", 0, 1), L1g, 128.0 * me, O.is_ge)
+    ts(X("fOW", 1, 2), L1g, 128.0 * me + 128, O.is_lt)
+    tt(X("fOW", 2, 3), X("fOW", 0, 1), X("fOW", 1, 2), O.mult)
+    ts(X("fIDW"), X("fR96", 0, 32), P32, O.is_equal, X("fOW", 2, 3), O.mult)
+    if me in x2:
+        owners([(X("fMM", 0, 32), (L1g, o2g, c2g)[x2.index(me) // 2])], 16, P16, 2)
+    owners([(CT(96, 128), L1g)], 4, P4, 1)
+
+    def new(nt, q0):
+        for b in range(4):
+            cp(X(nt, b, 512, 0, 128, 4), X("p%d" % (2 + b), 0, 128))
+        quant("QT", q0, q0 + 128, nt, 0, 512)
+
+    for b in range(4):
+        mm("p%d" % (2 + b), 128, "EQ", 128 * b, "UD", 0, False, True)
+    new("NT0", 288)
+    mm("p6", 128, "UQ", 0, "QT", 288)
+    tt(X("fSC"), X("p6", 0, 32), X("fIDW"), O.mult)
+    red(X("fNK", 4 * me, 4 * me + 1), X("fSC"), O.add, True, True)
+    send1(3, "QT", 288, lambda: send_scores(2, "fNK", 4 * me, 1))
+    if me in x2:
+        pick("MG2", 16, "LD2", 0, 128, ("Mo", 4))
+    send2(2)
+
+    tiles = {"": ("fEP", "fEQr", "fMK", "fMG", "fMT", "fMH", "fML")}
+    tiles["b"] = tuple(n + "b" for n in tiles[""])
+
+    def prep(w, ak, ag, bg):
+        e, r, k, gl = tiles[w][:4]
+        for i, c in enumerate((ak, ag, bg)):
+            times(X(e, 32 * i, 32 * i + 32), X("fON"), c)
+        tr(X(k, 32, 64), X(e, 0, 32))
+        tr(X(r, 0, 64), X(e, 32, 96))
+        o = O.is_lt if w else O.is_ge
+        ts(X(gl, 0, 32), X(r, 32, 64), ag, o, -step, O.mult)
+        ts(X(gl, 32, 96), X(r, 0, 64), bg, o, -step, O.mult)
+        ts(X(gl, 0, 96), X(gl, 0, 96), 1.0, O.add)
+
+    def ranks(w, ak, bk, raw, cut):
+        e, r, k, gl, t, h, ml = tiles[w]
+        if cut is None:
+            ts(X(e, 96, 128), X("fON"), raw, O.mult)
+        else:
+            ts(X(e, 96, 128), X("fON"), raw, O.mult, cut, O.min)
+        tr(X(k, 64, 96), X(e, 96, 128))
+        tt(X(t, 0, 32), X(k, 64, 96), X(gl, 0, 32), O.mult)
+        tt(X(t, 32, 96), X(k, 32, 96), X(gl, 32, 96), O.mult)
+        o = O.is_gt if w else O.is_ge
+        ts(X(t, 96, 128), X(t, 0, 32), ak, o)
+        ts(X(t, 128, 192), X(t, 32, 96), bk, o)
+        total(X(ml, 0, 1), X(t, 96, 128))
+        total(X(ml, 1, 2), X(t, 128, 192))
+
+    def hot(w, at, wide, va, vb, outs):
+        e, r, k, gl, t, h, ml = tiles[w]
+        n = 64 if wide else 32
+        for i in range(n // 32):
+            ra = X("fRP", 32 * i, 32 * i + 32) if wide else X("fRP", 64, 96)
+            rb = X("fROW", 32 * i, 32 * i + 32) if wide else X("fR96", 0, 32)
+            o = at + 64 * i
+            ts(X(h, o, o + 32), ra, X(ml, 0, 1), O.is_equal, va, O.mult)
+            ts(X(h, o + 32, o + 64), rb, X(ml, 1, 2), O.is_equal, vb, O.mult)
+        tr(X(h, at + 2 * n, at + 4 * n), X(h, at, at + 2 * n))
+        for i, o in enumerate(outs):
+            total(o, X(h, at + 2 * n + 64 * i, at + 2 * n + 64 * i + 64))
+
+    def pc(i, v):
+        ts(X("fFM", i, i + 1), P32, float(v), O.add)
+        return X("fFM", i, i + 1)
+
+    def final(i, gcol, acol, out):
+        ts(X("fFH", 192 * i, 192 * i + 192), X("fPT"), gcol, O.is_equal, acol, O.mult)
+        tr(X("fFT%d" % i), X("fFH", 192 * i, 192 * i + 192))
+        for c in range(6):
+            total(X("fFR", 6 * i + c, 6 * i + c + 1), X("fFT%d" % i, 32 * c, 32 * c + 32))
+        tt(out, X("fFR", 6 * i, 6 * i + 6), out, O.max)
+
+    prep("", c2k, c2g, D1g)
+    ranks("", c2k, z1, z1, None)
+    hot("", 0, True, pc(0, 64), P32, [X("fML", 4, 5), X("fML", 5, 6)])
+    cp(X("B2o"), X("fML", 4, 6))
+    prep("b", o2k, o2g, L1g)
+    hot("", 256, False, c2g, D1g, [H2g])
+    cp(X("fFL"), X("fJB"))
+    cp(X("fFD"), X("fJB"))
+    final(0, L1g, pc(1, 288), X("fFL"))
+    final(1, D1g, pc(2, 96), X("fFD"))
+    a416, a128, a192 = pc(3, 416), pc(4, 128), pc(5, 192)
+
+    red(X("fNB"), ("fNK", 0, 32, 0, 128, 4))
+    ts(X("fNS", 1, 2), X("fNB"), -low, O.min)
+    ranks("b", o2k, X("fNS", 1, 2), X("fNB"), -low)
+    hot("b", 0, True, o2g, L1g, [X("fMLb", 4, 5), X("fMLb", 5, 6)])
+    ts(X("N2o"), X("fMLb", 4, 6), 128.0 * me, O.subtract, 95.0, O.min)
+    pick("BP2", 32, "DW", 96, 192, ("B2o", 0))
+    for b in range(4):
+        mm("p%d" % (2 + b), 128, "EQ", 128 * b, "BP2", 0, True, False)
+    pick("NP2", 32, "QT", 192, 288, ("N2o", 0))
+    for b in range(4):
+        mm("p%d" % (2 + b), 128, "EQ", 128 * b, "NP2", 0, False, True)
+    pick("MG3", 16, "LD3", 0, 32, ("Mo", 2))
+    send2(3)
+    hot("b", 256, False, o2g, L1g, [L2g])
+    final(2, L2g, a416, X("fFL"))
+    cp(X("FLo", 0, 6), X("fFL"))
+    new("NT1", 416)
+    pick("LF", 128, "QT", 0, 544, ("FLo", 0))
+    mm("p7", 128, "WQ", 0, "LF", 0)
+    dma("y", T.oc[:, 0:384], _codes(T, "LF", 0, 96), [X("LF", 0, 96)], [])
+    for k in range(4):
+        dma("y", T.osc[4 * k:4 * k + 4, 0:96], T.LFs[32 * k:32 * k + 4, 0:96], [X("LFs", 0, 96)], [])
+    cp(X("fY"), X("p7", 0, 96))
+    dma("a", T.y[:], T.fY[:], [X("fY")], [])
+
+    hot("b", 384, False, a128, a192, [X("fMLb", 6, 7)])
+    final(3, H2g, X("fMLb", 6, 7), X("fFD"))
+    cp(X("FDo"), X("fFD"))
+    pick("DF", 96, "DW", 0, 224, ("FDo", 0))
+    dma("y", T.oc[:, 384:768], _codes(T, "DF", 0, 96), [X("DF", 0, 96)], [])
+    for k in range(4):
+        dma("a" if k % 2 else "y", T.osc[4 * k:4 * k + 4, 96:192], T.DFs[32 * k:32 * k + 4, 0:96], [X("DFs", 0, 96)], [])
+    cp(L1q, L1g)
+    cp(X("GI"), X("fG4", 0, 4))
+    op("v", lambda: g.vector.tensor_scalar(T.GJ[:], T.GI[:], 7, None, O.arith_shift_right), [X("GI")], [X("GJ")], el(1))
+    ts(X("GK"), X("GJ"), -32, O.mult)
+    ms(X("fG4t", 0, 32), 0.0)
+    tt(X("fG4t", 0, 4), X("GI"), X("GK"), O.add)
+    tr(X("fG4t", 32, 64), X("fG4t", 0, 32))
+    dma("a", T.lw[:], T.fG4t[0:2, 32:64], [X("fG4t", 32, 64)], [])
+    dma("a", T.sw[:], T.fG4t[2:4, 32:64], [X("fG4t", 32, 64)], [])
+    schedule()
+    cnt["ls"] = ls[0]
+    for s in sorted(cnt):
+        if waited["g"].get(s, 0) < cnt[s]:
+            g.wait_ge(T.sem[s], cnt[s])

@@ -6,57 +6,47 @@ O = AluOpType
 AF = ActivationFunctionType
 P = 96
 F32, BF, I32, U16 = "float32", "bfloat16", "int32", "uint16"
-SCRATCH = {
-    "BT": ("sbuf", [128, 1152], BF), "WT": ("sbuf", [128, 512], BF), "UZ": ("sbuf", [128, 8], BF),
-    "UT": ("sbuf", [128, 512], BF), "ZT": ("sbuf", [128, 512], BF), "ONB": ("sbuf", [128, 128], BF),
-    "HAF": ("sbuf", [128, 128], BF), "DG": ("sbuf", [128, 128], BF), "ET": ("sbuf", [128, 2048], BF),
-    "NT0": ("sbuf", [128, 512], BF), "NT1": ("sbuf", [128, 512], BF),
-    "PI": ("sbuf", [128, 1], I32), "PJ": ("sbuf", [128, 4], I32), "MI": ("sbuf", [128, 3], I32),
-    "DPo": ("sbuf", [128, 2], U16), "LPo": ("sbuf", [128, 2], U16), "Mo": ("sbuf", [128, 6], U16),
-    "O1o": ("sbuf", [128, 2], U16), "UOo": ("sbuf", [128, 2], U16), "X2o": ("sbuf", [128, 6], U16), "B2o": ("sbuf", [128, 2], U16), "N2o": ("sbuf", [128, 2], U16),
-    "FLo": ("sbuf", [128, 8], U16), "FDo": ("sbuf", [128, 6], U16), "GI": ("sbuf", [128, 4], I32), "GJ": ("sbuf", [128, 4], I32),
-    "GK": ("sbuf", [128, 4], I32),
-}
-for _n, _w in {"QT": 544, "UQ": 128, "ZQ": 128, "EQ": 512, "WQ": 128, "SL1": 32, "LD1": 128, "MG1": 32, "UO": 36, "UD": 128, "SL2": 96,
-               "LD2": 128, "MG2": 16, "LD3": 32, "MG3": 16, "DW": 224, "NP1": 128, "BP2": 128, "NP2": 128, "LF": 128, "DF": 96}.items():
+SCRATCH = {}
+for _n, _w in {"BT": 1280, "WT": 512, "UZ": 8, "UT": 512, "ZT": 512, "ONB": 128, "HAF": 128, "DG": 128, "ET": 1056, "NT": 512, "HT": 512,
+               "MT": 528, "SG": 384, "MK": 128, "R32": 192, "R64": 128}.items():
+    SCRATCH[_n] = ("sbuf", [128, _w], BF)
+for _n, _w in {"PJ": 6, "MI": 2}.items():
+    SCRATCH[_n] = ("sbuf", [128, _w], I32)
+for _n, _w in {"LO": 4, "Mo": 4, "O1o": 2, "UOo": 2, "X2o": 6, "B2o": 2, "N2o": 2, "FLo": 8, "FDo": 6}.items():
+    SCRATCH[_n] = ("sbuf", [128, _w], U16)
+for _n, _w in {"QT": 576, "UQ": 128, "ZQ": 128, "EQ": 512, "WQ": 128, "HQ": 128, "HQ2": 128, "MQ": 132, "SL1": 32, "LD1": 128, "MG1": 32, "UO": 36,
+               "SL2": 96, "LD2": 128, "MG2": 16, "LD3": 32, "MG3": 16, "DW": 224, "MV": 192, "LF": 128, "DF": 96,
+               "RC1": 16, "RC2": 48, "RC3": 16, "RW1": 18, "RW2": 16, "RW3": 4}.items():
     SCRATCH[_n] = ("sbuf", [128, _w], "float8_e4m3fn_x4")
     SCRATCH[_n + "s"] = ("sbuf", [128, _w], "uint8")
-for _x, _n, _w in ((1, 16, 18), (2, 48, 16), (3, 16, 4)):
-    SCRATCH["RC%d" % _x] = ("sbuf", [128, _n], "float8_e4m3fn_x4")
-    SCRATCH["RC%ds" % _x] = ("sbuf", [128, _n], "uint8")
-    SCRATCH["RW%d" % _x] = ("sbuf", [128, _w], "float8_e4m3fn_x4")
-    SCRATCH["RW%ds" % _x] = ("sbuf", [128, _w], "uint8")
-_F = {"RS1": 1, "RS2": 1, "RS3": 1, "RS4": 1, "SD": 32, "NL": 32, "NM": 32, "DQ": 1, "GV": 2, "CX": 256, "CY": 256, "SWA": 8, "HN": 128, "HM": 128,
-      "T4": 4, "TS": 2, "G2": 2, "GA": 8, "NS2": 1, "NK": 32, "ON": 32, "ROW": 192, "R96": 96, "PC": 8, "LC": 1, "TL": 32, "CT": 416, "UZ": 8,
-      "FT": 96, "FK": 96, "JB": 6, "PT": 192, "K0": 192, "KK": 192, "TT": 192, "KF": 96, "TF": 96, "CL": 288, "RB": 4,
-      "EO": 32, "RO": 32, "CW": 256, "CV": 256, "NF": 4, "CN": 1, "CF": 1, "CTO": 64, "IDW": 32, "RP": 96,
-      "HL": 288, "HT": 288, "H1": 64, "H1t": 64, "OL": 2,
-      "VO": 2, "H2": 192, "H2t": 192, "OX": 6, "XO": 24, "XP": 18,
-      "OW": 4, "MM": 32, "MW": 384, "MV": 384, "OM": 6,
-      "SC": 32, "NS": 4, "FM": 12, "FH": 768, "FR": 24, "FL": 6, "FD": 6, "Y": 96, "G4": 8, "G4t": 64, "NB": 1,
-      "PR": 64, "PM": 64, "HP": 64, "HPt": 64, "DL": 2, "OE": 32, "OR": 32, "KM": 64, "OT": 64, "Q1": 2, "KC": 2, "QA": 2, "PA": 4,
-      "K4": 4, "KT": 4, "KE": 128, "KR": 128, "GR": 128, "GP": 4, "FF": 512, "WW": 512, "CC": 512, "N1": 4, "RB2": 4, "CO": 128, "AD": 4,
-      "HO": 256, "HQ": 256, "MO": 2,
-      "FT0": 192, "FT1": 192, "FT2": 192, "FT3": 192}
-for _n, _w in (("EP", 128), ("EQr", 128), ("MK", 128), ("MG", 192), ("MT", 512), ("MH", 640), ("ML", 16)):
+for _n, _w in {"RS1": 1, "RS2": 1, "RS3": 1, "RS4": 1, "SD": 32, "NL": 32, "NM": 32, "NK": 36, "Y": 96, "KT": 32}.items():
+    SCRATCH["f" + _n] = ("sbuf", [128, _w], F32)
+_V = {"UZ": 8, "PC": 16, "AD": 128, "AL": 96, "CD": 4, "CC": 192, "RK": 4, "TG": 128, "TG2": 128, "TG3": 128, "OA": 128, "OC": 128, "DN": 384, "DB": 128}
+_F = {"ON": 32, "ROW": 192, "R32": 32, "PT": 192, "JB": 6, "KR": 128, "PR": 128, "ZA": 128, "ZR": 128, "RO": 32, "GZ": 64, "GT": 64, "GV": 4,
+      "CT": 128, "CTX": 128, "CT1": 32, "TH": 128, "RP": 96, "ID": 32, "SWA": 8, "CW": 256, "CV": 256, "CX": 256, "CY": 256, "NF": 4, "CF": 1,
+      "HN": 96, "HM": 96, "H2": 128, "H2t": 128, "H2s": 128, "XT": 4, "XU": 4, "G2": 2, "DQ": 2, "GA": 8, "UX": 128, "UT": 128, "US": 128,
+      "OW": 2, "IDW": 32, "MM": 32, "MW": 64, "MX": 64, "MS": 64, "OM": 2, "SC": 32, "NB": 1, "FM": 8, "G4": 4, "FL": 6, "FD": 6}
+for _i in range(4):
+    for _n in ("FH", "FT", "FS"):
+        _F[_n + str(_i)] = 192
+for _n, _w in (("ME", 64), ("MR", 32), ("MG", 64), ("MK", 32), ("MT", 96), ("MU", 64), ("ML", 4), ("MH", 256), ("MI", 256), ("MJ", 128)):
     _F[_n] = _F[_n + "b"] = _w
-_AT, _o = {}, 0
-for _n, _w in _F.items():
-    if _n in ("RS1", "RS2", "RS3", "RS4", "SD", "NL", "NM", "NK", "Y", "G4t"):
-        SCRATCH["f" + _n] = ("sbuf", [128, _w], F32)
-    else:
-        _AT["f" + _n] = (_o, _w)
+_AT = {}
+for _b, _d in (("fV", _V), ("fW", _F)):
+    _o = 0
+    for _n, _w in _d.items():
+        _AT["f" + _n] = (_b, _o, _w)
         _o += -(-_w // 32) * 32
-SCRATCH["fW"] = ("sbuf", [128, _o], F32)
+    SCRATCH[_b] = ("sbuf", [128, _o], F32)
 for _i in range(8):
     SCRATCH["p%d" % _i] = ("psum", [128, 512], F32)
 SEMAPHORES = ["vs", "ac", "te", "gp", "ls"] + [_s + str(_k) for _k in (1, 2, 3, 4) for _s in ("sa", "sn", "sr")]
 for _x in (1, 2, 3):
     SEMAPHORES += ["a%d" % _x, "b%d" % _x, "qc%d" % _x, "qs%d" % _x, "wc%d" % _x, "ws%d" % _x]
 SEMAPHORES += ["d%d" % _i for _i in range(60)]
-WAKE, PIPE, CYCLE, SLACK = 0.1, 0.06, 0.00083, 0.03
-LATE = {"n1": 2.53, "s1": 3.9, "a1": 4.9, "b1": 2.63, "n3": 1.9, "s3": 2.97, "n4": 1.9, "s4": 3.09, "n2": 2.14, "s2": 5.03, "a2": 4.51, "b2": 5.0,
-        "a3": 3.82, "b3": 2.45}
+WAKE, PIPE, CYCLE, SLACK, QUIET, GAP = 0.1, 0.06, 0.00083, 0.03, 1.8, 0.05
+LATE = {"n1": 2.0, "s1": 4.0, "a1": 4.2, "b1": 3.03, "n3": 1.9, "s3": 2.0, "n4": 1.9, "s4": 3.1, "n2": 2.14, "s2": 3.5, "a2": 3.2, "b2": 4.1,
+        "a3": 3.5, "b3": 3.45, "small": 1.5, "big": 1.8, "dma": 2.0, "c0": 1.5, "c1": 0.4, "c2": 0.5, "c": 0.3}
 NX = {1: 16, 2: 16, 3: 4}
 NY = {1: 18, 2: 16, 3: 4}
 LAND = {1: ("UO", 0), 2: ("DW", 96), 3: ("DW", 192)}
@@ -107,11 +97,11 @@ def _hand_on(g, core, T, topo, rank, far):
     n_on = len(topo.engines(home, core)) - len(eng)
     a, b = _layout(T, topo)
 
-    def scores(k, w):
+    def scores(k):
         g.wait_ge(T.sem["sr%d" % k], n_on)
         dst = ("fSD", "fNK", "fNL", "fNM")[k - 1]
         to = far[:len(far) // 2] if me < 2 else far[len(far) // 2:]
-        return _remote(g, T, topo, core, [(T["fRS%d" % k][:], [(T.cores[r], T[dst][:, 4 * rank:4 * rank + w]) for r in to], eng)], "sa%d" % k)
+        return _remote(g, T, topo, core, [(T["fRS%d" % k][:], [(T.cores[r], T[dst][:, 4 * rank:4 * rank + 1]) for r in to], eng)], "sa%d" % k)
 
     def first(x, codes):
         n = NX[x]
@@ -141,15 +131,15 @@ def _hand_on(g, core, T, topo, rank, far):
         return _remote(g, T, topo, core, mv, "b%d" % x)
 
     if me in (1, 2):
-        ls += scores(1, 1)
         for x in (1, 3):
             ls += first(x, me == 1)
             ls += second(x, me == 1)
     elif me in (0, 3):
-        ls += scores(3, 1)
-        ls += scores(4, 1)
+        ls += scores(1)
+        ls += scores(3)
+        ls += scores(4)
         ls += first(2, me == 0)
-        ls += scores(2, 1)
+        ls += scores(2)
         ls += second(2, me == 0)
     g.wait_ge(T.sem.ls, ls)
 
@@ -177,14 +167,20 @@ def rank_program(g, core, T, topo):
     nd, ls, sent = [0], [0], []
 
     def X(name, c0=0, c1=None, r0=0, r1=128, st=1):
-        o, w = _AT[name] if name in _AT else (0, SCRATCH[name][1][1])
-        return ("fW" if name in _AT else name, o + c0, o + (w if c1 is None else c1), r0, r1, st)
+        b, o, w = _AT[name] if name in _AT else (name, 0, SCRATCH[name][1][1])
+        return (b, o + c0, o + (w if c1 is None else c1), r0, r1, st)
 
     def ap(v):
         n, c0, c1, r0, r1, st = v
         if (r0, r1) == (0, 128):
             return T[n][:, c0:c1] if st == 1 else T[n][:, c0:c1:st]
         return T[n][r0:r1, c0:c1] if st == 1 else T[n][r0:r1, c0:c1:st]
+
+    def rows(v, r0, r1):
+        return (v[0], v[1], v[2], r0, r1, v[5])
+
+    def blk(v, a):
+        return rows(v, 32 * a, 32 * a + 32)
 
     def width(v):
         return -(-(v[2] - v[1]) // v[5])
@@ -226,7 +222,7 @@ def rank_program(g, core, T, topo):
         know[ev] = dict(waited[q])
         enter(acc, reads, writes, ev, q)
 
-    nodes, seen = [], {}
+    nodes, seen, fill = [], {}, set()
 
     def note(ways, reads, writes, after=(), late=0.0):
         k = len(nodes)
@@ -252,27 +248,27 @@ def rank_program(g, core, T, topo):
         path = [0.0] * n
         for k in range(n - 1, -1, -1):
             path[k] = dur[k] + max([path[x] + WAKE for x in succ[k]], default=0.0)
-        left = [len(pr) for _, pr, _ in nodes]
-        at = [0.0] * n
-        free = {q: 0.0 for q in Q}
-        ready = {k for k in range(n) if not left[k]}
-        while ready:
-            opt = []
-            for k in ready:
-                q, t = min(((q, max(free.get(q, 0.0), at[k])) for q in nodes[k][0]), key=lambda x: x[1] + nodes[k][0][x[0]][1])
-                opt.append((t, k, q))
-            first = min(opt)[0]
-            t, k, q = max((o for o in opt if o[0] <= first + SLACK), key=lambda o: (path[o[1]], -o[1]))
-            ready.discard(k)
-            issue, c = nodes[k][0][q]
-            issue()
-            if q in free:
-                free[q] = t + c - (PIPE if q in SEM else 0.0)
-            for x in succ[k]:
-                at[x] = max(at[x], t + c + nodes[k][2] + WAKE)
-                left[x] -= 1
-                if not left[x]:
-                    ready.add(x)
+        busy, start, done = {q: [] for q in Q}, [None] * n, [0.0] * n
+        for k in sorted(range(n), key=lambda k: (-path[k], k)):
+            at = max([done[p] + WAKE for p in nodes[k][1]], default=0.0)
+            best = None
+            for q, (_, c) in nodes[k][0].items():
+                t, d = at, c - (PIPE if q in SEM else 0.0)
+                keep = []
+                if k in fill and q in SEM:
+                    keep = [(QUIET if q != "g" else done[sent[0]] - LATE["c0"] - 0.8, done[sent[0]])]
+                for b0, b1 in sorted(busy.get(q, []) + keep):
+                    if t + d + (GAP if k in fill else -SLACK) <= b0:
+                        break
+                    t = max(t, b1)
+                if best is None or t + c < best[0] + nodes[k][0][best[1]][1]:
+                    best = (t, q, d)
+            t, q, d = best
+            if q in busy:
+                busy[q].append((t, t + d))
+            start[k], done[k] = (t, -path[k], k, q), t + nodes[k][0][q][1] + nodes[k][2]
+        for t, _, k, q in sorted(start):
+            nodes[k][0][q][0]()
 
     def issue_op(q, call, reads, writes):
         pre(q, reads, writes)
@@ -291,10 +287,10 @@ def rank_program(g, core, T, topo):
     def op(q, call, reads, writes, cost):
         note({q: (lambda: issue_op(q, call, reads, writes), cost)}, reads, writes)
 
-    def either(v, a, reads, writes, n):
-        note({"v": (lambda: issue_op("v", v, reads, writes), el(n)), "a": (lambda: issue_op("a", a, reads, writes), el(n) + 0.02)}, reads, writes)
+    def either(v, a, reads, writes, c):
+        note({"v": (lambda: issue_op("v", v, reads, writes), c), "a": (lambda: issue_op("a", a, reads, writes), c + 0.02)}, reads, writes)
 
-    def dma(q, out, in_, reads=(), writes=()):
+    def dma(q, out, in_, reads=(), writes=(), late="dma"):
         def issue():
             pre(q, reads, writes)
             s = "d%d" % nd[0]
@@ -302,13 +298,13 @@ def rank_program(g, core, T, topo):
             Q[q].dma_start(out, in_).then_inc(T.sem[s], 16)
             cnt[s] = 16
             post(q, reads, writes, (s, 16))
-        note({q: (issue, 0.06)}, reads, writes, (), 2.0)
+        note({q: (issue, 0.06)}, reads, writes, (), LATE[late])
 
     def send(moves, sem, reads):
         def issue():
             pre("g", reads, [])
             ls[0] += _remote(g, T, topo, core, moves, sem)
-        sent.append(note({"g": (issue, 0.4)}, reads, [], sent[-1:]))
+        sent.append(note({"g": (issue, LATE.get("c%d" % len(sent), LATE["c"]))}, reads, [], sent[-1:]))
 
     def arrive(views, sem, total, late):
         def issue():
@@ -338,32 +334,40 @@ def rank_program(g, core, T, topo):
     def cp(out, a):
         v = lambda: g.vector.tensor_copy(ap(out), ap(a))
         if SCRATCH[out[0]][2] in (F32, BF) and SCRATCH[a[0]][2] in (F32, BF):
-            either(v, lambda: g.scalar.activation(ap(out), ap(a), AF.Copy), [a], [out], width(out))
+            either(v, lambda: g.scalar.activation(ap(out), ap(a), AF.Copy), [a], [out], el(width(out)))
         else:
             op("v", v, [a], [out], el(width(out)))
 
     def times(out, a, col):
-        either(lambda: g.vector.tensor_scalar(ap(out), ap(a), ap(col), None, O.mult), lambda: g.scalar.activation(ap(out), ap(a), AF.Copy, scale=ap(col)), [a, col], [out], width(out))
+        either(lambda: g.vector.tensor_scalar(ap(out), ap(a), ap(col), None, O.mult), lambda: g.scalar.activation(ap(out), ap(a), AF.Copy, scale=ap(col)), [a, col], [out], el(width(out)))
 
     def red(out, a, o=O.add, neg=False, ab=False):
         op("v", lambda: g.vector.tensor_reduce(ap(out), ap(a), AxisListType.X, o, negate=neg, apply_absolute_value=ab), [a], [out], el(width(a)))
 
     def total(out, a):
         either(lambda: g.vector.tensor_reduce(ap(out), ap(a), AxisListType.X, O.add),
-               lambda: g.scalar.activation(ap(a), ap(a), AF.Copy, accum_out=ap(out)), [a], [a, out], width(a))
+               lambda: g.scalar.activation(ap(a), ap(a), AF.Copy, accum_out=ap(out)), [a], [a, out], el(width(a)))
+
+    def sums(out, a, n):
+        r = X("R%d" % n, 0, width(a))
+        op("v", lambda: g.vector.tensor_tensor_scan(ap(out), ap(r), ap(a), 0.0, O.mult, O.add), [r, a], [out], el(width(a)))
+        return (out[0], out[1] + n - 1, out[2], out[3], out[4], n)
 
     def tr(out, a):
         op("v", lambda: g.vector.transpose(ap(out), ap(a)), [a], [out], el(width(a)))
 
     def ms(out, c):
-        op("v", lambda: g.vector.memset(ap(out), c), [], [out], el(width(out)))
+        op("v", lambda: g.vector.memset(ap(out), c), [], [out], el(width(out), 0.5 if SCRATCH[out[0]][2] == BF else 1.0))
 
-    def act(out, a, func):
-        op("a", lambda: g.scalar.activation(ap(out), ap(a), func), [a], [out], el(width(out)) + 0.02)
+    def act(out, a, func, bias=None, scale=1.0):
+        if bias is None:
+            op("a", lambda: g.scalar.activation(ap(out), ap(a), func), [a], [out], el(width(out)) + 0.02)
+        else:
+            op("a", lambda: g.scalar.activation(ap(out), ap(a), func, bias=ap(bias), scale=scale), [a, bias], [out], el(width(out)) + 0.02)
 
     def iota(out, pat, base, cm=0):
         kw = {} if SCRATCH[out[0]][2] == I32 else {"allow_small_or_imprecise_dtypes": True}
-        op("g", lambda: g.iota(ap(out), pat, base, cm, **kw), [], [out], 0.13 + 2 * CYCLE * width(out))
+        op("g", lambda: g.iota(ap(out), pat, base, cm, **kw), [], [out], 0.3 + 2 * CYCLE * width(out))
 
     def quant(dst, d0, d1, src, s0, s1):
         op("v", lambda: g.vector.quantize_mx(T[dst][:, d0:d1], T[dst + "s"][:, d0:d1], T[src][:, s0:s1]), [X(src, s0, s1)], [X(dst, d0, d1), X(dst + "s", d0, d1)], 0.07 + 0.00022 * (s1 - s0))
@@ -372,17 +376,21 @@ def rank_program(g, core, T, topo):
         op("t", lambda: g.tensor.matmul_mx(T[bank][:, 0:n], T[l][:, l0:l0 + 128], T[l + "s"][:, l0:l0 + 128], T[r][:, r0:r0 + n], T[r + "s"][:, r0:r0 + n], start, stop),
            [X(l, l0, l0 + 128), X(l + "s", l0, l0 + 128), X(r, r0, r0 + n), X(r + "s", r0, r0 + n)], [X(bank, 0, n)], PIPE + 0.001 * (n + 16))
 
-    def pick(dst, n, win, a, b, off):
+    def pick(dst, d0, n, win, a, b, off):
         ov = X(off[0], off[1], off[1] + n // 16)
-        op("a", lambda: g.scalar.activation(T[dst + "s"][:, 0:n], T[win + "s"][:, a:b].indirect(ap(ov)), AF.Copy), [X(win + "s", a, b), ov], [X(dst + "s", 0, n)], el(n, 1.5) + 0.02)
-        op("v", lambda: g.vector.tensor_copy(T[dst][:, 0:n].bitcast(dt.uint32), T[win][:, a:b].bitcast(dt.uint32).indirect(ap(ov))), [X(win, a, b), ov], [X(dst, 0, n)], el(n, 1.5))
+        op("a", lambda: g.scalar.activation(T[dst + "s"][:, d0:d0 + n], T[win + "s"][:, a:b].indirect(ap(ov)), AF.Copy), [X(win + "s", a, b), ov], [X(dst + "s", d0, d0 + n)], el(40 + 1.5 * n) + 0.02)
+        op("v", lambda: g.vector.tensor_copy(T[dst][:, d0:d0 + n].bitcast(dt.uint32), T[win][:, a:b].bitcast(dt.uint32).indirect(ap(ov))), [X(win, a, b), ov], [X(dst, d0, d0 + n)], el(40 + 1.5 * n))
+
+    def gather(out, win, ov):
+        either(lambda: g.vector.tensor_copy(ap(out), ap(win).indirect(ap(ov))), lambda: g.scalar.activation(ap(out), ap(win).indirect(ap(ov)), AF.Copy),
+               [win, ov], [out], el(40 + 1.5 * width(out)))
 
     def send1(x, src, s0, between=lambda: None):
         n, own, ps = NX[x], _owners(x, order), src + "s"
         fo = [r for r in own if r in far]
         p, w = s0 + n * own.index(fo[0]), n * len(fo)
-        send([(_codes(T, src, p, p + w), [(hs[0 if x == 2 else 1], _codes(T, "RC%d" % x, 0, w))], e_on)], "qc%d" % x, [X(src, p, p + w)])
-        send([(T[ps][:, p:p + w], [(hs[3 if x == 2 else 2], T["RC%ds" % x][:])], e_on)], "qs%d" % x, [X(ps, p, p + w)])
+        fc = (_codes(T, src, p, p + w), [(hs[0 if x == 2 else 1], _codes(T, "RC%d" % x, 0, w))], e_on, "qc%d" % x)
+        fp = (T[ps][:, p:p + w], [(hs[3 if x == 2 else 2], T["RC%ds" % x][:])], e_on, "qs%d" % x)
         mc, mp, rd, rp = [], [], [], []
         for i, r in enumerate([r for r in near if r in own]):
             c = s0 + n * own.index(r)
@@ -391,8 +399,13 @@ def rank_program(g, core, T, topo):
             mp.append((T[ps][:, c:c + n], [(T.cores[r], T["LD%ds" % x][:, n * me:n * me + n])], e))
             rd.append(X(src, c, c + n))
             rp.append(X(ps, c, c + n))
-        between()
-        if mc:
+        if x == 1:
+            send([fc] + mc, "a1", [X(src, p, p + w)] + rd)
+            send([fp] + mp, "a1", [X(ps, p, p + w)] + rp)
+        else:
+            send([fc], None, [X(src, p, p + w)])
+            send([fp], None, [X(ps, p, p + w)])
+            between()
             send(mc, "a%d" % x, rd)
             send(mp, "a%d" % x, rp)
         if me in own:
@@ -416,176 +429,186 @@ def rank_program(g, core, T, topo):
         oth = [(base + n * i, r) for i, r in enumerate(own) if r != me]
         arrive([X(k, c, c + n) for k in (nm, nm + "s") for c, r in oth], "b%d" % x, len(oth) * 2 * len(e_off), LATE["b%d" % x])
 
-    def send_scores(k, src, c0, w):
-        sap = T[src][:, c0:c0 + w]
-        rd = [X(src, c0, c0 + w)]
-        fm = (sap, [(h, T["fRS%d" % k][:]) for h in (hs[1:3] if k == 1 else (hs[0], hs[3]))], e_on, "sr%d" % k)
-        nm = (sap, [(T.cores[r], T[src][:, c0:c0 + w]) for r in near], e_off, "sn%d" % k)
+    def send_scores(k, src, dst):
+        fm = (ap(src), [(h, T["fRS%d" % k][:]) for h in (hs[0], hs[3])], e_on, "sr%d" % k)
+        nm = (ap(src), [(T.cores[r], T[dst][:, 4 * me:4 * me + 1]) for r in near], e_off, "sn%d" % k)
         for mv in ([fm], [nm]) if k == 1 else ([fm, nm],):
-            send(mv, None, rd)
-        arrive([X(src, 4 * r, 4 * r + w) for r in near], "sn%d" % k, len(near) * len(e_off), LATE["n%d" % k])
-        arrive([X(src, 4 * r, 4 * r + w) for r in far], "sa%d" % k, len(far) * len(e_off), LATE["s%d" % k])
+            send(mv, None, [src])
+        arrive([X(dst, 4 * r, 4 * r + 1) for r in near], "sn%d" % k, len(near) * len(e_off), LATE["n%d" % k])
+        arrive([X(dst, 4 * r, 4 * r + 1) for r in far], "sa%d" % k, len(far) * len(e_off), LATE["s%d" % k])
 
-    def load(q, buf, c0, c1, ext):
-        dma(q, T[buf][:, c0:c1], ext, [], [X(buf, c0, c1)])
+    def load(q, buf, c0, c1, ext, late):
+        dma(q, T[buf][:, c0:c1], ext, [], [X(buf, c0, c1)], late)
 
-    load("y", "UZ", 4, 8, T.z[:, 0:4])
-    load("a", "UZ", 0, 4, T.u[:, 0:4])
-    load("y", "BT", 384, 768, T.dm[:])
-    load("a", "BT", 0, 384, T.lv[:])
-    load("y", "BT", 768, 1152, T.nz[:])
-    load("a", "WT", 0, 512, T.w[:])
-    iota(X("PI"), [[1, 1]], 0, 1)
-    iota(X("fR96"), [[0, 3], [1, 32]], 0)
-    iota(X("fROW"), [[16, 6], [0, 2], [1, 16]], 0)
-    CT = lambda a, b, r0=0, r1=128: X("fCT", a, b, r0, r1)
-    iota(CT(96, 128), [[0, 8], [1, 4]], 4 * m)
-    iota(X("fJB"), [[16, 6]], 0)
-    e1 = _owners(1, order)
-    cl = [order.index(s) % 2 for s in range(8)]
-    a0, a1 = -cl[me] % 2, (1 - cl[me]) % 2
-    iota(X("fPR"), [[a1 - a0, 2], [0, 2], [2, 16]], a0)
-    if me in e1:
-        ow = e1.index(me)
-        pairs = [(order[2 * q + ow], order[2 * q + 1 - ow]) for q in range(4)]
-        for q, (s0, s1) in enumerate(pairs):
-            iota(X("fGR", 32 * q, 32 * q + 32), [[2, 16], [1 + 32 * (s1 - s0), 2]], 32 * s0)
+    load("y", "UZ", 4, 8, T.z[:, 0:4], "small")
+    load("a", "UZ", 0, 4, T.u[:, 0:4], "small")
+    load("y", "BT", 384, 768, T.dm[:], "big")
+    load("a", "BT", 0, 384, T.lv[:], "big")
+    load("y", "BT", 768, 1152, T.nz[:], "big")
+    load("a", "WT", 0, 512, T.w[:], "big")
+    e1, x2 = _owners(1, order), _owners(2, order)
+    cl = order.index(me) % 2
+    iota(X("PJ", 5, 6), [[1, 1]], 0, 1)
+    iota(X("fTG", 0, 64), [[32, 2], [0, 2], [1, 16]], 0)
+    iota(X("fTG2"), [[0, 8], [2, 16]], 0)
+    iota(X("fPR", 0, 128, 0, 64), [[1, 128]], P * me - 32)
+    iota(X("fPR", 0, 128, 64, 128), [[1, 128]], P * me)
     ms(X("ONB"), 1.0)
-    ms(X("fON"), 1.0)
     ms(X("HAF"), 0.5)
-    ms(CT(192, 320, 0, 64), -1000.0)
-    ms(CT(320, 384, 64, 128), -1000.0)
-    op("g", lambda: g.affine_select(T.DG[:], T.HAF[:], [[-1, 128]], O.is_equal, 0.0, 0, 1), [X("HAF")], [X("DG")], 0.4)
-    for i, k in enumerate((31, 15, 3, 1)):
-        op("v", lambda k=k, i=i: g.vector.tensor_scalar(T.PJ[:, i:i + 1], T.PI[:], k, None, O.bitwise_and), [X("PI")], [X("PJ", i, i + 1)], el(1))
-    cp(X("fPC", 0, 3), X("PJ", 0, 3))
-    cp(X("fPA", 0, 1), X("PJ", 3, 4))
-    P32, P16, P4 = X("fPC", 0, 1), X("fPC", 1, 2), X("fPC", 2, 3)
-    for a in range(4):
-        ts(X("fLC", 0, 1, 32 * a, 32 * a + 32), X("fPC", 0, 1, 32 * a, 32 * a + 32), 32.0 * (a % 2), O.add)
-    ts(X("fTL"), X("fR96", 0, 32), X("fLC"), O.add, P32, O.subtract)
-    step = 2.0 ** -24
-    ms(X("fFT", 0, 96, 64, 128), 1.0)
-    ms(X("fFK", 0, 96, 0, 64), 1.0)
-    for n, r0 in (("fFT", 0), ("fFK", 64)):
-        v = X(n, 0, 96, r0, r0 + 64)
-        ts(v, X("fR96", 0, 96, r0, r0 + 64), X("fPC", 0, 1, r0, r0 + 64), O.is_lt, -step, O.mult)
-        ts(v, v, 1.0, O.add)
-    for b in range(3):
-        ts(X("fPC", 3 + b, 4 + b), P32, 32.0 * b, O.add)
+    op("g", lambda: g.affine_select(T.MK[:], T.HAF[:], [[1, 128]], O.is_ge, -0.5, 0, -1), [X("HAF")], [X("MK")], 0.55)
+    for i, k in enumerate((31, 15, 3, 1, 63)):
+        op("v", lambda k=k, i=i: g.vector.tensor_scalar(T.PJ[:, i:i + 1], T.PJ[:, 5:6], k, None, O.bitwise_and), [X("PJ", 5, 6)], [X("PJ", i, i + 1)], el(1))
+    cp(X("fPC", 0, 6), X("PJ"))
+    PC = lambda i: X("fPC", i, i + 1)
+    P32, P16, P4, PAR, LC, PF = (PC(i) for i in range(6))
+    cp(X("fTG", 64, 128), X("fTG", 0, 64))
+    ms(blk(X("fTG", 0, 64), 0), -1000.0)
+    ms(blk(X("fTG", 64, 128), 3), -1000.0)
+    ms(blk(X("fTG2"), 0), -1000.0)
+    ms(X("MT"), 0.0)
+    ts(PC(6), PF, P16, O.subtract)
+    times(X("MT", 0, 16, 0, 128, 5), X("ONB", 0, 4), PC(6))
+    times(X("MT", 16, 32, 0, 128, 5), X("ONB", 0, 4), P16)
+    quant("MQ", 0, 132, "MT", 0, 528)
+    ms(X("fKR", 0, 32, 0, 64), 0.0)
+    ms(X("fKR", 96, 128, 64, 128), 0.0)
     cp(X("fUZ"), X("UZ"))
     for nm, c, q in (("ZT", 4, "ZQ"), ("UT", 0, "UQ")):
         for t in range(4):
             times(X(nm, t, 512, 0, 128, 4), X("ONB"), X("fUZ", c + t, c + t + 1))
         quant(q, 0, 128, nm, 0, 512)
-    quant("QT", 0, 288, "BT", 0, 1152)
-    mm("p0", 192, "ZQ", 0, "QT", 0)
-    mm("p1", 128, "UQ", 0, "QT", 0)
-    act(X("fK0", 0, 96, 0, 64), X("p0", 96, 192, 0, 64), AF.Abs)
-    act(X("fK0", 0, 96, 64, 128), X("p1", 0, 96, 64, 128), AF.Abs)
-    act(X("fK0", 96, 192), X("p0", 0, 96), AF.Abs)
+    quant("QT", 0, 192, "BT", 0, 768)
+
+    def ahead(i, row, col, sign, c0, n, out):
+        red(X("fCD", i, i + 1), X(col, 0, 1), O.add, sign > 0, True)
+        s = X("SG", 128 * i, 128 * i + n)
+        act(s, row, AF.Sign, X("fCD", i, i + 1), float(sign))
+        tt(out, s, X("MK", c0, c0 + n), O.is_gt)
+        total(X("fRK", i, i + 1), out)
+
+    def places(q, out, n):
+        quant(q, 0, 128, "HT", 0, 512)
+        mm("p1", 128, q, 0, "MQ", 0, True, False)
+        mm("p1", 128, q, 0, "MQ", 4, False, True)
+        cp(X(out, 0, n), X("p1", 0, n))
+
+    mm("p0", 128, "ZQ", 0, "QT", 64)
+    mm("p1", 128, "QT", 64, "ZQ", 0)
+    mm("p6", 128, "UQ", 0, "QT", 0)
+    mm("p7", 128, "QT", 0, "UQ", 0)
+    mm("p2", 128, "ZQ", 0, "QT", 0)
+    act(X("fAD", 32, 128), X("p0", 32, 128), AF.Abs)
+    act(X("fAL"), X("p6", 0, 96), AF.Abs)
+    ahead(0, X("fAD", 32, 128), "p1", 1, 32, 96, X("fCC", 0, 96))
+    ahead(1, X("fAL"), "p7", -1, 0, 96, X("fCC", 96, 192))
+    for t in range(2):
+        ts(X("HT", t, 256, 0, 128, 4), X("fTG", 0, 64), X("fRK", 0, 1), O.subtract, -16.0 * t, O.is_equal)
+        ts(X("HT", 256 + t, 512, 0, 128, 4), X("fTG", 64, 128), X("fRK", 1, 2), O.subtract, -16.0 * t, O.is_equal)
+        ts(X("HT", 2 + t, 512, 0, 128, 4), X("fTG2"), X("fRK", 0, 1), O.subtract, -float((t - cl) % 2), O.is_equal)
+    places("HQ", "LO", 4)
     low = 2.0 ** -110
-    ts(X("fKK", 0, 96, 0, 64), X("fK0", 0, 96, 0, 64), low, O.max)
-    ts(X("fKK", 0, 96, 64, 128), X("fK0", 0, 96, 64, 128), -1.0, O.mult, -low, O.min)
-    ts(X("fKK", 96, 192), X("fK0", 96, 192), low, O.max)
-    tr(X("fTT"), X("fKK"))
-    tt(X("fKF"), X("fKK", 0, 96), X("fFK"), O.mult)
-    tt(X("fTF"), X("fTT", 0, 96), X("fFT"), O.mult)
-    for b in range(3):
-        s = X("fTT", 32 * b, 32 * b + 1)
-        if b:
-            ts(X("fCL", 96 * b, 96 * b + 32 * b), X("fKK", 0, 32 * b), s, O.is_ge)
-        if b < 2:
-            ts(X("fCL", 96 * b + 32 * b + 32, 96 * b + 96), X("fKK", 32 * b + 32, 96), s, O.is_gt)
-        tt(X("fCL", 128 * b, 128 * b + 32), X("fKF", 32 * b, 32 * b + 32), X("fTF", 32 * b, 32 * b + 32), O.is_gt)
-    for b in range(3):
-        total(X("fRB", b, b + 1), X("fCL", 96 * b, 96 * b + 96))
-    for i, val in enumerate((lambda b: X("fTT", 32 * b, 32 * b + 1), lambda b: X("fPC", 3 + b, 4 + b), lambda b: X("fTT", 96 + 32 * b, 97 + 32 * b))):
-        for b in range(3):
-            ts(X("fHL", 96 * i + 32 * b, 96 * i + 32 * b + 32), X("fTL"), X("fRB", b, b + 1), O.is_equal, val(b), O.mult)
-        tr(X("fHT", 96 * i, 96 * i + 96), X("fHL", 96 * i, 96 * i + 96))
-        total(X("fSD", 4 * me + i, 4 * me + i + 1), X("fHT", 96 * i, 96 * i + 96))
-    send_scores(1, "fSD", 4 * me, 1)
-
-    B0 = lambda n, c0=0, c1=None: X(n, c0, c1, 0, 32)
-    ts(B0("fPM"), B0("fPR"), B0("fPC", 0, 1), O.is_equal)
-    times(B0("fHP"), B0("fPM"), B0("fSD", 4 * me + 1, 4 * me + 2))
-    tr(B0("fHPt"), B0("fHP"))
-    total(B0("fDL", 0, 1), B0("fHPt", 0, 32))
-    total(B0("fDL", 1, 2), B0("fHPt", 32, 64))
-    for d in range(4):
-        cp(("DPo", 0, 2, 32 * d, 32 * d + 32, 1), ("fW",) + X("fDL")[1:3] + (0, 32, 1))
-    pick("SL1", 32, "QT", 96, 192, ("DPo", 0))
+    ts(X("fKR", 32, 128, 0, 64), X("fAD", 32, 128, 0, 64), low, O.max)
+    ts(X("fKR", 0, 96, 64, 128), X("fAL", 0, 96, 64, 128), -1.0, O.mult, -low, O.min)
+    gather(X("fRO"), X("fKR"), X("LO", 0, 2))
+    tr(X("fKT"), X("fRO"))
+    KEY = X("fKT", 0, 1)
+    pick("SL1", 0, 32, "QT", 64, 192, ("LO", 2))
     send1(1, "SL1", 0)
+    send_scores(1, KEY, "fSD")
+    cp(X("fSD", 4 * me, 4 * me + 1), KEY)
+    act(X("fZA"), X("p2", 0, 128), AF.Abs)
+    ts(X("fZR"), X("fZA"), low, O.max)
+    gather(X("fGZ", 0, 32), X("fPR"), X("LO", 0, 2))
+    gather(X("fGZ", 32, 64), X("fZR"), X("LO", 0, 2))
+    tr(X("fGT"), X("fGZ"))
+    GN, ZL = X("fGT", 0, 1), X("fGT", 32, 33)
 
-    LCv = X("fLC")
-    ts(CT(0, 64), X("fROW", 0, 64), LCv, O.subtract)
-    ts(CT(64, 96), X("fR96", 0, 32), LCv, O.subtract)
-    ts(CT(128, 160), X("fR96", 0, 32), LCv, O.subtract, 32.0, O.add)
+    f0 = len(nodes)
+    iota(X("fROW"), [[16, 6], [0, 2], [1, 16]], 0)
+    iota(X("fR32"), [[1, 32]], 0)
+    iota(X("fCT", 96, 128), [[0, 8], [1, 4]], 4 * m)
+    iota(X("fJB"), [[16, 6]], 0)
+    ms(X("BT", 1152, 1280), 0.0)
+    quant("QT", 192, 320, "BT", 768, 1280)
+    ms(X("fON"), 1.0)
+    for n in (32, 64):
+        ms(X("R%d" % n), 1.0)
+        ms(X("R%d" % n, 0, None, 0, 128, n), 0.0)
+    CT = lambda a, b: X("fCT", a, b)
+    ts(CT(0, 32), X("fR32"), LC, O.subtract)
+    ts(CT(32, 64), X("fR32"), LC, O.subtract, 32.0, O.add)
     ts(CT(96, 128), CT(96, 128), P32, O.is_equal)
-    x2 = _owners(2, order)
+    ms(X("fCTX", 64, 128, 0, 64), -1000.0)
+    ts(X("fCTX", 0, 64, 0, 64), X("fROW", 0, 64, 0, 64), rows(LC, 0, 64), O.subtract, 32.0, O.add)
+    ts(X("fCTX", 0, 128, 64, 128), X("fROW", 0, 128, 64, 128), rows(LC, 64, 128), O.subtract)
     if me in x2:
-        ts(X("fMM", 0, 32), X("fROW", 0, 32), 16.0 * (x2.index(me) % 2), O.add, P32, O.is_equal)
-    ts(X("fGV", 0, 1), X("fSD", 4 * me + 1, 4 * me + 2), 128.0 * me, O.add)
-    cp(X("fGV", 1, 2, 32, 64), X("fGV", 0, 1, 32, 64))
-    cp(X("fGV", 1, 2, 64, 128), X("fGV", 0, 1, 64, 128))
-    ts(B0("fNS2"), B0("fPA", 0, 1), float(cl[me]), O.not_equal, 1024.0, O.mult)
-    tt(B0("fGV", 1, 2), B0("fGV", 0, 1), B0("fNS2"), O.add)
-    ms(X("fNL", 4 * me, 4 * me + 1, 96, 128), 0.0)
+        ts(X("fMM"), X("fROW", 0, 32), 16.0 * (x2.index(me) % 2), O.add, P32, O.is_equal)
+    else:
+        iota(X("fTG3"), [[0, 8], [1, 16]], 0)
+    GQ, VO, VK = (X("fGV", i, i + 1) for i in range(3))
+    ts(blk(PC(7), 0), blk(PAR, 0), float(cl), O.not_equal, 1024.0, O.mult)
+    ts(blk(GQ, 0), blk(GN, 0), blk(PC(7), 0), O.add)
+    ts(rows(VO, 0, 64), rows(GN, 0, 64), float(P - P * me), O.add)
+    ts(rows(VO, 64, 128), rows(GN, 64, 128), -float(P * me), O.add)
+    ts(PC(8), LC, 32.0, O.is_lt)
+    ts(PC(9), LC, 32.0, O.is_ge)
+    times(X("fGV", 3, 4), KEY, PC(8))
+    ts(VK, GN, PC(9), O.mult, X("fGV", 3, 4), O.add)
+    ts(X("fTH", 0, 64), X("fROW", 0, 64), P32, O.is_le, 3072.0, O.mult)
+    ts(X("fTH", 64, 128), X("fROW", 0, 64), P32, O.not_equal, 3072.0, O.mult)
+    ts(X("fTH"), X("fTH"), 1024.0, O.add)
+    ts(PC(10), P32, 1.0, O.add)
     for h in range(2):
-        ts(X("fKC", h, h + 1), P16, 16.0 * h, O.add)
-        ts(X("fKM", 32 * h, 32 * h + 32), X("fR96", 0, 32), X("fKC", h, h + 1), O.is_equal, 64.0, O.mult)
-        ts(X("fOT", 32 * h, 32 * h + 32), X("fR96", 0, 32), X("fKC", h, h + 1), O.is_lt)
-    tt(X("fKM"), X("fKM"), X("fOT"), O.add)
-    if me in e1:
-        par, npar = B0("fPA", 0, 1), B0("fPA", 1, 2)
-        ts(npar, par, -1.0, O.mult, 1.0, O.add)
-        ts(B0("fPA", 2, 3), B0("fPC", 0, 1), 0.5, O.mult)
-        for q, (s0, s1) in enumerate(pairs):
-            ts(B0("fAD", q, q + 1), par, 16.0 * (s1 - s0) - 0.5, O.mult, 16.0 * s0, O.add)
-            tt(B0("fAD", q, q + 1), B0("fAD", q, q + 1), B0("fPA", 2, 3), O.add)
-            ts(B0("fGP", q, q + 1), par, 32.0 * (s1 - s0), O.mult, B0("fPC", 0, 1), O.add)
-            ts(B0("fGP", q, q + 1), B0("fGP", q, q + 1), 32.0 * s0, O.add)
-            ff = B0("fFF", 128 * q, 128 * q + 128)
-            ts(ff, B0("fGR"), B0("fGP", q, q + 1), O.is_ge, -step, O.mult)
-            ts(ff, ff, 1.0, O.add)
-    ts(CT(192, 320, 64, 128), X("fROW", 0, 128, 64, 128), X("fLC", 0, 1, 64, 128), O.subtract)
-    ts(CT(320, 384, 0, 64), X("fROW", 0, 64, 0, 64), X("fLC", 0, 1, 0, 64), O.subtract, 32.0, O.add)
-    ts(X("fPT"), X("fROW"), 128.0 * me, O.add)
+        ts(PC(11 + h), P16, -1.0, O.mult, 17.0 - 16 * h, O.add)
+    ts(PC(13), P32, 32.0, O.add)
+    ts(X("fRP", 0, 64), X("fROW", 0, 64), PC(13), O.subtract, -1.0, O.mult)
+    ts(X("fRP", 64, 96), X("fR32"), PC(13), O.subtract, -1.0, O.mult)
+    ts(X("fID"), X("fR32"), P32, O.is_equal)
+    ts(X("fPT"), X("fROW"), float(P * me), O.add)
     ts(X("fJB"), X("fJB"), P16, O.add)
-    ts(X("fRP", 0, 64), X("fROW", 0, 64), P32, O.subtract)
-    ts(X("fRP", 64, 96), X("fR96", 0, 32), P32, O.subtract)
-    ms(X("fVO", 0, 1, 0, 64), 96.0)
-    ms(X("fVO", 0, 1, 64, 128), 0.0)
-    for b in range(8):
-        ms(X("ET", 256 * b, 256 * b + 256), 0.0)
-    for b in range(4):
-        cp(X("ET", 513 * b, 512 * b + 512, 0, 128, 4), X("DG"))
-    for b in range(4):
-        quant("EQ", 128 * b, 128 * b + 128, "ET", 512 * b, 512 * b + 512)
+    op("g", lambda: g.affine_select(T.DG[:], T.HAF[:], [[-1, 128]], O.is_equal, 0.0, 0, 1), [X("HAF")], [X("DG")], 0.55)
+    for i in range(2):
+        for j in range(2):
+            ms(X("ET", 528 * i + 264 * j, 528 * i + 264 * j + 264), 0.0)
+        cp(X("ET", 528 * i + 2 + i, 528 * i + 514, 0, 128, 4), X("DG"))
+        for j in range(2):
+            quant("EQ", 128 * (i + 2 * j), 128 * (i + 2 * j) + 128, "ET", 528 * i + 2 - 2 * j, 528 * i + 514 - 2 * j)
     quant("WQ", 0, 128, "WT", 0, 512)
     ms(X("FLo", 6, 8), 0)
-    for d in ("UD", "NP1", "BP2", "NP2"):
-        dcol("y", d, 32, "QT", 0, 96)
+    ms(X("NT", 128, 512), 0.0)
+    ms(X("fNK", 32, 33), -low)
+    dcol("y", "MV", 96, "QT", 0, 96)
     dcol("y", "DW", 0, "QT", 96, 96)
+    for b in range(4):
+        mm("p%d" % (2 + b), 128, "EQ", 128 * b, "QT", 192)
+        act(X("fDN", 96 * b, 96 * b + 96), X("p%d" % (2 + b), 0, 96), AF.Copy)
+    mids = [X("fFM", i, i + 1) for i in range(6)]
+    for v, c in zip(mids, (64, 320, 96, 448, 128, 192)):
+        ts(v, P32, float(c), O.add)
+    a64, a320, a96, a448, a128, a192 = mids
+    fill.update(range(f0, len(nodes)))
 
     def key(s):
         return X("fSD", 4 * s, 4 * s + 1)
 
-    def rows4(v, a):
-        return (v[0], v[1], v[2], 32 * a, 32 * a + 32, v[5])
+    if me in e1:
+        mm("p0", 128, "ZQ", 0, "LD1", 0)
+        mm("p7", 128, "LD1", 0, "ZQ", 0)
+        act(X("fOA"), X("p0", 0, 128), AF.Abs)
+        ahead(2, X("fOA"), "p7", 1, 0, 128, X("fOC"))
+        for t in range(2):
+            if e1.index(me):
+                ts(X("HT", t, 512, 0, 128, 4), X("fTG3"), X("fRK", 2, 3), O.subtract, -16.0 * t, O.is_equal)
+            else:
+                ts(X("HT", t, 512, 0, 128, 4), X("fTG3"), X("fRK", 2, 3), O.add, 17.0 - 16 * t, O.is_equal)
+        places("HQ2", "O1o", 2)
+        pick("MG1", 0, 32, "LD1", 0, 128, ("O1o", 0))
 
-    def to_all(out, src, a):
-        for d in range(4):
-            cp(rows4(out, d), rows4(src, a))
-
-    times(X("fEO"), X("fON"), key(me))
-    tr(X("fRO"), X("fEO"))
     planes = (pa, pb) if rank in pa else (pb, pa)
     for i, grp in enumerate((near, far)):
         n, pl = 32 * len(grp), planes[i]
         for a in range(4):
-            cp(X("fSWA", 4 * i, 4 * i + 4, 32 * a, 32 * a + 32), ("fSD", 4 * pl[0], 4 * pl[-1] + 1, 32 * (a ^ 1), 32 * (a ^ 1) + 32, 4 * (pl[1] - pl[0])))
+            cp(blk(X("fSWA", 4 * i, 4 * i + 4), a), ("fSD", 4 * pl[0], 4 * pl[-1] + 1, 32 * (a ^ 1), 32 * (a ^ 1) + 32, 4 * (pl[1] - pl[0])))
         for j, s in enumerate(grp):
             o = O.is_le if s < me else O.is_lt
             w = 4 * i + pl.index(s)
@@ -595,252 +618,170 @@ def rank_program(g, core, T, topo):
             tr(X(v, 128 * i, 128 * i + n), X(w, 128 * i, 128 * i + n))
             total(X("fNF", 2 * k + i, 2 * k + i + 1), X(v, 128 * i, 128 * i + n))
         if i == 0:
-            ts(X("fCTO"), CT(0, 64), X("fNF", 0, 1), O.subtract)
+            ts(X("fCT1"), CT(0, 32), X("fNF", 0, 1), O.subtract)
             tt(X("fNF", 2, 3), X("fNF", 0, 1), X("fNF", 2, 3), O.add)
-    ts(X("fCN"), X("fNF", 0, 1), X("fNF", 1, 2), O.add)
-    ts(X("fCF"), X("fNF", 2, 3), X("fNF", 1, 2), O.add, X("fNF", 3, 4), O.add)
-    NL = lambda a, n="fNL": X(n, 4 * me, 4 * me + 1, 32 * a, 32 * a + 32)
-    T4 = lambda a, c: X("fT4", c, c + 1, 32 * a, 32 * a + 32)
-    TS = lambda a, c: X("fTS", c, c + 1, 32 * a, 32 * a + 32)
-    entries = lambda i, t, n, v: ts(X("fHN", 32 * i, 32 * i + 32), t, X(n), O.is_equal, v, O.mult)
-    entries(0, CT(64, 96), "fCN", X("fGV", 1, 2))
-    entries(1, CT(64, 96), "fCN", X("fSD", 4 * me + 2, 4 * me + 3))
-    tr(X("fHM", 0, 64), X("fHN", 0, 64))
-    for a in (0, 2):
-        total(NL(a), X("fHM", 0, 32, 32 * a, 32 * a + 32))
-    total(T4(2, 0), X("fHM", 32, 64, 64, 96))
-    cp(NL(1), T4(2, 0))
-    send_scores(3, "fNL", 4 * me, 1)
-
-    if me in e1:
-        nq = [2 * ow, 2 * ow + 1]
-        n0, f0 = 64 * ow, 64 - 64 * ow
-        for q in nq + [q for q in range(4) if q not in nq]:
-            k4 = B0("fK4", q, q + 1)
-            times(B0("fKT", q, q + 1), par, B0("fSD", 4 * pairs[q][1], 4 * pairs[q][1] + 1))
-            ts(k4, npar, B0("fSD", 4 * pairs[q][0], 4 * pairs[q][0] + 1), O.mult, B0("fKT", q, q + 1), O.add)
-            times(B0("fKE", 32 * q, 32 * q + 32), B0("fON"), k4)
-            if q % 2:
-                tr(B0("fKR", 32 * q - 32, 32 * q + 32), B0("fKE", 32 * q - 32, 32 * q + 32))
-
-        def ahead(q, c0, c1, out):
-            w, c = B0("fWW", 128 * q + c0, 128 * q + c1), B0("fCC", 128 * q + c0, 128 * q + c1)
-            tt(w, B0("fKR", c0, c1), B0("fFF", 128 * q + c0, 128 * q + c1), O.mult)
-            ts(c, w, B0("fK4", q, q + 1), O.is_ge)
-            total(out, c)
-
-        for i, q in enumerate(nq):
-            ahead(q, n0, n0 + 64, B0("fN1", q, q + 1))
-            ts(B0("fCO", 64 * i, 64 * i + 64), B0("fROW", 0, 64), B0("fN1", q, q + 1), O.subtract)
-        for q in range(4):
-            if q in nq:
-                ahead(q, f0, f0 + 64, B0("fRB2", q, q + 1))
-            else:
-                ahead(q, 0, 128, B0("fRB2", q, q + 1))
-            for h in range(2):
-                t = B0("fCO", 64 * nq.index(q) + 32 * h, 64 * nq.index(q) + 32 * h + 32) if q in nq else B0("fROW", 32 * h, 32 * h + 32)
-                ts(B0("fHO", 128 * h + 32 * q, 128 * h + 32 * q + 32), t, B0("fRB2", q, q + 1), O.is_equal, B0("fAD", q, q + 1), O.mult)
-        for h in range(2):
-            tr(B0("fHQ", 128 * h, 128 * h + 128), B0("fHO", 128 * h, 128 * h + 128))
-            total(B0("fMO", h, h + 1), B0("fHQ", 128 * h, 128 * h + 128))
-        for d in range(4):
-            cp(("O1o", 0, 2, 32 * d, 32 * d + 32, 1), B0("fMO"))
-        pick("MG1", 32, "LD1", 0, 128, ("O1o", 0))
+    CF = X("fCF")
+    ts(CF, X("fNF", 2, 3), X("fNF", 1, 2), O.add, X("fNF", 3, 4), O.add)
+    NF1 = X("fNF", 1, 2)
+    ts(blk(X("fHN", 0, 32), 0), blk(X("fCT1"), 0), blk(NF1, 0), O.is_equal, blk(GQ, 0), O.mult)
+    ts(rows(X("fHN", 0, 32), 64, 128), rows(X("fCT1"), 64, 128), rows(NF1, 64, 128), O.is_equal, rows(GN, 64, 128), O.mult)
+    ts(blk(X("fHN", 0, 32), 1), blk(X("fCT1"), 2), blk(NF1, 2), O.is_equal, blk(ZL, 2), O.mult)
+    tr(X("fHM", 0, 32), X("fHN", 0, 32))
+    total(X("fNL", 4 * me, 4 * me + 1), X("fHM", 0, 32))
+    send_scores(3, X("fNL", 4 * me, 4 * me + 1), "fNL")
     send2(1)
-
-    entries(2, CT(128, 160), "fCF", X("fGV", 0, 1))
-    entries(3, CT(128, 160), "fCF", key(me))
-    tr(X("fHM", 64, 128), X("fHN", 64, 128))
-    for i in (2, 3):
-        total(X("fT4", i, i + 1), X("fHM", 32 * i, 32 * i + 32))
+    ts(X("fHN", 32, 64), CT(32, 64), CF, O.is_equal, VK, O.mult)
     for a in range(4):
-        c = 2 if a % 2 else 3
-        cp(TS(a, c - 2), T4(a ^ 1, c))
-        tt(NL(a, "fNM"), T4(a, c), TS(a, c - 2), O.add)
-    send_scores(4, "fNM", 4 * me, 1)
+        ts(blk(X("fHN", 64, 96), a), blk(CT(32, 64), a ^ 1), blk(CF, a ^ 1), O.is_equal, blk(GN if a % 2 else KEY, a ^ 1), O.mult)
+    tr(X("fHM", 32, 96), X("fHN", 32, 96))
+    total(X("fNM", 4 * me, 4 * me + 1), X("fHM", 32, 96))
+    send_scores(4, X("fNM", 4 * me, 4 * me + 1), "fNM")
 
-    ts(X("fH1"), X("fCTO"), X("fNF", 1, 2), O.is_equal, X("fSD", 4 * me + 1, 4 * me + 2), O.mult)
-    tr(X("fH1t"), X("fH1"))
-    total(X("fOL", 0, 1), X("fH1t", 0, 32))
-    total(X("fOL", 1, 2), X("fH1t", 32, 64))
-
-    def owners(parts, mul, add, i):
-        n = len(parts)
-        for j, (mask, col) in enumerate(parts):
-            ts(X("fMW", 128 * i + 32 * j, 128 * i + 32 * j + 32), mask, col, O.mult)
-        tr(X("fMV", 128 * i, 128 * i + 32 * n), X("fMW", 128 * i, 128 * i + 32 * n))
-        red(X("fOM", 2 * i, 2 * i + 1), X("fMV", 128 * i, 128 * i + 32 * n))
-        ts(X("fOM", 2 * i + 1, 2 * i + 2), X("fOM", 2 * i, 2 * i + 1), 63.5, O.subtract, 1.0 / 128, O.mult)
-        cp(X("MI", i, i + 1), X("fOM", 2 * i + 1, 2 * i + 2))
-        ts(X("Mo", 2 * i, 2 * i + 1), X("MI", i, i + 1), float(mul), O.mult, add, O.add)
-
-    tt(X("fVO", 1, 2), X("fVO", 0, 1), X("fSD", 4 * me + 1, 4 * me + 2), O.add)
-    ts(X("fH2"), CT(192, 384), X("fCF"), O.is_equal, X("fVO", 1, 2), O.mult)
+    ts(X("fH2"), X("fCTX"), CF, O.is_equal, VO, O.mult)
     tr(X("fH2t"), X("fH2"))
-    for c in range(6):
-        total(X("fOX", c, c + 1), X("fH2t", 32 * c, 32 * c + 32))
+    s4 = sums(X("fH2s"), X("fH2t"), 32)
     for a in range(4):
-        to_all(X("fXO", 6 * a, 6 * a + 6), X("fOX"), a)
-    tt(X("fXP", 0, 12), X("fXO", 0, 12), X("fXO", 12, 24), O.add)
-    tt(X("fXP", 12, 18), X("fXP", 0, 6), X("fXP", 6, 12), O.add)
-    cp(X("X2o"), X("fXP", 12, 18))
-    pick("SL2", 96, "QT", 0, 192, ("X2o", 0))
+        cp(blk(X("fXT"), a), blk(s4, a ^ 1))
+    tt(X("fXU"), s4, X("fXT"), O.add)
+    for h in (0, 64):
+        cp(X("X2o", 0, 4, h, h + 64), X("fXU", 0, 4, 64, 128))
+        cp(X("X2o", 4, 6, h, h + 64), X("fXU", 0, 2, 0, 64))
+    pick("SL2", 0, 96, "QT", 0, 192, ("X2o", 0))
     send1(2, "SL2", 0)
+    pick("MV", 64, 32, "QT", 192, 288, ("X2o", 0))
+    for b in range(4):
+        mm("p%d" % (2 + b), 128, "EQ", 128 * b, "MV", 64, True, False)
 
-    L1q, L2g, D1g, H2g = (X("fG4", i, i + 1) for i in range(4))
     red(X("fG2", 0, 1), ("fNL", 0, 32, 0, 128, 4))
-    DQ = X("fDQ")
-    to_all(DQ, X("fG2", 0, 1), 0)
-    ts(X("fOE"), X("fON"), DQ, O.mult, 1024.0, O.is_ge)
-    tr(X("fOR"), X("fOE"))
+    DQ = X("fDQ", 0, 1)
+    for d in range(4):
+        cp(blk(DQ, d), blk(X("fG2", 0, 1), 0))
+    ts(X("fUX", 32, 96), X("fTH", 64, 128), DQ, O.is_le, PC(10), O.mult)
+    ts(X("fUX", 0, 32), X("fTH", 0, 32), DQ, O.is_le)
+    ts(X("fUX", 96, 128), X("fTH", 32, 64), DQ, O.is_le)
+    tr(X("fUT"), X("fUX"))
+    sums(X("fUS"), X("fUT"), 64)
     for h in range(2):
-        tt(X("fOT", 32 * h, 32 * h + 32), X("fOR"), X("fKM", 32 * h, 32 * h + 32), O.mult)
-        total(X("fQ1", h, h + 1), X("fOT", 32 * h, 32 * h + 32))
-    tt(X("fQA"), X("fKC"), X("fQ1"), O.subtract)
-    for h in range(2):
-        ts(X("UOo", h, h + 1), X("fQ1", h, h + 1), 46.0, O.subtract, X("fQA", h, h + 1), O.max)
-    pick("UD", 32, "UO", 0, 36, ("UOo", 0))
+        ts(X("UOo", h, h + 1), X("fUS", 64 * h + 63, 64 * h + 64), PC(11 + h), O.add)
+    pick("MV", 32, 32, "UO", 0, 36, ("UOo", 0))
     red(X("fG2", 1, 2), ("fNM", 0, 32, 0, 128, 4))
     for a in range(4):
-        to_all(X("fGA", 2 * a, 2 * a + 2), X("fG2"), a)
+        for d in (a, a ^ 1):
+            cp(blk(X("fGA", 2 * a, 2 * a + 2), d), blk(X("fG2"), a))
+    cp(X("fGA", 0, 4, 64, 128), X("fGA", 0, 4, 0, 64))
+    cp(X("fGA", 4, 8, 0, 64), X("fGA", 4, 8, 64, 128))
     _, c2k, z1, c2g, L1g, o2k, _, o2g = (X("fGA", i, i + 1) for i in range(8))
-    ts(D1g, DQ, 1024.0, O.is_ge, -1024.0, O.mult)
-    tt(D1g, D1g, DQ, O.add)
-
-    to_all(X("LPo"), X("fOL"), 2)
-    pick("NP1", 32, "QT", 192, 288, ("LPo", 0))
-    for b in range(4):
-        mm("p%d" % (2 + b), 128, "EQ", 128 * b, "NP1", 0, True, False)
-    ts(X("fOW", 0, 1), L1g, 128.0 * me, O.is_ge)
-    ts(X("fOW", 1, 2), L1g, 128.0 * me + 128, O.is_lt)
-    tt(X("fOW", 2, 3), X("fOW", 0, 1), X("fOW", 1, 2), O.mult)
-    ts(X("fIDW"), X("fR96", 0, 32), P32, O.is_equal, X("fOW", 2, 3), O.mult)
+    D1g, L2g, H2g, A2 = (X("fG4", i, i + 1) for i in range(4))
+    ts(X("fDQ", 1, 2), DQ, 1024.0, O.is_ge, -1024.0, O.mult)
+    ts(D1g, DQ, X("fDQ", 1, 2), O.add)
+    dma("y", T.sw[0:1, :], ap(blk(D1g, 0)), [blk(D1g, 0)], [])
+    dma("y", T.lw[0:1, :], ap(blk(L1g, 0)), [blk(L1g, 0)], [])
+    ts(X("fOW", 0, 1), L1g, float(P * me), O.max, float(P * me + P - 1), O.min)
+    ts(X("fOW", 1, 2), X("fOW", 0, 1), L1g, O.is_equal)
+    times(X("fIDW"), X("fID"), X("fOW", 1, 2))
+    n = 2 if me in x2 else 1
+    times(X("fMW", 0, 32), CT(96, 128), L1g)
     if me in x2:
-        owners([(X("fMM", 0, 32), (L1g, o2g, c2g)[x2.index(me) // 2])], 16, P16, 2)
-    owners([(CT(96, 128), L1g)], 4, P4, 1)
-
-    def new(nt, q0):
-        for b in range(4):
-            cp(X(nt, b, 512, 0, 128, 4), X("p%d" % (2 + b), 0, 128))
-        quant("QT", q0, q0 + 128, nt, 0, 512)
+        times(X("fMW", 32, 64), X("fMM"), (L1g, o2g, c2g)[x2.index(me) // 2])
+    tr(X("fMX", 0, 32 * n), X("fMW", 0, 32 * n))
+    ts(X("fOM", 0, n), sums(X("fMS", 0, 32 * n), X("fMX", 0, 32 * n), 32), (P - 1) / 2, O.subtract, 1.0 / P, O.mult)
+    cp(X("MI", 0, n), X("fOM", 0, n))
+    ts(X("Mo", 0, 1), X("MI", 0, 1), 4.0, O.mult, P4, O.add)
+    if me in x2:
+        ts(X("Mo", 2, 3), X("MI", 1, 2), 16.0, O.mult, P16, O.add)
 
     for b in range(4):
-        mm("p%d" % (2 + b), 128, "EQ", 128 * b, "UD", 0, False, True)
-    new("NT0", 288)
-    mm("p6", 128, "UQ", 0, "QT", 288)
+        mm("p%d" % (2 + b), 128, "EQ", 128 * b, "MV", 32, False, True)
+    for b in range(4):
+        cp(X("NT", b, 128, 0, 128, 4), X("p%d" % (2 + b), 0, 32))
+    quant("QT", 320, 448, "NT", 0, 512)
+    mm("p6", 128, "UQ", 0, "QT", 320)
     tt(X("fSC"), X("p6", 0, 32), X("fIDW"), O.mult)
     red(X("fNK", 4 * me, 4 * me + 1), X("fSC"), O.add, True, True)
-    send1(3, "QT", 288, lambda: send_scores(2, "fNK", 4 * me, 1))
+    send1(3, "QT", 320, lambda: send_scores(2, X("fNK", 4 * me, 4 * me + 1), "fNK"))
     if me in x2:
-        pick("MG2", 16, "LD2", 0, 128, ("Mo", 4))
+        pick("MG2", 0, 16, "LD2", 0, 128, ("Mo", 2))
     send2(2)
 
-    tiles = {"": ("fEP", "fEQr", "fMK", "fMG", "fMT", "fMH", "fML")}
-    tiles["b"] = tuple(n + "b" for n in tiles[""])
+    step = 2.0 ** -24
 
     def prep(w, ak, ag, bg):
-        e, r, k, gl = tiles[w][:4]
-        for i, c in enumerate((ak, ag, bg)):
-            times(X(e, 32 * i, 32 * i + 32), X("fON"), c)
-        tr(X(k, 32, 64), X(e, 0, 32))
-        tr(X(r, 0, 64), X(e, 32, 96))
-        o = O.is_lt if w else O.is_ge
-        ts(X(gl, 0, 32), X(r, 32, 64), ag, o, -step, O.mult)
-        ts(X(gl, 32, 96), X(r, 0, 64), bg, o, -step, O.mult)
-        ts(X(gl, 0, 96), X(gl, 0, 96), 1.0, O.add)
+        times(X("fME" + w, 0, 32), X("fON"), bg)
+        tr(X("fMR" + w), X("fME" + w, 0, 32))
+        for i, c in enumerate((ag, bg)):
+            ts(X("fMG" + w, 32 * i, 32 * i + 32), X("fMR" + w), c, O.is_gt if w else O.is_le, -step, O.mult)
+        ts(X("fME" + w, 32, 64), X("fMG" + w, 0, 32), 1.0, O.add, ak, O.mult)
+        tr(X("fMK" + w), X("fME" + w, 32, 64))
 
-    def ranks(w, ak, bk, raw, cut):
-        e, r, k, gl, t, h, ml = tiles[w]
-        if cut is None:
-            ts(X(e, 96, 128), X("fON"), raw, O.mult)
-        else:
-            ts(X(e, 96, 128), X("fON"), raw, O.mult, cut, O.min)
-        tr(X(k, 64, 96), X(e, 96, 128))
-        tt(X(t, 0, 32), X(k, 64, 96), X(gl, 0, 32), O.mult)
-        tt(X(t, 32, 96), X(k, 32, 96), X(gl, 32, 96), O.mult)
-        o = O.is_gt if w else O.is_ge
-        ts(X(t, 96, 128), X(t, 0, 32), ak, o)
-        ts(X(t, 128, 192), X(t, 32, 96), bk, o)
-        total(X(ml, 0, 1), X(t, 96, 128))
-        total(X(ml, 1, 2), X(t, 128, 192))
+    def ranks(w, bk):
+        t, u, o = "fMT" + w, "fMU" + w, O.is_gt if w else O.is_ge
+        ts(X(t, 0, 32), X("fMG" + w, 32, 64), 1.0, O.add, bk, O.mult)
+        ts(X(t, 32, 64), X("fMK" + w), bk, o)
+        tr(X(u), X(t, 0, 64))
+        ts(X(t, 64, 96), X(u, 0, 32), bk, o)
+        total(X("fML" + w, 0, 1), X(u, 32, 64))
+        total(X("fML" + w, 1, 2), X(t, 32, 96))
 
-    def hot(w, at, wide, va, vb, outs):
-        e, r, k, gl, t, h, ml = tiles[w]
-        n = 64 if wide else 32
-        for i in range(n // 32):
+    def hot(w, at, wide, va, vb, out=None):
+        h, ht = "fMH" + w, "fMI" + w
+        n = 128 if wide else 64
+        for i in range(n // 64):
             ra = X("fRP", 32 * i, 32 * i + 32) if wide else X("fRP", 64, 96)
-            rb = X("fROW", 32 * i, 32 * i + 32) if wide else X("fR96", 0, 32)
+            rb = X("fROW", 32 * i, 32 * i + 32) if wide else X("fR32")
             o = at + 64 * i
-            ts(X(h, o, o + 32), ra, X(ml, 0, 1), O.is_equal, va, O.mult)
-            ts(X(h, o + 32, o + 64), rb, X(ml, 1, 2), O.is_equal, vb, O.mult)
-        tr(X(h, at + 2 * n, at + 4 * n), X(h, at, at + 2 * n))
-        for i, o in enumerate(outs):
-            total(o, X(h, at + 2 * n + 64 * i, at + 2 * n + 64 * i + 64))
+            ts(X(h, o, o + 32), ra, X("fML" + w, 0, 1), O.is_equal, va, O.mult)
+            ts(X(h, o + 32, o + 64), rb, X("fML" + w, 1, 2), O.is_equal, vb, O.mult)
+        tr(X(ht, at, at + n), X(h, at, at + n))
+        if wide:
+            return sums(X("fMJ" + w), X(ht, at, at + n), 64)
+        total(out, X(ht, at, at + n))
 
-    def pc(i, v):
-        ts(X("fFM", i, i + 1), P32, float(v), O.add)
-        return X("fFM", i, i + 1)
-
-    def final(i, gcol, acol, out):
-        ts(X("fFH", 192 * i, 192 * i + 192), X("fPT"), gcol, O.is_equal, acol, O.mult)
-        tr(X("fFT%d" % i), X("fFH", 192 * i, 192 * i + 192))
-        for c in range(6):
-            total(X("fFR", 6 * i + c, 6 * i + c + 1), X("fFT%d" % i, 32 * c, 32 * c + 32))
-        tt(out, X("fFR", 6 * i, 6 * i + 6), out, O.max)
+    def final(i, gcol, acol, out, old):
+        ts(X("fFH%d" % i), X("fPT"), gcol, O.is_equal, acol, O.mult)
+        tr(X("fFT%d" % i), X("fFH%d" % i))
+        tt(out, sums(X("fFS%d" % i), X("fFT%d" % i), 32), old, O.max)
 
     prep("", c2k, c2g, D1g)
-    ranks("", c2k, z1, z1, None)
-    hot("", 0, True, pc(0, 64), P32, [X("fML", 4, 5), X("fML", 5, 6)])
-    cp(X("B2o"), X("fML", 4, 6))
+    ranks("", z1)
+    cp(X("B2o"), hot("", 0, True, a64, P32))
     prep("b", o2k, o2g, L1g)
-    hot("", 256, False, c2g, D1g, [H2g])
-    cp(X("fFL"), X("fJB"))
-    cp(X("fFD"), X("fJB"))
-    final(0, L1g, pc(1, 288), X("fFL"))
-    final(1, D1g, pc(2, 96), X("fFD"))
-    a416, a128, a192 = pc(3, 416), pc(4, 128), pc(5, 192)
+    hot("", 128, False, c2g, D1g, H2g)
+    dma("y", T.sw[1:2, :], ap(blk(H2g, 0)), [blk(H2g, 0)], [])
+    final(0, L1g, a320, X("fFL"), X("fJB"))
+    final(1, D1g, a96, X("fFD"), X("fJB"))
+    pick("MV", 0, 32, "DW", 96, 192, ("B2o", 0))
+    for b in range(4):
+        mm("p%d" % (2 + b), 128, "EQ", 128 * b, "MV", 0)
+        cp(X("fDB", 32 * b, 32 * b + 32), X("p%d" % (2 + b), 0, 32))
 
-    red(X("fNB"), ("fNK", 0, 32, 0, 128, 4))
-    ts(X("fNS", 1, 2), X("fNB"), -low, O.min)
-    ranks("b", o2k, X("fNS", 1, 2), X("fNB"), -low)
-    hot("b", 0, True, o2g, L1g, [X("fMLb", 4, 5), X("fMLb", 5, 6)])
-    ts(X("N2o"), X("fMLb", 4, 6), 128.0 * me, O.subtract, 95.0, O.min)
-    pick("BP2", 32, "DW", 96, 192, ("B2o", 0))
+    red(X("fNB"), ("fNK", 0, 36, 0, 128, 4), O.min)
+    ranks("b", X("fNB"))
+    ts(X("N2o"), hot("b", 0, True, o2g, L1g), float(P * me), O.subtract, P - 1.0, O.min)
     for b in range(4):
-        mm("p%d" % (2 + b), 128, "EQ", 128 * b, "BP2", 0, True, False)
-    pick("NP2", 32, "QT", 192, 288, ("N2o", 0))
-    for b in range(4):
-        mm("p%d" % (2 + b), 128, "EQ", 128 * b, "NP2", 0, False, True)
-    pick("MG3", 16, "LD3", 0, 32, ("Mo", 2))
+        o, w, d = X("NT", b, 128, 0, 128, 4), X("fDN", 96 * b, 96 * b + 96), X("fDB", 32 * b, 32 * b + 32)
+        op("v", lambda o=o, w=w, d=d: g.vector.tensor_tensor(ap(o), ap(w).indirect(T.N2o[:]), ap(d), O.add), [w, d, X("N2o")], [o], el(110))
+    quant("QT", 448, 576, "NT", 0, 512)
+    pick("MG3", 0, 16, "LD3", 0, 32, ("Mo", 0))
     send2(3)
-    hot("b", 256, False, o2g, L1g, [L2g])
-    final(2, L2g, a416, X("fFL"))
+    hot("b", 128, False, o2g, L1g, L2g)
+    final(2, L2g, a448, X("fFL"), X("fFL"))
     cp(X("FLo", 0, 6), X("fFL"))
-    new("NT1", 416)
-    pick("LF", 128, "QT", 0, 544, ("FLo", 0))
+    pick("LF", 0, 128, "QT", 0, 576, ("FLo", 0))
     mm("p7", 128, "WQ", 0, "LF", 0)
     dma("y", T.oc[:, 0:384], _codes(T, "LF", 0, 96), [X("LF", 0, 96)], [])
     for k in range(4):
         dma("y", T.osc[4 * k:4 * k + 4, 0:96], T.LFs[32 * k:32 * k + 4, 0:96], [X("LFs", 0, 96)], [])
     cp(X("fY"), X("p7", 0, 96))
     dma("a", T.y[:], T.fY[:], [X("fY")], [])
+    dma("a", T.lw[1:2, :], ap(blk(L2g, 0)), [blk(L2g, 0)], [])
 
-    hot("b", 384, False, a128, a192, [X("fMLb", 6, 7)])
-    final(3, H2g, X("fMLb", 6, 7), X("fFD"))
+    hot("b", 192, False, a128, a192, A2)
+    final(3, H2g, A2, X("fFD"), X("fFD"))
     cp(X("FDo"), X("fFD"))
-    pick("DF", 96, "DW", 0, 224, ("FDo", 0))
+    pick("DF", 0, 96, "DW", 0, 224, ("FDo", 0))
     dma("y", T.oc[:, 384:768], _codes(T, "DF", 0, 96), [X("DF", 0, 96)], [])
     for k in range(4):
         dma("a" if k % 2 else "y", T.osc[4 * k:4 * k + 4, 96:192], T.DFs[32 * k:32 * k + 4, 0:96], [X("DFs", 0, 96)], [])
-    cp(L1q, L1g)
-    cp(X("GI"), X("fG4", 0, 4))
-    op("v", lambda: g.vector.tensor_scalar(T.GJ[:], T.GI[:], 7, None, O.arith_shift_right), [X("GI")], [X("GJ")], el(1))
-    ts(X("GK"), X("GJ"), -32, O.mult)
-    ms(X("fG4t", 0, 32), 0.0)
-    tt(X("fG4t", 0, 4), X("GI"), X("GK"), O.add)
-    tr(X("fG4t", 32, 64), X("fG4t", 0, 32))
-    dma("a", T.lw[:], T.fG4t[0:2, 32:64], [X("fG4t", 32, 64)], [])
-    dma("a", T.sw[:], T.fG4t[2:4, 32:64], [X("fG4t", 32, 64)], [])
     schedule()
     cnt["ls"] = ls[0]
     for s in sorted(cnt):

@@ -7,29 +7,27 @@ AF = ActivationFunctionType
 P = 96
 F32, BF, I32, U16 = "float32", "bfloat16", "int32", "uint16"
 SCRATCH = {}
-for _n, _w in {"BT": 1280, "WT": 512, "UZ": 8, "UT": 512, "ZT": 512, "ONB": 128, "HAF": 128, "DG": 128, "ET": 1056, "NT": 512, "HT": 512,
+for _n, _w in {"BT": 1280, "WT": 512, "UZ": 8, "UT": 512, "ZT": 512, "ONB": 128, "HAF": 128, "DG": 128, "ET": 1056, "NT": 512, "HT": 512, "HU": 512,
                "MT": 528, "SG": 384, "MK": 128, "R32": 192, "R64": 128}.items():
     SCRATCH[_n] = ("sbuf", [128, _w], BF)
-for _n, _w in {"PJ": 6, "MI": 2}.items():
+for _n, _w in {"PJ": 6, "MI": 4}.items():
     SCRATCH[_n] = ("sbuf", [128, _w], I32)
 for _n, _w in {"LO": 4, "Mo": 4, "O1o": 2, "UOo": 2, "X2o": 6, "B2o": 2, "N2o": 2, "FLo": 8, "FDo": 6}.items():
     SCRATCH[_n] = ("sbuf", [128, _w], U16)
-for _n, _w in {"QT": 576, "UQ": 128, "ZQ": 128, "EQ": 512, "WQ": 128, "HQ": 128, "HQ2": 128, "MQ": 132, "SL1": 32, "LD1": 128, "MG1": 32, "UO": 36,
-               "SL2": 96, "LD2": 128, "MG2": 16, "LD3": 32, "MG3": 16, "DW": 224, "MV": 192, "LF": 128, "DF": 96,
-               "RC1": 16, "RC2": 48, "RC3": 16, "RW1": 18, "RW2": 16, "RW3": 4}.items():
+for _n, _w in {"QT": 576, "UQ": 128, "ZQ": 128, "EQ": 512, "WQ": 128, "HQ": 128, "HQ2": 128, "HQ3": 128, "MQ": 132, "SL1": 32, "LD1": 128, "MG1": 32,
+               "UO": 36, "SL2": 96, "LD2": 160, "MG2": 32, "LD3": 96, "MG3": 16, "DW": 224, "MV": 192, "LF": 128, "DF": 96,
+               "RC1": 16, "RC2": 48, "RC3": 16, "RW1": 18, "RW2": 20, "RW3": 12}.items():
     SCRATCH[_n] = ("sbuf", [128, _w], "float8_e4m3fn_x4")
     SCRATCH[_n + "s"] = ("sbuf", [128, _w], "uint8")
 for _n, _w in {"RS1": 1, "RS2": 1, "RS3": 1, "RS4": 1, "SD": 32, "NL": 32, "NM": 32, "NK": 36, "Y": 96, "KT": 32}.items():
     SCRATCH["f" + _n] = ("sbuf", [128, _w], F32)
 _V = {"UZ": 8, "PC": 16, "AD": 128, "AL": 96, "CD": 4, "CC": 192, "RK": 4, "TG": 128, "TG2": 128, "TG3": 128, "OA": 128, "OC": 128, "DN": 384, "DB": 128}
 _F = {"ON": 32, "ROW": 192, "R32": 32, "PT": 192, "JB": 6, "KR": 128, "PR": 128, "ZA": 128, "ZR": 128, "RO": 32, "GZ": 64, "GT": 64, "GV": 4,
-      "CT": 128, "CTX": 128, "CT1": 32, "TH": 128, "RP": 96, "ID": 32, "SWA": 8, "CW": 256, "CV": 256, "CX": 256, "CY": 256, "NF": 4, "CF": 1,
-      "HN": 96, "HM": 96, "H2": 128, "H2t": 128, "H2s": 128, "XT": 4, "XU": 4, "G2": 2, "DQ": 2, "GA": 8, "UX": 128, "UT": 128, "US": 128,
-      "OW": 2, "IDW": 32, "MM": 32, "MW": 64, "MX": 64, "MS": 64, "OM": 2, "SC": 32, "NB": 1, "FM": 8, "G4": 4, "FL": 6, "FD": 6}
-for _i in range(4):
-    for _n in ("FH", "FT", "FS"):
-        _F[_n + str(_i)] = 192
-for _n, _w in (("ME", 64), ("MR", 32), ("MG", 64), ("MK", 32), ("MT", 96), ("MU", 64), ("ML", 4), ("MH", 256), ("MI", 256), ("MJ", 128)):
+      "CT": 64, "CTX": 128, "CT1": 32, "TH": 128, "RP": 96, "ID": 32, "SWA": 8, "CW": 256, "CV": 256, "CX": 256, "CY": 256, "NF": 4, "CF": 1,
+      "HN": 96, "HM": 96, "H2": 128, "H2t": 128, "H2s": 128, "XT": 4, "XU": 4, "G2": 2, "DQ": 4, "GA": 8, "UX": 128, "UT": 128, "US": 128,
+      "OW": 2, "IDW": 32, "MM": 160, "MW": 160, "MX": 160, "OM": 8, "SC": 32, "NB": 1, "FM": 8, "G4": 4, "G5": 4, "FL": 6,
+      "FH0": 192, "FH1": 192, "FH2": 192, "FT0": 192, "FT1": 192, "FS0": 192, "FS1": 192}
+for _n, _w in (("ME", 64), ("MR", 32), ("MG", 64), ("MK", 32), ("MT", 96), ("MU", 64), ("ML", 4), ("MH", 192), ("MI", 192), ("MJ", 128)):
     _F[_n] = _F[_n + "b"] = _w
 _AT = {}
 for _b, _d in (("fV", _V), ("fW", _F)):
@@ -44,12 +42,18 @@ SEMAPHORES = ["vs", "ac", "te", "gp", "ls"] + [_s + str(_k) for _k in (1, 2, 3, 
 for _x in (1, 2, 3):
     SEMAPHORES += ["a%d" % _x, "b%d" % _x, "qc%d" % _x, "qs%d" % _x, "wc%d" % _x, "ws%d" % _x]
 SEMAPHORES += ["d%d" % _i for _i in range(60)]
-WAKE, PIPE, CYCLE, SLACK, QUIET, GAP = 0.1, 0.06, 0.00083, 0.03, 1.8, 0.05
-LATE = {"n1": 2.0, "s1": 4.0, "a1": 4.2, "b1": 3.03, "n3": 1.9, "s3": 2.0, "n4": 1.9, "s4": 3.1, "n2": 2.14, "s2": 3.5, "a2": 3.2, "b2": 4.1,
-        "a3": 3.5, "b3": 3.45, "small": 1.5, "big": 1.8, "dma": 2.0, "c0": 1.5, "c1": 0.4, "c2": 0.5, "c": 0.3}
-NX = {1: 16, 2: 16, 3: 4}
-NY = {1: 18, 2: 16, 3: 4}
+WAKE, PIPE, CYCLE, SLACK, QUIET, GAP, BIAS = 0.1, 0.06, 0.00083, 0.03, 1.8, 0.05, 0.08
+LATE = {"n1": 2.0, "s1": 4.0, "a1": 4.2, "b1": 3.03, "n3": 1.9, "s3": 2.0, "n4": 1.9, "s4": 3.1, "n2": 2.14, "s2": 3.5, "a2": 3.2, "b2": 3.1,
+        "a3": 3.5, "b3": 3.45, "small": 1.5, "big": 1.8, "dma": 2.0, "c0": 1.5, "c1": 0.3, "c2": 0.3, "c3": 0.7, "c": 0.6}
+WHEN = {"sn1": [9.8, 10.1, 10.4, 10.4], "sa1": [12.0, 12.3, 12.2, 12.5], "a1": [11.7, 0.0, 0.0, 0.0], "b1": [18.8, 19.1, 19.4, 19.6],
+        "sn3": [15.6, 15.9, 16.1, 15.8], "sa3": [16.9, 17.2, 17.1, 17.4], "sn4": [16.7, 18.8, 19.1, 19.4], "sa4": [19.1, 19.4, 19.4, 19.6],
+        "a2": [0.0, 21.8, 21.1, 21.4], "sn2": [24.0, 24.3, 24.5, 24.4], "sa2": [24.9, 25.1, 25.1, 25.4], "b2": [26.4, 26.6, 26.9, 27.0],
+        "a3": [24.9, 24.4, 0.0, 0.0], "b3": [29.2, 29.4, 29.7, 29.9]}
+SHARE = {1: (16, 0, 0, 0), 2: (0, 8, 20, 20), 3: (4, 12, 0, 0)}
+HALF = {_x: sum(_v) for _x, _v in SHARE.items()}
 LAND = {1: ("UO", 0), 2: ("DW", 96), 3: ("DW", 192)}
+PAIR = {1: (1, 2), 2: (0, 3), 3: (1, 2)}
+OTHER = {2: (1, 2), 3: (0, 3)}
 
 
 def _layout(T, topo):
@@ -59,8 +63,15 @@ def _layout(T, topo):
     return a, b
 
 
-def _owners(x, order):
-    return {1: [order[0], order[4]], 2: order[1:4] + order[5:8], 3: order}[x]
+def _owners(x, order, step=1):
+    out, at = [], 0
+    for pl in (order[:4], order[4:]):
+        for r, n in zip(pl, SHARE[x]):
+            if n:
+                n += 2 * (x == 1 and step == 2)
+                out.append((r, at, n))
+                at += n
+    return out
 
 
 def _helpers(home, far, topo):
@@ -68,9 +79,9 @@ def _helpers(home, far, topo):
     return sorted(h, key=lambda c: (topo.die(c) != topo.die(home), c))
 
 
-def _remote(g, T, topo, core, moves, sem):
+def _remote(g, T, topo, core, moves):
     tr = []
-    for src, dsts, eng, *own in moves:
+    for src, dsts, eng, sem in moves:
         ids = []
         for c, _ in dsts:
             rid, pid = topo.addr(c, core)
@@ -78,69 +89,54 @@ def _remote(g, T, topo, core, moves, sem):
         m = 0
         for e in eng:
             m |= 1 << e
-        tr.append(RemoteDMATransfer(dst_ids=ids, dma_engine_mask=m, remote_sem=T.sem[own[0] if own else sem], srcs=[src], dsts=[d for _, d in dsts]))
+        tr.append(RemoteDMATransfer(dst_ids=ids, dma_engine_mask=m, remote_sem=T.sem[sem], srcs=[src], dsts=[d for _, d in dsts]))
     g.remote_dma_fused(tr, local_sem=T.sem.ls)
     return sum(len(mv[2]) for mv in moves)
 
 
-def _codes(T, name, a, b):
-    return T[name][:, a:b].bitcast(dt.uint8)
+def _view(T, name, a, b, codes=True):
+    return T[name][:, a:b].bitcast(dt.uint8) if codes else T[name + "s"][:, a:b]
 
 
 def _hand_on(g, core, T, topo, rank, far):
     home = T.cores[rank]
+    a, b = _layout(T, topo)
     hs = _helpers(home, T.cores[far[0]], topo)
     if core not in hs:
         return
-    me, ls = hs.index(core), 0
+    me = hs.index(core)
+    near = [r for r in (a if rank in a else b) if r != rank]
     eng = topo.engines(core, T.cores[far[0]])
     n_on = len(topo.engines(home, core)) - len(eng)
-    a, b = _layout(T, topo)
+    codes = me < 2
 
     def scores(k):
         g.wait_ge(T.sem["sr%d" % k], n_on)
         dst = ("fSD", "fNK", "fNL", "fNM")[k - 1]
         to = far[:len(far) // 2] if me < 2 else far[len(far) // 2:]
-        return _remote(g, T, topo, core, [(T["fRS%d" % k][:], [(T.cores[r], T[dst][:, 4 * rank:4 * rank + 1]) for r in to], eng)], "sa%d" % k)
+        return _remote(g, T, topo, core, [(T["fRS%d" % k][:], [(T.cores[r], T[dst][:, 4 * rank:4 * rank + 1]) for r in to], eng, "sa%d" % k)])
 
-    def first(x, codes):
-        n = NX[x]
+    def first(x, to):
         g.wait_ge(T.sem[("qc%d" if codes else "qs%d") % x], n_on)
-        mv = []
-        to = [r for r in _owners(x, a + b) if r in far]
-        for i, r in enumerate(to):
-            e = eng if x == 1 else eng[2 * i:2 * i + 2]
-            if codes:
-                mv.append((_codes(T, "RC%d" % x, n * i, n * i + n), [(T.cores[r], _codes(T, "LD%d" % x, n * rank, n * rank + n))], e))
-            else:
-                mv.append((T["RC%ds" % x][:, n * i:n * i + n], [(T.cores[r], T["LD%ds" % x][:, n * rank:n * rank + n])], e))
-        return _remote(g, T, topo, core, mv, "a%d" % x)
+        n = 0
+        for r, s0, w in sorted(_owners(x, a + b), key=lambda o: -o[2]):
+            if r in to:
+                s0 %= HALF[x]
+                n += _remote(g, T, topo, core, [(_view(T, "RC%d" % x, s0, s0 + w, codes), [(T.cores[r], _view(T, "LD%d" % x, w * rank, w * rank + w, codes))], eng, "a%d" % x)])
+        return n
 
-    def second(x, codes):
-        own = _owners(x, a + b)
-        if rank not in own:
-            return 0
-        n = NY[x]
+    def second(x):
         nm, base = LAND[x]
-        base += n * own.index(rank)
-        g.wait_ge(T.sem[("wc%d" if codes else "ws%d") % x], n_on)
-        if codes:
-            mv = [(_codes(T, "RW%d" % x, 0, n), [(T.cores[r], _codes(T, nm, base, base + n)) for r in far], eng)]
-        else:
-            mv = [(T["RW%ds" % x][:], [(T.cores[r], T[nm + "s"][:, base:base + n]) for r in far], eng)]
-        return _remote(g, T, topo, core, mv, "b%d" % x)
+        for r, s0, n in _owners(x, a + b, 2):
+            if r == rank:
+                g.wait_ge(T.sem[("wc%d" if codes else "ws%d") % x], n_on)
+                return _remote(g, T, topo, core, [(_view(T, "RW%d" % x, 0, n, codes), [(T.cores[r], _view(T, nm, base + s0, base + s0 + n, codes)) for r in far], eng, "b%d" % x)])
+        return 0
 
-    if me in (1, 2):
-        for x in (1, 3):
-            ls += first(x, me == 1)
-            ls += second(x, me == 1)
-    elif me in (0, 3):
-        ls += scores(1)
-        ls += scores(3)
-        ls += scores(4)
-        ls += first(2, me == 0)
-        ls += scores(2)
-        ls += second(2, me == 0)
+    if me in PAIR[1]:
+        ls = first(1, far) + second(1) + first(2, near) + first(3, far) + second(3)
+    else:
+        ls = scores(1) + scores(3) + scores(4) + first(2, far) + first(3, near) + scores(2) + second(2)
     g.wait_ge(T.sem.ls, ls)
 
 
@@ -182,6 +178,12 @@ def rank_program(g, core, T, topo):
     def blk(v, a):
         return rows(v, 32 * a, 32 * a + 32)
 
+    def top(v):
+        return rows(v, 0, 64)
+
+    def bot(v):
+        return rows(v, 64, 128)
+
     def width(v):
         return -(-(v[2] - v[1]) // v[5])
 
@@ -222,7 +224,7 @@ def rank_program(g, core, T, topo):
         know[ev] = dict(waited[q])
         enter(acc, reads, writes, ev, q)
 
-    nodes, seen, fill = [], {}, set()
+    nodes, seen, fill, floor = [], {}, set(), {}
 
     def note(ways, reads, writes, after=(), late=0.0):
         k = len(nodes)
@@ -261,12 +263,14 @@ def rank_program(g, core, T, topo):
                     if t + d + (GAP if k in fill else -SLACK) <= b0:
                         break
                     t = max(t, b1)
-                if best is None or t + c < best[0] + nodes[k][0][best[1]][1]:
+                if best is None or t + c < best[0] + nodes[k][0][best[1]][1] + BIAS:
                     best = (t, q, d)
             t, q, d = best
             if q in busy:
                 busy[q].append((t, t + d))
             start[k], done[k] = (t, -path[k], k, q), t + nodes[k][0][q][1] + nodes[k][2]
+            if floor.get(k):
+                done[k] = max(t, floor[k])
         for t, _, k, q in sorted(start):
             nodes[k][0][q][0]()
 
@@ -287,8 +291,8 @@ def rank_program(g, core, T, topo):
     def op(q, call, reads, writes, cost):
         note({q: (lambda: issue_op(q, call, reads, writes), cost)}, reads, writes)
 
-    def either(v, a, reads, writes, c):
-        note({"v": (lambda: issue_op("v", v, reads, writes), c), "a": (lambda: issue_op("a", a, reads, writes), c + 0.02)}, reads, writes)
+    def either(v, a, reads, writes, c, more=0.02):
+        note({"v": (lambda: issue_op("v", v, reads, writes), c), "a": (lambda: issue_op("a", a, reads, writes), c + more)}, reads, writes)
 
     def dma(q, out, in_, reads=(), writes=(), late="dma"):
         def issue():
@@ -300,10 +304,10 @@ def rank_program(g, core, T, topo):
             post(q, reads, writes, (s, 16))
         note({q: (issue, 0.06)}, reads, writes, (), LATE[late])
 
-    def send(moves, sem, reads):
+    def send(moves, reads):
         def issue():
             pre("g", reads, [])
-            ls[0] += _remote(g, T, topo, core, moves, sem)
+            ls[0] += _remote(g, T, topo, core, moves)
         sent.append(note({"g": (issue, LATE.get("c%d" % len(sent), LATE["c"]))}, reads, [], sent[-1:]))
 
     def arrive(views, sem, total, late):
@@ -311,10 +315,10 @@ def rank_program(g, core, T, topo):
             cnt[sem] = total
             for v in views:
                 acc.setdefault(v[0], []).append((v, True, (sem, total), "r"))
-        note({"r": (issue, 0.0)}, [], views, sent[-1:], late)
+        floor[note({"r": (issue, 0.0)}, [], views, sent[-1:], late)] = WHEN.get(sem, [0.0] * 4)[m % 4]
 
     def dcol(q, dst, d0, src, s0, n):
-        dma(q, _codes(T, dst, d0, d0 + n), _codes(T, src, s0, s0 + n), [X(src, s0, s0 + n)], [X(dst, d0, d0 + n)])
+        dma(q, _view(T, dst, d0, d0 + n), _view(T, src, s0, s0 + n), [X(src, s0, s0 + n)], [X(dst, d0, d0 + n)])
         dma(q, T[dst + "s"][:, d0:d0 + n], T[src + "s"][:, s0:s0 + n], [X(src + "s", s0, s0 + n)], [X(dst + "s", d0, d0 + n)])
 
     def sc(s):
@@ -323,7 +327,12 @@ def rank_program(g, core, T, topo):
     def ts(out, a, s1, op0, s2=None, op1=None):
         p1, r1 = sc(s1)
         p2, r2 = sc(s2)
-        if op1 is None:
+        plain = SCRATCH[out[0]][2] == F32 and SCRATCH[a[0]][2] == F32
+        if plain and op1 is None and op0 == O.add:
+            either(lambda: g.vector.tensor_scalar(ap(out), ap(a), p1, None, op0), lambda: g.scalar.activation(ap(out), ap(a), AF.Identity, bias=p1), [a] + r1, [out], el(width(out)))
+        elif plain and op0 == O.mult and op1 == O.add:
+            either(lambda: g.vector.tensor_scalar(ap(out), ap(a), p1, p2, op0, op1), lambda: g.scalar.activation(ap(out), ap(a), AF.Identity, bias=p2, scale=p1), [a] + r1 + r2, [out], el(width(out)))
+        elif op1 is None:
             op("v", lambda: g.vector.tensor_scalar(ap(out), ap(a), p1, None, op0), [a] + r1, [out], el(width(out)))
         else:
             op("v", lambda: g.vector.tensor_scalar(ap(out), ap(a), p1, p2, op0, op1), [a] + r1 + r2, [out], el(width(out)))
@@ -359,6 +368,10 @@ def rank_program(g, core, T, topo):
     def ms(out, c):
         op("v", lambda: g.vector.memset(ap(out), c), [], [out], el(width(out), 0.5 if SCRATCH[out[0]][2] == BF else 1.0))
 
+    def zero(out):
+        src, n = X("MT", 32, 32 + width(out)), width(out)
+        either(lambda: g.vector.memset(ap(out), 0.0), lambda: g.scalar.activation(ap(out), ap(src), AF.Copy), [src], [out], el(n, 0.5), el(n) - el(n, 0.5) + 0.02)
+
     def act(out, a, func, bias=None, scale=1.0):
         if bias is None:
             op("a", lambda: g.scalar.activation(ap(out), ap(a), func), [a], [out], el(width(out)) + 0.02)
@@ -386,54 +399,47 @@ def rank_program(g, core, T, topo):
                [win, ov], [out], el(40 + 1.5 * width(out)))
 
     def send1(x, src, s0, between=lambda: None):
-        n, own, ps = NX[x], _owners(x, order), src + "s"
-        fo = [r for r in own if r in far]
-        p, w = s0 + n * own.index(fo[0]), n * len(fo)
-        fc = (_codes(T, src, p, p + w), [(hs[0 if x == 2 else 1], _codes(T, "RC%d" % x, 0, w))], e_on, "qc%d" % x)
-        fp = (T[ps][:, p:p + w], [(hs[3 if x == 2 else 2], T["RC%ds" % x][:])], e_on, "qs%d" % x)
-        mc, mp, rd, rp = [], [], [], []
-        for i, r in enumerate([r for r in near if r in own]):
-            c = s0 + n * own.index(r)
-            e = e_off if x == 1 else e_off[2 * i:2 * i + 2]
-            mc.append((_codes(T, src, c, c + n), [(T.cores[r], _codes(T, "LD%d" % x, n * me, n * me + n))], e))
-            mp.append((T[ps][:, c:c + n], [(T.cores[r], T["LD%ds" % x][:, n * me:n * me + n])], e))
-            rd.append(X(src, c, c + n))
-            rp.append(X(ps, c, c + n))
-        if x == 1:
-            send([fc] + mc, "a1", [X(src, p, p + w)] + rd)
-            send([fp] + mp, "a1", [X(ps, p, p + w)] + rp)
-        else:
-            send([fc], None, [X(src, p, p + w)])
-            send([fp], None, [X(ps, p, p + w)])
-            between()
-            send(mc, "a%d" % x, rd)
-            send(mp, "a%d" % x, rp)
-        if me in own:
-            dcol("y", "LD%d" % x, n * me, src, s0 + n * own.index(me), n)
-            oth = [X(k, n * r, n * r + n) for k in ("LD%d" % x, "LD%ds" % x) for r in range(8) if r != me]
-            arrive(oth, "a%d" % x, 7 * 2 * (len(e_off) if x == 1 else 2), LATE["a%d" % x])
+        own, w = _owners(x, order), HALF[x]
+        p, p2 = (s0 + w, s0) if me in pa else (s0, s0 + w)
+        for h, k in enumerate(("qc%d" % x, "qs%d" % x)):
+            mv = [(_view(T, src, p, p + w, not h), [(hs[PAIR[x][h]], _view(T, "RC%d" % x, 0, w, not h))], e_on, k)]
+            if x in OTHER:
+                mv.append((_view(T, src, p2, p2 + w, not h), [(hs[OTHER[x][h]], _view(T, "RC%d" % x, 0, w, not h))], e_off, k))
+            send(mv, [X(src + "s" * h, s0, s0 + 2 * w)])
+        between()
+        for r, c, n in own:
+            if r in near and x not in OTHER:
+                for h in range(2):
+                    send([(_view(T, src, s0 + c, s0 + c + n, not h), [(T.cores[r], _view(T, "LD%d" % x, n * me, n * me + n, not h))], e_off, "a%d" % x)], [X(src + "s" * h, s0 + c, s0 + c + n)])
+            if r == me:
+                dcol("y", "LD%d" % x, n * me, src, s0 + c, n)
+                oth = [X(k, n * r, n * r + n) for k in ("LD%d" % x, "LD%ds" % x) for r in range(8) if r != me]
+                arrive(oth, "a%d" % x, 7 * 2 * len(e_off), LATE["a%d" % x])
 
     def send2(x):
-        n, own = NY[x], _owners(x, order)
+        own = _owners(x, order, 2)
         nm, base = LAND[x]
         src = "MG%d" % x
-        if me in own:
-            c = base + n * own.index(me)
-            for s, hc, h, k in ((src, "RW%d" % x, hs[0 if x == 2 else 1], "wc%d"), (src + "s", "RW%ds" % x, hs[3 if x == 2 else 2], "ws%d")):
-                code = s == src
-                sap = _codes(T, s, 0, n) if code else T[s][:, 0:n]
-                dap = _codes(T, nm, c, c + n) if code else T[nm + "s"][:, c:c + n]
-                hap = _codes(T, hc, 0, n) if code else T[hc][:]
-                send([(sap, [(h, hap)], e_on, k % x), (sap, [(T.cores[r], dap) for r in near], e_off, "b%d" % x)], None, [X(s, 0, n)])
-            dcol("y", nm, c, src, 0, n)
-        oth = [(base + n * i, r) for i, r in enumerate(own) if r != me]
-        arrive([X(k, c, c + n) for k in (nm, nm + "s") for c, r in oth], "b%d" % x, len(oth) * 2 * len(e_off), LATE["b%d" % x])
+        for r, c, n in own:
+            if r == me:
+                for h, k in enumerate(("wc%d" % x, "ws%d" % x)):
+                    sap = _view(T, src, 0, n, not h)
+                    send([(sap, [(hs[PAIR[x][h]], _view(T, "RW%d" % x, 0, n, not h))], e_on, k),
+                          (sap, [(T.cores[r], _view(T, nm, base + c, base + c + n, not h)) for r in near], e_off, "b%d" % x)], [X(src + "s" * h, 0, n)])
+                dcol("y", nm, base + c, src, 0, n)
+        oth = [(base + c, n) for r, c, n in own if r != me]
+        arrive([X(k, c, c + n) for k in (nm, nm + "s") for c, n in oth], "b%d" % x, len(oth) * 2 * len(e_off), LATE["b%d" % x])
 
     def send_scores(k, src, dst):
-        fm = (ap(src), [(h, T["fRS%d" % k][:]) for h in (hs[0], hs[3])], e_on, "sr%d" % k)
+        to = [(hs[h], T["fRS%d" % k][:]) for h in PAIR[2]]
+        fm = (ap(src), to, e_on, "sr%d" % k)
         nm = (ap(src), [(T.cores[r], T[dst][:, 4 * me:4 * me + 1]) for r in near], e_off, "sn%d" % k)
-        for mv in ([fm], [nm]) if k == 1 else ([fm, nm],):
-            send(mv, None, [src])
+        if k == 2:
+            calls = ([(ap(src), to[:1], e_on, "sr2"), (ap(src), to[1:], e_off, "sr2")], [nm])
+        else:
+            calls = ([fm], [nm]) if k == 1 else ([fm, nm],)
+        for mv in calls:
+            send(mv, [src])
         arrive([X(dst, 4 * r, 4 * r + 1) for r in near], "sn%d" % k, len(near) * len(e_off), LATE["n%d" % k])
         arrive([X(dst, 4 * r, 4 * r + 1) for r in far], "sa%d" % k, len(far) * len(e_off), LATE["s%d" % k])
 
@@ -446,21 +452,24 @@ def rank_program(g, core, T, topo):
     load("a", "BT", 0, 384, T.lv[:], "big")
     load("y", "BT", 768, 1152, T.nz[:], "big")
     load("a", "WT", 0, 512, T.w[:], "big")
-    e1, x2 = _owners(1, order), _owners(2, order)
-    cl = order.index(me) % 2
+    e1 = [o[0] for o in _owners(1, order)]
+    own2, own3 = ([o for o in _owners(x, order) if o[0] == me] for x in (2, 3))
+    cl = m % 2
     iota(X("PJ", 5, 6), [[1, 1]], 0, 1)
     iota(X("fTG", 0, 64), [[32, 2], [0, 2], [1, 16]], 0)
     iota(X("fTG2"), [[0, 8], [2, 16]], 0)
-    iota(X("fPR", 0, 128, 0, 64), [[1, 128]], P * me - 32)
-    iota(X("fPR", 0, 128, 64, 128), [[1, 128]], P * me)
+    iota(top(X("fPR")), [[1, 128]], P * me - 32)
+    iota(bot(X("fPR")), [[1, 128]], P * me)
     ms(X("ONB"), 1.0)
     ms(X("HAF"), 0.5)
     op("g", lambda: g.affine_select(T.MK[:], T.HAF[:], [[1, 128]], O.is_ge, -0.5, 0, -1), [X("HAF")], [X("MK")], 0.55)
     for i, k in enumerate((31, 15, 3, 1, 63)):
-        op("v", lambda k=k, i=i: g.vector.tensor_scalar(T.PJ[:, i:i + 1], T.PJ[:, 5:6], k, None, O.bitwise_and), [X("PJ", 5, 6)], [X("PJ", i, i + 1)], el(1))
-    cp(X("fPC", 0, 6), X("PJ"))
+        if i != 2:
+            op("v", lambda k=k, i=i: g.vector.tensor_scalar(T.PJ[:, i:i + 1], T.PJ[:, 5:6], k, None, O.bitwise_and), [X("PJ", 5, 6)], [X("PJ", i, i + 1)], el(1))
+    cp(X("fPC", 0, 2), X("PJ", 0, 2))
+    cp(X("fPC", 3, 6), X("PJ", 3, 6))
     PC = lambda i: X("fPC", i, i + 1)
-    P32, P16, P4, PAR, LC, PF = (PC(i) for i in range(6))
+    P32, P16, _, PAR, LC, PF = (PC(i) for i in range(6))
     cp(X("fTG", 64, 128), X("fTG", 0, 64))
     ms(blk(X("fTG", 0, 64), 0), -1000.0)
     ms(blk(X("fTG", 64, 128), 3), -1000.0)
@@ -470,13 +479,17 @@ def rank_program(g, core, T, topo):
     times(X("MT", 0, 16, 0, 128, 5), X("ONB", 0, 4), PC(6))
     times(X("MT", 16, 32, 0, 128, 5), X("ONB", 0, 4), P16)
     quant("MQ", 0, 132, "MT", 0, 528)
-    ms(X("fKR", 0, 32, 0, 64), 0.0)
-    ms(X("fKR", 96, 128, 64, 128), 0.0)
-    cp(X("fUZ"), X("UZ"))
-    for nm, c, q in (("ZT", 4, "ZQ"), ("UT", 0, "UQ")):
-        for t in range(4):
-            times(X(nm, t, 512, 0, 128, 4), X("ONB"), X("fUZ", c + t, c + t + 1))
-        quant(q, 0, 128, nm, 0, 512)
+    for h in ("HT", "HU"):
+        for t in (2, 3):
+            ms(X(h, t, 512, 0, 128, 4), 0.0)
+    ms(top(X("fKR", 0, 32)), 0.0)
+    ms(bot(X("fKR", 96, 128)), 0.0)
+    cp(X("fUZ", 0, 4), X("UZ", 0, 4))
+    for t in range(4):
+        ts(X("ZT", t, 512, 0, 128, 4), X("ONB"), X("UZ", 4 + t, 5 + t), O.mult)
+        times(X("UT", t, 512, 0, 128, 4), X("ONB"), X("fUZ", t, t + 1))
+    quant("ZQ", 0, 128, "ZT", 0, 512)
+    quant("UQ", 0, 128, "UT", 0, 512)
     quant("QT", 0, 192, "BT", 0, 768)
 
     def ahead(i, row, col, sign, c0, n, out):
@@ -486,11 +499,11 @@ def rank_program(g, core, T, topo):
         tt(out, s, X("MK", c0, c0 + n), O.is_gt)
         total(X("fRK", i, i + 1), out)
 
-    def places(q, out, n):
-        quant(q, 0, 128, "HT", 0, 512)
-        mm("p1", 128, q, 0, "MQ", 0, True, False)
-        mm("p1", 128, q, 0, "MQ", 4, False, True)
-        cp(X(out, 0, n), X("p1", 0, n))
+    def places(q, h, bank, out):
+        quant(q, 0, 128, h, 0, 512)
+        mm(bank, 128, q, 0, "MQ", 0, True, False)
+        mm(bank, 128, q, 0, "MQ", 4, False, True)
+        cp(out, X(bank, 0, 2))
 
     mm("p0", 128, "ZQ", 0, "QT", 64)
     mm("p1", 128, "QT", 64, "ZQ", 0)
@@ -500,21 +513,22 @@ def rank_program(g, core, T, topo):
     act(X("fAD", 32, 128), X("p0", 32, 128), AF.Abs)
     act(X("fAL"), X("p6", 0, 96), AF.Abs)
     ahead(0, X("fAD", 32, 128), "p1", 1, 32, 96, X("fCC", 0, 96))
+    for t in range(2):
+        ts(X("HU", t, 512, 0, 128, 4), X("fTG2"), X("fRK", 0, 1), O.subtract, -float((t - cl) % 2), O.is_equal)
+    places("HQ3", "HU", "p3", X("LO", 2, 4))
     ahead(1, X("fAL"), "p7", -1, 0, 96, X("fCC", 96, 192))
     for t in range(2):
         ts(X("HT", t, 256, 0, 128, 4), X("fTG", 0, 64), X("fRK", 0, 1), O.subtract, -16.0 * t, O.is_equal)
         ts(X("HT", 256 + t, 512, 0, 128, 4), X("fTG", 64, 128), X("fRK", 1, 2), O.subtract, -16.0 * t, O.is_equal)
-        ts(X("HT", 2 + t, 512, 0, 128, 4), X("fTG2"), X("fRK", 0, 1), O.subtract, -float((t - cl) % 2), O.is_equal)
-    places("HQ", "LO", 4)
+    places("HQ", "HT", "p1", X("LO", 0, 2))
     low = 2.0 ** -110
-    ts(X("fKR", 32, 128, 0, 64), X("fAD", 32, 128, 0, 64), low, O.max)
-    ts(X("fKR", 0, 96, 64, 128), X("fAL", 0, 96, 64, 128), -1.0, O.mult, -low, O.min)
+    ts(top(X("fKR", 32, 128)), top(X("fAD", 32, 128)), low, O.max)
+    ts(bot(X("fKR", 0, 96)), bot(X("fAL")), -1.0, O.mult, -low, O.min)
     gather(X("fRO"), X("fKR"), X("LO", 0, 2))
     tr(X("fKT"), X("fRO"))
     KEY = X("fKT", 0, 1)
     pick("SL1", 0, 32, "QT", 64, 192, ("LO", 2))
-    send1(1, "SL1", 0)
-    send_scores(1, KEY, "fSD")
+    send1(1, "SL1", 0, lambda: send_scores(1, KEY, "fSD"))
     cp(X("fSD", 4 * me, 4 * me + 1), KEY)
     act(X("fZA"), X("p2", 0, 128), AF.Abs)
     ts(X("fZR"), X("fZA"), low, O.max)
@@ -526,7 +540,6 @@ def rank_program(g, core, T, topo):
     f0 = len(nodes)
     iota(X("fROW"), [[16, 6], [0, 2], [1, 16]], 0)
     iota(X("fR32"), [[1, 32]], 0)
-    iota(X("fCT", 96, 128), [[0, 8], [1, 4]], 4 * m)
     iota(X("fJB"), [[16, 6]], 0)
     ms(X("BT", 1152, 1280), 0.0)
     quant("QT", 192, 320, "BT", 768, 1280)
@@ -536,20 +549,31 @@ def rank_program(g, core, T, topo):
         ms(X("R%d" % n, 0, None, 0, 128, n), 0.0)
     CT = lambda a, b: X("fCT", a, b)
     ts(CT(0, 32), X("fR32"), LC, O.subtract)
-    ts(CT(32, 64), X("fR32"), LC, O.subtract, 32.0, O.add)
-    ts(CT(96, 128), CT(96, 128), P32, O.is_equal)
-    ms(X("fCTX", 64, 128, 0, 64), -1000.0)
-    ts(X("fCTX", 0, 64, 0, 64), X("fROW", 0, 64, 0, 64), rows(LC, 0, 64), O.subtract, 32.0, O.add)
-    ts(X("fCTX", 0, 128, 64, 128), X("fROW", 0, 128, 64, 128), rows(LC, 64, 128), O.subtract)
-    if me in x2:
-        ts(X("fMM"), X("fROW", 0, 32), 16.0 * (x2.index(me) % 2), O.add, P32, O.is_equal)
-    else:
+    ts(CT(32, 64), CT(0, 32), 32.0, O.add)
+    ms(top(X("fCTX", 64, 128)), -1000.0)
+    ts(top(X("fCTX", 0, 64)), top(X("fROW", 0, 64)), top(LC), O.subtract, 32.0, O.add)
+    ts(bot(X("fCTX")), bot(X("fROW", 0, 128)), bot(LC), O.subtract)
+    cols, parts = [], []
+    for own, col in ((own3, 0), (own2, 2)):
+        for _, s0, n in own:
+            for c in range(-(-n // 16)):
+                lo = s0 + 16 * c
+                for lst in sorted({lo // 32, (min(lo + 16, s0 + n) - 1) // 32}):
+                    at = 32 * len(parts)
+                    ts(X("fMM", at, at + 32), X("fROW", 0, 32), float(lo - 32 * lst), O.add, P32, O.is_equal)
+                    for h in (0, 16):
+                        if s0 + n - lo < 16:
+                            ms(X("fMM", at + h + s0 + n - lo, at + h + 16), 0.0)
+                    parts.append((len(cols), lst))
+                cols.append((n, col + c))
+    ts(PC(14), P16, 16.0, O.add)
+    if me in e1:
         iota(X("fTG3"), [[0, 8], [1, 16]], 0)
     GQ, VO, VK = (X("fGV", i, i + 1) for i in range(3))
     ts(blk(PC(7), 0), blk(PAR, 0), float(cl), O.not_equal, 1024.0, O.mult)
     ts(blk(GQ, 0), blk(GN, 0), blk(PC(7), 0), O.add)
-    ts(rows(VO, 0, 64), rows(GN, 0, 64), float(P - P * me), O.add)
-    ts(rows(VO, 64, 128), rows(GN, 64, 128), -float(P * me), O.add)
+    ts(top(VO), top(GN), float(P - P * me), O.add)
+    ts(bot(VO), bot(GN), -float(P * me), O.add)
     ts(PC(8), LC, 32.0, O.is_lt)
     ts(PC(9), LC, 32.0, O.is_ge)
     times(X("fGV", 3, 4), KEY, PC(8))
@@ -561,31 +585,31 @@ def rank_program(g, core, T, topo):
     for h in range(2):
         ts(PC(11 + h), P16, -1.0, O.mult, 17.0 - 16 * h, O.add)
     ts(PC(13), P32, 32.0, O.add)
-    ts(X("fRP", 0, 64), X("fROW", 0, 64), PC(13), O.subtract, -1.0, O.mult)
-    ts(X("fRP", 64, 96), X("fR32"), PC(13), O.subtract, -1.0, O.mult)
+    ts(X("fRP", 0, 64), X("fROW", 0, 64), -1.0, O.mult, PC(13), O.add)
+    ts(X("fRP", 64, 96), X("fR32"), -1.0, O.mult, PC(13), O.add)
     ts(X("fID"), X("fR32"), P32, O.is_equal)
     ts(X("fPT"), X("fROW"), float(P * me), O.add)
     ts(X("fJB"), X("fJB"), P16, O.add)
     op("g", lambda: g.affine_select(T.DG[:], T.HAF[:], [[-1, 128]], O.is_equal, 0.0, 0, 1), [X("HAF")], [X("DG")], 0.55)
     for i in range(2):
         for j in range(2):
-            ms(X("ET", 528 * i + 264 * j, 528 * i + 264 * j + 264), 0.0)
+            zero(X("ET", 528 * i + 264 * j, 528 * i + 264 * j + 264))
         cp(X("ET", 528 * i + 2 + i, 528 * i + 514, 0, 128, 4), X("DG"))
         for j in range(2):
             quant("EQ", 128 * (i + 2 * j), 128 * (i + 2 * j) + 128, "ET", 528 * i + 2 - 2 * j, 528 * i + 514 - 2 * j)
     quant("WQ", 0, 128, "WT", 0, 512)
     ms(X("FLo", 6, 8), 0)
-    ms(X("NT", 128, 512), 0.0)
+    zero(X("NT", 128, 320))
+    zero(X("NT", 320, 512))
     ms(X("fNK", 32, 33), -low)
     dcol("y", "MV", 96, "QT", 0, 96)
     dcol("y", "DW", 0, "QT", 96, 96)
     for b in range(4):
         mm("p%d" % (2 + b), 128, "EQ", 128 * b, "QT", 192)
         act(X("fDN", 96 * b, 96 * b + 96), X("p%d" % (2 + b), 0, 96), AF.Copy)
-    mids = [X("fFM", i, i + 1) for i in range(6)]
-    for v, c in zip(mids, (64, 320, 96, 448, 128, 192)):
-        ts(v, P32, float(c), O.add)
-    a64, a320, a96, a448, a128, a192 = mids
+    a64, a320, a448, a128, a192 = (X("fFM", i, i + 1) for i in range(5))
+    for v, c in ((a64, 64), (top(a320), 320), (bot(a320), 96), (top(a448), 448), (bot(a128), 128), (bot(a192), 192)):
+        ts(v, rows(P32, v[3], v[4]), float(c), O.add)
     fill.update(range(f0, len(nodes)))
 
     def key(s):
@@ -601,30 +625,38 @@ def rank_program(g, core, T, topo):
                 ts(X("HT", t, 512, 0, 128, 4), X("fTG3"), X("fRK", 2, 3), O.subtract, -16.0 * t, O.is_equal)
             else:
                 ts(X("HT", t, 512, 0, 128, 4), X("fTG3"), X("fRK", 2, 3), O.add, 17.0 - 16 * t, O.is_equal)
-        places("HQ2", "O1o", 2)
+        places("HQ2", "HT", "p1", X("O1o"))
         pick("MG1", 0, 32, "LD1", 0, 128, ("O1o", 0))
 
     planes = (pa, pb) if rank in pa else (pb, pa)
+    RO = X("fRO")
     for i, grp in enumerate((near, far)):
         n, pl = 32 * len(grp), planes[i]
         for a in range(4):
             cp(blk(X("fSWA", 4 * i, 4 * i + 4), a), ("fSD", 4 * pl[0], 4 * pl[-1] + 1, 32 * (a ^ 1), 32 * (a ^ 1) + 32, 4 * (pl[1] - pl[0])))
         for j, s in enumerate(grp):
-            o = O.is_le if s < me else O.is_lt
-            w = 4 * i + pl.index(s)
-            ts(X("fCW", 128 * i + 32 * j, 128 * i + 32 * j + 32), X("fRO"), key(s), o)
-            ts(X("fCX", 128 * i + 32 * j, 128 * i + 32 * j + 32), X("fRO"), X("fSWA", w, w + 1), o)
+            w, at = 4 * i + pl.index(s), 128 * i + 32 * j
+            for out, kk in ((X("fCW", at, at + 32), key(s)), (X("fCX", at, at + 32), X("fSWA", w, w + 1))):
+                if s > me:
+                    either(lambda out=out, kk=kk: g.vector.tensor_scalar(ap(out), ap(RO), ap(kk), None, O.is_lt),
+                           lambda out=out, kk=kk: g.scalar.activation(ap(out), ap(RO), AF.Sign, bias=ap(kk), scale=-1.0), [RO, kk], [out], el(32))
+                else:
+                    ts(out, RO, kk, O.is_le)
         for k, (w, v) in enumerate((("fCW", "fCV"), ("fCX", "fCY"))):
-            tr(X(v, 128 * i, 128 * i + n), X(w, 128 * i, 128 * i + n))
-            total(X("fNF", 2 * k + i, 2 * k + i + 1), X(v, 128 * i, 128 * i + n))
+            vv, oo = X(v, 128 * i, 128 * i + n), X("fNF", 2 * k + i, 2 * k + i + 1)
+            tr(vv, X(w, 128 * i, 128 * i + n))
+            if max(grp) > me:
+                op("a", lambda vv=vv, oo=oo: g.scalar.activation(ap(vv), ap(vv), AF.Relu, accum_out=ap(oo)), [vv], [vv, oo], el(n) + 0.02)
+            else:
+                total(oo, vv)
         if i == 0:
             ts(X("fCT1"), CT(0, 32), X("fNF", 0, 1), O.subtract)
-            tt(X("fNF", 2, 3), X("fNF", 0, 1), X("fNF", 2, 3), O.add)
+            ts(X("fNF", 2, 3), X("fNF", 2, 3), X("fNF", 0, 1), O.add)
     CF = X("fCF")
     ts(CF, X("fNF", 2, 3), X("fNF", 1, 2), O.add, X("fNF", 3, 4), O.add)
     NF1 = X("fNF", 1, 2)
     ts(blk(X("fHN", 0, 32), 0), blk(X("fCT1"), 0), blk(NF1, 0), O.is_equal, blk(GQ, 0), O.mult)
-    ts(rows(X("fHN", 0, 32), 64, 128), rows(X("fCT1"), 64, 128), rows(NF1, 64, 128), O.is_equal, rows(GN, 64, 128), O.mult)
+    ts(bot(X("fHN", 0, 32)), bot(X("fCT1")), bot(NF1), O.is_equal, bot(GN), O.mult)
     ts(blk(X("fHN", 0, 32), 1), blk(X("fCT1"), 2), blk(NF1, 2), O.is_equal, blk(ZL, 2), O.mult)
     tr(X("fHM", 0, 32), X("fHN", 0, 32))
     total(X("fNL", 4 * me, 4 * me + 1), X("fHM", 0, 32))
@@ -643,9 +675,9 @@ def rank_program(g, core, T, topo):
     for a in range(4):
         cp(blk(X("fXT"), a), blk(s4, a ^ 1))
     tt(X("fXU"), s4, X("fXT"), O.add)
-    for h in (0, 64):
-        cp(X("X2o", 0, 4, h, h + 64), X("fXU", 0, 4, 64, 128))
-        cp(X("X2o", 4, 6, h, h + 64), X("fXU", 0, 2, 0, 64))
+    for h in (top, bot):
+        cp(h(X("X2o", 0, 4)), bot(X("fXU")))
+        cp(h(X("X2o", 4, 6)), top(X("fXU", 0, 2)))
     pick("SL2", 0, 96, "QT", 0, 192, ("X2o", 0))
     send1(2, "SL2", 0)
     pick("MV", 64, 32, "QT", 192, 288, ("X2o", 0))
@@ -653,9 +685,10 @@ def rank_program(g, core, T, topo):
         mm("p%d" % (2 + b), 128, "EQ", 128 * b, "MV", 64, True, False)
 
     red(X("fG2", 0, 1), ("fNL", 0, 32, 0, 128, 4))
-    DQ = X("fDQ", 0, 1)
+    DQ, L1g = X("fDQ", 0, 1), X("fDQ", 2, 3)
     for d in range(4):
         cp(blk(DQ, d), blk(X("fG2", 0, 1), 0))
+        cp(blk(L1g, d), blk(X("fG2", 0, 1), 2))
     ts(X("fUX", 32, 96), X("fTH", 64, 128), DQ, O.is_le, PC(10), O.mult)
     ts(X("fUX", 0, 32), X("fTH", 0, 32), DQ, O.is_le)
     ts(X("fUX", 96, 128), X("fTH", 32, 64), DQ, O.is_le)
@@ -668,10 +701,10 @@ def rank_program(g, core, T, topo):
     for a in range(4):
         for d in (a, a ^ 1):
             cp(blk(X("fGA", 2 * a, 2 * a + 2), d), blk(X("fG2"), a))
-    cp(X("fGA", 0, 4, 64, 128), X("fGA", 0, 4, 0, 64))
-    cp(X("fGA", 4, 8, 0, 64), X("fGA", 4, 8, 64, 128))
-    _, c2k, z1, c2g, L1g, o2k, _, o2g = (X("fGA", i, i + 1) for i in range(8))
-    D1g, L2g, H2g, A2 = (X("fG4", i, i + 1) for i in range(4))
+    cp(bot(X("fGA", 0, 4)), top(X("fGA", 0, 4)))
+    cp(top(X("fGA", 4, 8)), bot(X("fGA", 4, 8)))
+    _, c2k, z1, c2g, _, o2k, _, o2g = (X("fGA", i, i + 1) for i in range(8))
+    D1g, L2g, H2g = (X("fG4", i, i + 1) for i in range(3))
     ts(X("fDQ", 1, 2), DQ, 1024.0, O.is_ge, -1024.0, O.mult)
     ts(D1g, DQ, X("fDQ", 1, 2), O.add)
     dma("y", T.sw[0:1, :], ap(blk(D1g, 0)), [blk(D1g, 0)], [])
@@ -679,16 +712,16 @@ def rank_program(g, core, T, topo):
     ts(X("fOW", 0, 1), L1g, float(P * me), O.max, float(P * me + P - 1), O.min)
     ts(X("fOW", 1, 2), X("fOW", 0, 1), L1g, O.is_equal)
     times(X("fIDW"), X("fID"), X("fOW", 1, 2))
-    n = 2 if me in x2 else 1
-    times(X("fMW", 0, 32), CT(96, 128), L1g)
-    if me in x2:
-        times(X("fMW", 32, 64), X("fMM"), (L1g, o2g, c2g)[x2.index(me) // 2])
-    tr(X("fMX", 0, 32 * n), X("fMW", 0, 32 * n))
-    ts(X("fOM", 0, n), sums(X("fMS", 0, 32 * n), X("fMX", 0, 32 * n), 32), (P - 1) / 2, O.subtract, 1.0 / P, O.mult)
-    cp(X("MI", 0, n), X("fOM", 0, n))
-    ts(X("Mo", 0, 1), X("MI", 0, 1), 4.0, O.mult, P4, O.add)
-    if me in x2:
-        ts(X("Mo", 2, 3), X("MI", 1, 2), 16.0, O.mult, P16, O.add)
+    for i, (c, lst) in enumerate(parts):
+        times(X("fMW", 32 * i, 32 * i + 32), X("fMM", 32 * i, 32 * i + 32), (L1g, o2g, c2g)[lst])
+    tr(X("fMX", 0, 32 * len(parts)), X("fMW", 0, 32 * len(parts)))
+    for j in range(len(cols)):
+        at = [i for i, (c, _) in enumerate(parts) if c == j]
+        total(X("fOM", 4 + j, 5 + j), X("fMX", 32 * at[0], 32 * at[-1] + 32))
+    ts(X("fOM", 0, len(cols)), X("fOM", 4, 4 + len(cols)), (P - 1) / 2, O.subtract, 1.0 / P, O.mult)
+    cp(X("MI", 0, len(cols)), X("fOM", 0, len(cols)))
+    for j, (n, col) in enumerate(cols):
+        ts(X("Mo", col, col + 1), X("MI", j, j + 1), float(n), O.mult, PC(14) if col == 3 else P16, O.add)
 
     for b in range(4):
         mm("p%d" % (2 + b), 128, "EQ", 128 * b, "MV", 32, False, True)
@@ -699,8 +732,8 @@ def rank_program(g, core, T, topo):
     tt(X("fSC"), X("p6", 0, 32), X("fIDW"), O.mult)
     red(X("fNK", 4 * me, 4 * me + 1), X("fSC"), O.add, True, True)
     send1(3, "QT", 320, lambda: send_scores(2, X("fNK", 4 * me, 4 * me + 1), "fNK"))
-    if me in x2:
-        pick("MG2", 0, 16, "LD2", 0, 128, ("Mo", 2))
+    if own2:
+        pick("MG2", 0, 16 * -(-own2[0][2] // 16), "LD2", 0, 8 * own2[0][2], ("Mo", 2))
     send2(2)
 
     step = 2.0 ** -24
@@ -736,10 +769,9 @@ def rank_program(g, core, T, topo):
             return sums(X("fMJ" + w), X(ht, at, at + n), 64)
         total(out, X(ht, at, at + n))
 
-    def final(i, gcol, acol, out, old):
-        ts(X("fFH%d" % i), X("fPT"), gcol, O.is_equal, acol, O.mult)
+    def final(i):
         tr(X("fFT%d" % i), X("fFH%d" % i))
-        tt(out, sums(X("fFS%d" % i), X("fFT%d" % i), 32), old, O.max)
+        tt(X("fFL"), sums(X("fFS%d" % i), X("fFT%d" % i), 32), X("fFL") if i else X("fJB"), O.max)
 
     prep("", c2k, c2g, D1g)
     ranks("", z1)
@@ -747,8 +779,13 @@ def rank_program(g, core, T, topo):
     prep("b", o2k, o2g, L1g)
     hot("", 128, False, c2g, D1g, H2g)
     dma("y", T.sw[1:2, :], ap(blk(H2g, 0)), [blk(H2g, 0)], [])
-    final(0, L1g, a320, X("fFL"), X("fJB"))
-    final(1, D1g, a96, X("fFD"), X("fJB"))
+    G1, VA, VB = (X("fG5", i, i + 1) for i in range(3))
+    for v, t, b in ((G1, L1g, D1g), (VA, o2g, a128), (VB, L1g, a192)):
+        cp(top(v), top(t))
+        cp(bot(v), bot(b))
+    ts(X("fFH0"), X("fPT"), G1, O.is_equal, a320, O.mult)
+    final(0)
+    ts(bot(X("fFH2")), bot(X("fPT")), bot(H2g), O.is_equal)
     pick("MV", 0, 32, "DW", 96, 192, ("B2o", 0))
     for b in range(4):
         mm("p%d" % (2 + b), 128, "EQ", 128 * b, "MV", 0)
@@ -761,25 +798,27 @@ def rank_program(g, core, T, topo):
         o, w, d = X("NT", b, 128, 0, 128, 4), X("fDN", 96 * b, 96 * b + 96), X("fDB", 32 * b, 32 * b + 32)
         op("v", lambda o=o, w=w, d=d: g.vector.tensor_tensor(ap(o), ap(w).indirect(T.N2o[:]), ap(d), O.add), [w, d, X("N2o")], [o], el(110))
     quant("QT", 448, 576, "NT", 0, 512)
-    pick("MG3", 0, 16, "LD3", 0, 32, ("Mo", 0))
+    if own3:
+        pick("MG3", 0, 16, "LD3", 0, 8 * own3[0][2], ("Mo", 0))
     send2(3)
-    hot("b", 128, False, o2g, L1g, L2g)
-    final(2, L2g, a448, X("fFL"), X("fFL"))
-    cp(X("FLo", 0, 6), X("fFL"))
+    hot("b", 128, False, VA, VB, L2g)
+    ts(top(X("fFH1")), top(X("fPT")), top(L2g), O.is_equal, top(a448), O.mult)
+    times(bot(X("fFH1")), bot(X("fFH2")), bot(L2g))
+    final(1)
+    for h in (top, bot):
+        cp(h(X("FLo", 0, 6)), top(X("fFL")))
     pick("LF", 0, 128, "QT", 0, 576, ("FLo", 0))
     mm("p7", 128, "WQ", 0, "LF", 0)
-    dma("y", T.oc[:, 0:384], _codes(T, "LF", 0, 96), [X("LF", 0, 96)], [])
+    dma("y", T.oc[:, 0:384], _view(T, "LF", 0, 96), [X("LF", 0, 96)], [])
     for k in range(4):
         dma("y", T.osc[4 * k:4 * k + 4, 0:96], T.LFs[32 * k:32 * k + 4, 0:96], [X("LFs", 0, 96)], [])
     cp(X("fY"), X("p7", 0, 96))
     dma("a", T.y[:], T.fY[:], [X("fY")], [])
     dma("a", T.lw[1:2, :], ap(blk(L2g, 0)), [blk(L2g, 0)], [])
-
-    hot("b", 192, False, a128, a192, A2)
-    final(3, H2g, A2, X("fFD"), X("fFD"))
-    cp(X("FDo"), X("fFD"))
+    for h in (top, bot):
+        cp(h(X("FDo")), bot(X("fFL")))
     pick("DF", 0, 96, "DW", 0, 224, ("FDo", 0))
-    dma("y", T.oc[:, 384:768], _codes(T, "DF", 0, 96), [X("DF", 0, 96)], [])
+    dma("y", T.oc[:, 384:768], _view(T, "DF", 0, 96), [X("DF", 0, 96)], [])
     for k in range(4):
         dma("a" if k % 2 else "y", T.osc[4 * k:4 * k + 4, 96:192], T.DFs[32 * k:32 * k + 4, 0:96], [X("DFs", 0, 96)], [])
     schedule()

@@ -8,24 +8,26 @@ P = 96
 F32, BF, I32, U16 = "float32", "bfloat16", "int32", "uint16"
 SCRATCH = {}
 for _n, _w in {"BT": 1280, "WT": 512, "UZ": 8, "UT": 512, "ZT": 512, "ONB": 128, "HAF": 128, "DG": 128, "ET": 1056, "NT": 512, "HT": 512, "HU": 512,
-               "MT": 528, "SG": 384, "MK": 128, "R32": 192, "R64": 128}.items():
+               "MT": 528, "SG": 384, "MK": 128, "fTG": 128, "fTG2": 128, "fTG3": 128, "R32": 192, "R64": 128}.items():
     SCRATCH[_n] = ("sbuf", [128, _w], BF)
 for _n, _w in {"PJ": 6, "MI": 4}.items():
     SCRATCH[_n] = ("sbuf", [128, _w], I32)
-for _n, _w in {"LO": 4, "Mo": 4, "O1o": 2, "UOo": 2, "X2o": 6, "B2o": 2, "N2o": 2, "FLo": 8, "FDo": 6}.items():
+for _n, _w in {"LO": 4, "Mo": 4, "O1o": 2, "UOo": 2, "X2o": 6, "B2o": 2, "N2o": 2, "FLo": 6, "FDo": 6}.items():
     SCRATCH[_n] = ("sbuf", [128, _w], U16)
 for _n, _w in {"QT": 576, "UQ": 128, "ZQ": 128, "EQ": 512, "WQ": 128, "HQ": 128, "HQ2": 128, "HQ3": 128, "MQ": 132, "SL1": 32, "LD1": 128, "MG1": 32,
-               "UO": 36, "SL2": 96, "LD2": 160, "MG2": 32, "LD3": 96, "MG3": 16, "DW": 224, "MV": 192, "LF": 128, "DF": 96,
+               "UO": 36, "SL2": 96, "LD2": 160, "MG2": 32, "LD3": 96, "MG3": 16, "DW": 224, "MV": 192, "LF": 224,
                "RC1": 16, "RC2": 48, "RC3": 16, "RW1": 18, "RW2": 20, "RW3": 12}.items():
     SCRATCH[_n] = ("sbuf", [128, _w], "float8_e4m3fn_x4")
     SCRATCH[_n + "s"] = ("sbuf", [128, _w], "uint8")
+for _n, _w in {"SL1s": 96, "RC1s": 64}.items():
+    SCRATCH[_n] = ("sbuf", [128, _w], "uint8")
 for _n, _w in {"RS1": 1, "RS2": 1, "RS3": 1, "RS4": 1, "SD": 32, "NL": 32, "NM": 32, "NK": 36, "Y": 96, "KT": 32}.items():
     SCRATCH["f" + _n] = ("sbuf", [128, _w], F32)
-_V = {"UZ": 8, "PC": 16, "AD": 128, "AL": 96, "CD": 4, "CC": 192, "RK": 4, "TG": 128, "TG2": 128, "TG3": 128, "OA": 128, "OC": 128, "DN": 384, "DB": 128}
+_V = {"UZ": 8, "PC": 16, "AD": 128, "AL": 96, "CD": 4, "CC": 192, "RK": 4, "OA": 128, "OC": 128, "DN": 384, "DB": 128}
 _F = {"ON": 32, "ROW": 192, "R32": 32, "PT": 192, "JB": 6, "KR": 128, "PR": 128, "ZA": 128, "ZR": 128, "RO": 32, "GZ": 64, "GT": 64, "GV": 4,
       "CT": 64, "CTX": 128, "CT1": 32, "TH": 128, "RP": 96, "ID": 32, "SWA": 8, "CW": 256, "CV": 256, "CX": 256, "CY": 256, "NF": 4, "CF": 1,
-      "HN": 96, "HM": 96, "H2": 128, "H2t": 128, "H2s": 128, "XT": 4, "XU": 4, "G2": 2, "DQ": 4, "GA": 8, "UX": 128, "UT": 128, "US": 128,
-      "OW": 2, "IDW": 32, "MM": 160, "MW": 160, "MX": 160, "OM": 8, "SC": 32, "NB": 1, "FM": 8, "G4": 4, "G5": 4, "FL": 6,
+      "HN": 96, "HM": 96, "H2": 128, "H2t": 128, "H2s": 128, "XT": 4, "XU": 4, "G2": 2, "DQ": 4, "GA": 8, "UX": 64, "UT": 64, "US": 64,
+      "OW": 2, "IDW": 32, "MM": 160, "MW": 160, "MX": 160, "OM": 8, "SC": 32, "NB": 1, "JK": 16, "FM": 8, "G4": 4, "G5": 4, "FL": 6,
       "FH0": 192, "FH1": 192, "FH2": 192, "FT0": 192, "FT1": 192, "FS0": 192, "FS1": 192}
 for _n, _w in (("ME", 64), ("MR", 32), ("MG", 64), ("MK", 32), ("MT", 96), ("MU", 64), ("ML", 4), ("MH", 192), ("MI", 192), ("MJ", 128)):
     _F[_n] = _F[_n + "b"] = _w
@@ -42,18 +44,18 @@ SEMAPHORES = ["vs", "ac", "te", "gp", "ls"] + [_s + str(_k) for _k in (1, 2, 3, 
 for _x in (1, 2, 3):
     SEMAPHORES += ["a%d" % _x, "b%d" % _x, "qc%d" % _x, "qs%d" % _x, "wc%d" % _x, "ws%d" % _x]
 SEMAPHORES += ["d%d" % _i for _i in range(60)]
-WAKE, PIPE, CYCLE, SLACK, QUIET, GAP, BIAS = 0.1, 0.06, 0.00083, 0.03, 1.8, 0.05, 0.08
-LATE = {"n1": 2.0, "s1": 4.0, "a1": 4.2, "b1": 3.03, "n3": 1.9, "s3": 2.0, "n4": 1.9, "s4": 3.1, "n2": 2.14, "s2": 3.5, "a2": 3.2, "b2": 3.1,
-        "a3": 3.5, "b3": 3.45, "small": 1.5, "big": 1.8, "dma": 2.0, "c0": 1.5, "c1": 0.3, "c2": 0.3, "c3": 0.7, "c": 0.6}
-WHEN = {"sn1": [9.8, 10.1, 10.4, 10.4], "sa1": [12.0, 12.3, 12.2, 12.5], "a1": [11.7, 0.0, 0.0, 0.0], "b1": [18.8, 19.1, 19.4, 19.6],
-        "sn3": [15.6, 15.9, 16.1, 15.8], "sa3": [16.9, 17.2, 17.1, 17.4], "sn4": [16.7, 18.8, 19.1, 19.4], "sa4": [19.1, 19.4, 19.4, 19.6],
-        "a2": [0.0, 21.8, 21.1, 21.4], "sn2": [24.0, 24.3, 24.5, 24.4], "sa2": [24.9, 25.1, 25.1, 25.4], "b2": [26.4, 26.6, 26.9, 27.0],
-        "a3": [24.9, 24.4, 0.0, 0.0], "b3": [29.2, 29.4, 29.7, 29.9]}
+WAKE, PIPE, CYCLE, QUIET, GAP, BIAS = 0.1, 0.06, 0.00083, 1.8, 0.05, 0.05
+LATE = {"n1": 2.0, "s1": 4.0, "a1": 4.2, "b1": 3.03, "n3": 1.9, "s3": 2.0, "n4": 1.9, "s4": 2.1, "n2": 2.14, "s2": 3.5, "a2": 3.2, "b2": 3.1,
+        "a3": 3.7, "b3": 3.45, "small": 1.5, "big": 1.6, "dma": 2.0, "c0": 1.5, "c1": 0.3, "c2": 0.7, "c3": 0.3, "c": 0.1}
+WHEN = {"sn1": [9.6, 9.8, 10.1, 10.1], "sa1": [11.9, 12.1, 12.1, 12.4], "a1": [11.6, 0.0, 0.0, 0.0], "b1": [17.8, 18.1, 17.9, 18.3],
+        "sn3": [15.4, 15.6, 15.9, 15.8], "sa3": [16.8, 16.9, 16.9, 17.2], "sn4": [16.8, 18.1, 18.4, 18.6], "sa4": [18.6, 18.9, 18.9, 19.1],
+        "a2": [0.0, 20.9, 20.4, 20.6], "sn2": [22.5, 22.8, 23.0, 22.9], "sa2": [23.8, 24.0, 24.1, 24.4], "b2": [25.1, 25.4, 25.4, 25.5],
+        "a3": [23.8, 23.4, 0.0, 0.0], "b3": [27.4, 27.5, 27.6, 27.9]}
 SHARE = {1: (16, 0, 0, 0), 2: (0, 8, 20, 20), 3: (4, 12, 0, 0)}
 HALF = {_x: sum(_v) for _x, _v in SHARE.items()}
 LAND = {1: ("UO", 0), 2: ("DW", 96), 3: ("DW", 192)}
 PAIR = {1: (1, 2), 2: (0, 3), 3: (1, 2)}
-OTHER = {2: (1, 2), 3: (0, 3)}
+OTHER = {1: (0, 3), 2: (1, 2), 3: (0, 3)}
 
 
 def _layout(T, topo):
@@ -117,7 +119,8 @@ def _hand_on(g, core, T, topo, rank, far):
         return _remote(g, T, topo, core, [(T["fRS%d" % k][:], [(T.cores[r], T[dst][:, 4 * rank:4 * rank + 1]) for r in to], eng, "sa%d" % k)])
 
     def first(x, to):
-        g.wait_ge(T.sem[("qc%d" if codes else "qs%d") % x], n_on)
+        half = x == 1 or (x == 2 and rank in (a[0], b[0]))
+        g.wait_ge(T.sem[("qc%d" if codes else "qs%d") % x], n_on // 2 if half else n_on)
         n = 0
         for r, s0, w in sorted(_owners(x, a + b), key=lambda o: -o[2]):
             if r in to:
@@ -127,16 +130,18 @@ def _hand_on(g, core, T, topo, rank, far):
 
     def second(x):
         nm, base = LAND[x]
+        h = 0 if me in PAIR[x] else 1
+        to = far[2 * h:2 * h + 2] + (near[h:h + 1] if codes else [])
         for r, s0, n in _owners(x, a + b, 2):
             if r == rank:
                 g.wait_ge(T.sem[("wc%d" if codes else "ws%d") % x], n_on)
-                return _remote(g, T, topo, core, [(_view(T, "RW%d" % x, 0, n, codes), [(T.cores[r], _view(T, nm, base + s0, base + s0 + n, codes)) for r in far], eng, "b%d" % x)])
+                return _remote(g, T, topo, core, [(_view(T, "RW%d" % x, 0, n, codes), [(T.cores[r], _view(T, nm, base + s0, base + s0 + n, codes)) for r in to], eng, "b%d" % x)])
         return 0
 
     if me in PAIR[1]:
-        ls = first(1, far) + second(1) + first(2, near) + first(3, far) + second(3)
+        ls = first(1, far) + second(1) + first(2, near) + first(3, far) + second(2) + second(3)
     else:
-        ls = scores(1) + scores(3) + scores(4) + first(2, far) + first(3, near) + scores(2) + second(2)
+        ls = scores(1) + scores(3) + second(1) + scores(4) + first(2, far) + first(3, near) + scores(2) + second(2) + second(3)
     g.wait_ge(T.sem.ls, ls)
 
 
@@ -155,6 +160,7 @@ def rank_program(g, core, T, topo):
     hs = _helpers(core, T.cores[far[0]], topo)
     e_off = topo.engines(core, T.cores[near[0]])
     e_on = [e for e in topo.engines(core, hs[0]) if e not in e_off]
+    e_a, e_b = e_on[:len(e_on) // 2], e_on[len(e_on) // 2:]
     me = rank
 
     Q = {"v": g.vector, "a": g.scalar, "t": g.tensor, "g": g, "y": g.sync}
@@ -260,7 +266,7 @@ def rank_program(g, core, T, topo):
                 if k in fill and q in SEM:
                     keep = [(QUIET if q != "g" else done[sent[0]] - LATE["c0"] - 0.8, done[sent[0]])]
                 for b0, b1 in sorted(busy.get(q, []) + keep):
-                    if t + d + (GAP if k in fill else -SLACK) <= b0:
+                    if t + d + (GAP if k in fill else 0.0) <= b0:
                         break
                     t = max(t, b1)
                 if best is None or t + c < best[0] + nodes[k][0][best[1]][1] + BIAS:
@@ -327,15 +333,21 @@ def rank_program(g, core, T, topo):
     def ts(out, a, s1, op0, s2=None, op1=None):
         p1, r1 = sc(s1)
         p2, r2 = sc(s2)
-        plain = SCRATCH[out[0]][2] == F32 and SCRATCH[a[0]][2] == F32
-        if plain and op1 is None and op0 == O.add:
-            either(lambda: g.vector.tensor_scalar(ap(out), ap(a), p1, None, op0), lambda: g.scalar.activation(ap(out), ap(a), AF.Identity, bias=p1), [a] + r1, [out], el(width(out)))
-        elif plain and op0 == O.mult and op1 == O.add:
-            either(lambda: g.vector.tensor_scalar(ap(out), ap(a), p1, p2, op0, op1), lambda: g.scalar.activation(ap(out), ap(a), AF.Identity, bias=p2, scale=p1), [a] + r1 + r2, [out], el(width(out)))
-        elif op1 is None:
-            op("v", lambda: g.vector.tensor_scalar(ap(out), ap(a), p1, None, op0), [a] + r1, [out], el(width(out)))
+        kinds = SCRATCH[out[0]][2], SCRATCH[a[0]][2]
+        args = (p1, None, op0) if op1 is None else (p1, p2, op0, op1)
+        v = lambda: g.vector.tensor_scalar(ap(out), ap(a), *args)
+        other = None
+        if kinds == (F32, F32):
+            if op1 is None and op0 == O.add:
+                other = {"bias": p1}
+            elif op0 == O.mult and op1 == O.add:
+                other = {"bias": p2, "scale": p1}
+            elif op0 == O.add and s1 == 1.0 and op1 == O.mult:
+                other = {"bias": p2, "scale": p2}
+        if other:
+            either(v, lambda: g.scalar.activation(ap(out), ap(a), AF.Identity, **other), [a] + r1 + r2, [out], el(width(out)))
         else:
-            op("v", lambda: g.vector.tensor_scalar(ap(out), ap(a), p1, p2, op0, op1), [a] + r1 + r2, [out], el(width(out)))
+            op("v", v, [a] + r1 + r2, [out], el(width(out), 0.5 if kinds == (BF, BF) and op1 is not None else 1.0))
 
     def tt(out, a, b, o):
         op("v", lambda: g.vector.tensor_tensor(ap(out), ap(a), ap(b), o), [a, b], [out], el(width(out), 2.0))
@@ -353,12 +365,13 @@ def rank_program(g, core, T, topo):
     def red(out, a, o=O.add, neg=False, ab=False):
         op("v", lambda: g.vector.tensor_reduce(ap(out), ap(a), AxisListType.X, o, negate=neg, apply_absolute_value=ab), [a], [out], el(width(a)))
 
-    def total(out, a):
+    def total(out, a, b=None):
+        b = b or a
         either(lambda: g.vector.tensor_reduce(ap(out), ap(a), AxisListType.X, O.add),
-               lambda: g.scalar.activation(ap(a), ap(a), AF.Copy, accum_out=ap(out)), [a], [a, out], el(width(a)))
+               lambda: g.scalar.activation(ap(b), ap(a), AF.Copy, accum_out=ap(out)), [a], [b, out], el(width(a)))
 
     def sums(out, a, n):
-        r = X("R%d" % n, 0, width(a))
+        r = X("R%d" % n, 0, width(a), a[3], a[4])
         op("v", lambda: g.vector.tensor_tensor_scan(ap(out), ap(r), ap(a), 0.0, O.mult, O.add), [r, a], [out], el(width(a)))
         return (out[0], out[1] + n - 1, out[2], out[3], out[4], n)
 
@@ -376,7 +389,7 @@ def rank_program(g, core, T, topo):
         if bias is None:
             op("a", lambda: g.scalar.activation(ap(out), ap(a), func), [a], [out], el(width(out)) + 0.02)
         else:
-            op("a", lambda: g.scalar.activation(ap(out), ap(a), func, bias=ap(bias), scale=scale), [a, bias], [out], el(width(out)) + 0.02)
+            op("a", lambda: g.scalar.activation(ap(out), ap(a), func, bias=sc(bias)[0], scale=sc(scale)[0]), [a] + sc(bias)[1] + sc(scale)[1], [out], el(width(out)) + 0.02)
 
     def iota(out, pat, base, cm=0):
         kw = {} if SCRATCH[out[0]][2] == I32 else {"allow_small_or_imprecise_dtypes": True}
@@ -387,7 +400,7 @@ def rank_program(g, core, T, topo):
 
     def mm(bank, n, l, l0, r, r0, start=True, stop=True):
         op("t", lambda: g.tensor.matmul_mx(T[bank][:, 0:n], T[l][:, l0:l0 + 128], T[l + "s"][:, l0:l0 + 128], T[r][:, r0:r0 + n], T[r + "s"][:, r0:r0 + n], start, stop),
-           [X(l, l0, l0 + 128), X(l + "s", l0, l0 + 128), X(r, r0, r0 + n), X(r + "s", r0, r0 + n)], [X(bank, 0, n)], PIPE + 0.001 * (n + 16))
+           [X(l, l0, l0 + 128), X(l + "s", l0, l0 + 128), X(r, r0, r0 + n), X(r + "s", r0, r0 + n)], [X(bank, 0, n)], PIPE + 0.0008 * (n + 16))
 
     def pick(dst, d0, n, win, a, b, off):
         ov = X(off[0], off[1], off[1] + n // 16)
@@ -401,14 +414,17 @@ def rank_program(g, core, T, topo):
     def send1(x, src, s0, between=lambda: None):
         own, w = _owners(x, order), HALF[x]
         p, p2 = (s0 + w, s0) if me in pa else (s0, s0 + w)
-        for h, k in enumerate(("qc%d" % x, "qs%d" % x)):
-            mv = [(_view(T, src, p, p + w, not h), [(hs[PAIR[x][h]], _view(T, "RC%d" % x, 0, w, not h))], e_on, k)]
-            if x in OTHER:
-                mv.append((_view(T, src, p2, p2 + w, not h), [(hs[OTHER[x][h]], _view(T, "RC%d" % x, 0, w, not h))], e_off, k))
-            send(mv, [X(src + "s" * h, s0, s0 + 2 * w)])
+        if x == 1:
+            send([(_view(T, src, p, p + w), [(hs[PAIR[x][0]], _view(T, "RC1", 0, w))], e_a, "qc1"),
+                  (_view(T, src, p, p + 4 * w, False), [(hs[PAIR[x][1]], _view(T, "RC1", 0, 4 * w, False))], e_b, "qs1")], [X(src, p, p + w), X(src + "s", p, p + 4 * w)])
+        else:
+            ea, eb = (e_a, e_b) if x == 2 and me in e1 else (e_on, e_off)
+            for h, k in enumerate(("qc%d" % x, "qs%d" % x)):
+                send([(_view(T, src, p, p + w, not h), [(hs[PAIR[x][h]], _view(T, "RC%d" % x, 0, w, not h))], ea, k),
+                      (_view(T, src, p2, p2 + w, not h), [(hs[OTHER[x][h]], _view(T, "RC%d" % x, 0, w, not h))], eb, k)], [X(src + "s" * h, s0, s0 + 2 * w)])
         between()
         for r, c, n in own:
-            if r in near and x not in OTHER:
+            if r in near and x == 1:
                 for h in range(2):
                     send([(_view(T, src, s0 + c, s0 + c + n, not h), [(T.cores[r], _view(T, "LD%d" % x, n * me, n * me + n, not h))], e_off, "a%d" % x)], [X(src + "s" * h, s0 + c, s0 + c + n)])
             if r == me:
@@ -423,22 +439,18 @@ def rank_program(g, core, T, topo):
         for r, c, n in own:
             if r == me:
                 for h, k in enumerate(("wc%d" % x, "ws%d" % x)):
-                    sap = _view(T, src, 0, n, not h)
-                    send([(sap, [(hs[PAIR[x][h]], _view(T, "RW%d" % x, 0, n, not h))], e_on, k),
-                          (sap, [(T.cores[r], _view(T, nm, base + c, base + c + n, not h)) for r in near], e_off, "b%d" % x)], [X(src + "s" * h, 0, n)])
+                    sap, hap = _view(T, src, 0, n, not h), _view(T, "RW%d" % x, 0, n, not h)
+                    send([(sap, [(hs[PAIR[x][h]], hap)], e_on, k), (sap, [(hs[OTHER[x][h]], hap)], e_off, k)], [X(src + "s" * h, 0, n)])
+                for h in (1, 0):
+                    send([(_view(T, src, 0, n, not h), [(T.cores[r], _view(T, nm, base + c, base + c + n, not h)) for r in (near if h else near[2:])], e_off, "b%d" % x)], [X(src + "s" * h, 0, n)])
                 dcol("y", nm, base + c, src, 0, n)
         oth = [(base + c, n) for r, c, n in own if r != me]
         arrive([X(k, c, c + n) for k in (nm, nm + "s") for c, n in oth], "b%d" % x, len(oth) * 2 * len(e_off), LATE["b%d" % x])
 
     def send_scores(k, src, dst):
-        to = [(hs[h], T["fRS%d" % k][:]) for h in PAIR[2]]
-        fm = (ap(src), to, e_on, "sr%d" % k)
+        fm = (ap(src), [(hs[h], T["fRS%d" % k][:]) for h in PAIR[2]], e_on, "sr%d" % k)
         nm = (ap(src), [(T.cores[r], T[dst][:, 4 * me:4 * me + 1]) for r in near], e_off, "sn%d" % k)
-        if k == 2:
-            calls = ([(ap(src), to[:1], e_on, "sr2"), (ap(src), to[1:], e_off, "sr2")], [nm])
-        else:
-            calls = ([fm], [nm]) if k == 1 else ([fm, nm],)
-        for mv in calls:
+        for mv in ([fm], [nm]) if k == 1 else ([fm, nm],):
             send(mv, [src])
         arrive([X(dst, 4 * r, 4 * r + 1) for r in near], "sn%d" % k, len(near) * len(e_off), LATE["n%d" % k])
         arrive([X(dst, 4 * r, 4 * r + 1) for r in far], "sa%d" % k, len(far) * len(e_off), LATE["s%d" % k])
@@ -499,11 +511,11 @@ def rank_program(g, core, T, topo):
         tt(out, s, X("MK", c0, c0 + n), O.is_gt)
         total(X("fRK", i, i + 1), out)
 
-    def places(q, h, bank, out):
+    def places(q, h, bank, out, c0):
         quant(q, 0, 128, h, 0, 512)
-        mm(bank, 128, q, 0, "MQ", 0, True, False)
-        mm(bank, 128, q, 0, "MQ", 4, False, True)
-        cp(out, X(bank, 0, 2))
+        mm(bank, 128, q, 0, "MQ", 0)
+        for t in range(2):
+            ts(X(out, c0 + t, c0 + t + 1), X(bank, t, t + 1), X(bank, 4 + t, 5 + t), O.add)
 
     mm("p0", 128, "ZQ", 0, "QT", 64)
     mm("p1", 128, "QT", 64, "ZQ", 0)
@@ -515,18 +527,19 @@ def rank_program(g, core, T, topo):
     ahead(0, X("fAD", 32, 128), "p1", 1, 32, 96, X("fCC", 0, 96))
     for t in range(2):
         ts(X("HU", t, 512, 0, 128, 4), X("fTG2"), X("fRK", 0, 1), O.subtract, -float((t - cl) % 2), O.is_equal)
-    places("HQ3", "HU", "p3", X("LO", 2, 4))
+    places("HQ3", "HU", "p3", "LO", 2)
     ahead(1, X("fAL"), "p7", -1, 0, 96, X("fCC", 96, 192))
     for t in range(2):
         ts(X("HT", t, 256, 0, 128, 4), X("fTG", 0, 64), X("fRK", 0, 1), O.subtract, -16.0 * t, O.is_equal)
         ts(X("HT", 256 + t, 512, 0, 128, 4), X("fTG", 64, 128), X("fRK", 1, 2), O.subtract, -16.0 * t, O.is_equal)
-    places("HQ", "HT", "p1", X("LO", 0, 2))
+    places("HQ", "HT", "p1", "LO", 0)
     low = 2.0 ** -110
     ts(top(X("fKR", 32, 128)), top(X("fAD", 32, 128)), low, O.max)
     ts(bot(X("fKR", 0, 96)), bot(X("fAL")), -1.0, O.mult, -low, O.min)
     gather(X("fRO"), X("fKR"), X("LO", 0, 2))
     tr(X("fKT"), X("fRO"))
     KEY = X("fKT", 0, 1)
+    dma("y", T.SL1s[:, 32:96], T.QTs[:, 0:64], [X("QTs", 0, 64)], [X("SL1s", 32, 96)], "small")
     pick("SL1", 0, 32, "QT", 64, 192, ("LO", 2))
     send1(1, "SL1", 0, lambda: send_scores(1, KEY, "fSD"))
     cp(X("fSD", 4 * me, 4 * me + 1), KEY)
@@ -569,21 +582,19 @@ def rank_program(g, core, T, topo):
     ts(PC(14), P16, 16.0, O.add)
     if me in e1:
         iota(X("fTG3"), [[0, 8], [1, 16]], 0)
-    GQ, VO, VK = (X("fGV", i, i + 1) for i in range(3))
-    ts(blk(PC(7), 0), blk(PAR, 0), float(cl), O.not_equal, 1024.0, O.mult)
-    ts(blk(GQ, 0), blk(GN, 0), blk(PC(7), 0), O.add)
+    VO, VK = (X("fGV", i, i + 1) for i in range(2))
+    ts(blk(PC(7), 0), blk(PAR, 0), 2.0 - 4.0 * cl, O.mult, 2.0 * cl - 1.0, O.add)
     ts(top(VO), top(GN), float(P - P * me), O.add)
     ts(bot(VO), bot(GN), -float(P * me), O.add)
     ts(PC(8), LC, 32.0, O.is_lt)
     ts(PC(9), LC, 32.0, O.is_ge)
     times(X("fGV", 3, 4), KEY, PC(8))
     ts(VK, GN, PC(9), O.mult, X("fGV", 3, 4), O.add)
-    ts(X("fTH", 0, 64), X("fROW", 0, 64), P32, O.is_le, 3072.0, O.mult)
-    ts(X("fTH", 64, 128), X("fROW", 0, 64), P32, O.not_equal, 3072.0, O.mult)
-    ts(X("fTH"), X("fTH"), 1024.0, O.add)
-    ts(PC(10), P32, 1.0, O.add)
-    for h in range(2):
-        ts(PC(11 + h), P16, -1.0, O.mult, 17.0 - 16 * h, O.add)
+    b3 = lambda v: blk(v, 3)
+    ts(b3(PC(10)), b3(P32), 0.5, O.mult, 0.5, O.add)
+    ts(b3(X("fTH", 0, 64)), b3(X("fROW", 0, 64)), b3(P32), O.is_gt, 0.5, O.mult)
+    ts(b3(X("fTH", 64, 128)), b3(X("fROW", 0, 64)), b3(P32), O.is_equal, b3(PC(10)), O.mult)
+    tt(b3(X("fTH", 0, 64)), b3(X("fTH", 0, 64)), b3(X("fTH", 64, 128)), O.add)
     ts(PC(13), P32, 32.0, O.add)
     ts(X("fRP", 0, 64), X("fROW", 0, 64), -1.0, O.mult, PC(13), O.add)
     ts(X("fRP", 64, 96), X("fR32"), -1.0, O.mult, PC(13), O.add)
@@ -598,7 +609,7 @@ def rank_program(g, core, T, topo):
         for j in range(2):
             quant("EQ", 128 * (i + 2 * j), 128 * (i + 2 * j) + 128, "ET", 528 * i + 2 - 2 * j, 528 * i + 514 - 2 * j)
     quant("WQ", 0, 128, "WT", 0, 512)
-    ms(X("FLo", 6, 8), 0)
+    dcol("y", "LF", 0, "QT", 0, 32)
     zero(X("NT", 128, 320))
     zero(X("NT", 320, 512))
     ms(X("fNK", 32, 33), -low)
@@ -607,9 +618,10 @@ def rank_program(g, core, T, topo):
     for b in range(4):
         mm("p%d" % (2 + b), 128, "EQ", 128 * b, "QT", 192)
         act(X("fDN", 96 * b, 96 * b + 96), X("p%d" % (2 + b), 0, 96), AF.Copy)
-    a64, a320, a448, a128, a192 = (X("fFM", i, i + 1) for i in range(5))
+    a64, a320, a448, a128, a192, n320 = (X("fFM", i, i + 1) for i in range(6))
     for v, c in ((a64, 64), (top(a320), 320), (bot(a320), 96), (top(a448), 448), (bot(a128), 128), (bot(a192), 192)):
         ts(v, rows(P32, v[3], v[4]), float(c), O.add)
+    ts(n320, a320, -1.0, O.mult, 0.0, O.add)
     fill.update(range(f0, len(nodes)))
 
     def key(s):
@@ -625,39 +637,38 @@ def rank_program(g, core, T, topo):
                 ts(X("HT", t, 512, 0, 128, 4), X("fTG3"), X("fRK", 2, 3), O.subtract, -16.0 * t, O.is_equal)
             else:
                 ts(X("HT", t, 512, 0, 128, 4), X("fTG3"), X("fRK", 2, 3), O.add, 17.0 - 16 * t, O.is_equal)
-        places("HQ2", "HT", "p1", X("O1o"))
+        places("HQ2", "HT", "p1", "O1o", 0)
         pick("MG1", 0, 32, "LD1", 0, 128, ("O1o", 0))
 
     planes = (pa, pb) if rank in pa else (pb, pa)
     RO = X("fRO")
     for i, grp in enumerate((near, far)):
         n, pl = 32 * len(grp), planes[i]
+        below = 2 * sum(s < me for s in grp) > len(grp)
         for a in range(4):
             cp(blk(X("fSWA", 4 * i, 4 * i + 4), a), ("fSD", 4 * pl[0], 4 * pl[-1] + 1, 32 * (a ^ 1), 32 * (a ^ 1) + 32, 4 * (pl[1] - pl[0])))
         for j, s in enumerate(grp):
             w, at = 4 * i + pl.index(s), 128 * i + 32 * j
             for out, kk in ((X("fCW", at, at + 32), key(s)), (X("fCX", at, at + 32), X("fSWA", w, w + 1))):
-                if s > me:
-                    either(lambda out=out, kk=kk: g.vector.tensor_scalar(ap(out), ap(RO), ap(kk), None, O.is_lt),
-                           lambda out=out, kk=kk: g.scalar.activation(ap(out), ap(RO), AF.Sign, bias=ap(kk), scale=-1.0), [RO, kk], [out], el(32))
+                args = (O.is_lt if s > me else O.is_le,) + ((O.subtract,) if below else ())
+                v = lambda out=out, kk=kk, args=args: g.vector.tensor_scalar(ap(out), ap(RO), ap(kk), 1.0 if len(args) > 1 else None, *args)
+                if (s < me) == below:
+                    either(v, lambda out=out, kk=kk: g.scalar.activation(ap(out), ap(RO), AF.Sign, bias=ap(kk), scale=-1.0), [RO, kk], [out], el(32))
                 else:
-                    ts(out, RO, kk, O.is_le)
+                    op("v", v, [RO, kk], [out], el(32))
         for k, (w, v) in enumerate((("fCW", "fCV"), ("fCX", "fCY"))):
             vv, oo = X(v, 128 * i, 128 * i + n), X("fNF", 2 * k + i, 2 * k + i + 1)
             tr(vv, X(w, 128 * i, 128 * i + n))
-            if max(grp) > me:
-                op("a", lambda vv=vv, oo=oo: g.scalar.activation(ap(vv), ap(vv), AF.Relu, accum_out=ap(oo)), [vv], [vv, oo], el(n) + 0.02)
-            else:
-                total(oo, vv)
+            f, b = (AF.Sign, 1.0) if below else (AF.Relu, 0.0)
+            op("a", lambda vv=vv, oo=oo, f=f, b=b: g.scalar.activation(ap(vv), ap(vv), f, bias=b, accum_out=ap(oo)), [vv], [vv, oo], el(n) + 0.02)
         if i == 0:
             ts(X("fCT1"), CT(0, 32), X("fNF", 0, 1), O.subtract)
             ts(X("fNF", 2, 3), X("fNF", 2, 3), X("fNF", 0, 1), O.add)
     CF = X("fCF")
     ts(CF, X("fNF", 2, 3), X("fNF", 1, 2), O.add, X("fNF", 3, 4), O.add)
     NF1 = X("fNF", 1, 2)
-    ts(blk(X("fHN", 0, 32), 0), blk(X("fCT1"), 0), blk(NF1, 0), O.is_equal, blk(GQ, 0), O.mult)
-    ts(bot(X("fHN", 0, 32)), bot(X("fCT1")), bot(NF1), O.is_equal, bot(GN), O.mult)
-    ts(blk(X("fHN", 0, 32), 1), blk(X("fCT1"), 2), blk(NF1, 2), O.is_equal, blk(ZL, 2), O.mult)
+    for d, a, v in ((0, 0, GN), (3, 0, PC(7)), (2, 2, GN), (1, 2, ZL)):
+        ts(blk(X("fHN", 0, 32), d), blk(X("fCT1"), a), blk(NF1, a), O.is_equal, blk(v, a), O.mult)
     tr(X("fHM", 0, 32), X("fHN", 0, 32))
     total(X("fNL", 4 * me, 4 * me + 1), X("fHM", 0, 32))
     send_scores(3, X("fNL", 4 * me, 4 * me + 1), "fNL")
@@ -684,29 +695,25 @@ def rank_program(g, core, T, topo):
     for b in range(4):
         mm("p%d" % (2 + b), 128, "EQ", 128 * b, "MV", 64, True, False)
 
-    red(X("fG2", 0, 1), ("fNL", 0, 32, 0, 128, 4))
-    DQ, L1g = X("fDQ", 0, 1), X("fDQ", 2, 3)
+    total(X("fG2", 0, 1), ("fNL", 0, 32, 0, 128, 4), X("fJK", 0, 8))
+    D1g, z1, L1g = (X("fDQ", i, i + 1) for i in range(3))
     for d in range(4):
-        cp(blk(DQ, d), blk(X("fG2", 0, 1), 0))
-        cp(blk(L1g, d), blk(X("fG2", 0, 1), 2))
-    ts(X("fUX", 32, 96), X("fTH", 64, 128), DQ, O.is_le, PC(10), O.mult)
-    ts(X("fUX", 0, 32), X("fTH", 0, 32), DQ, O.is_le)
-    ts(X("fUX", 96, 128), X("fTH", 32, 64), DQ, O.is_le)
-    tr(X("fUT"), X("fUX"))
-    sums(X("fUS"), X("fUT"), 64)
-    for h in range(2):
-        ts(X("UOo", h, h + 1), X("fUS", 64 * h + 63, 64 * h + 64), PC(11 + h), O.add)
+        for v, a in ((L1g, 2), (D1g, 0), (z1, 1)):
+            cp(blk(v, d), blk(X("fG2", 0, 1), a))
+    ts(b3(X("fUX")), b3(X("fTH", 0, 64)), b3(X("fG2", 0, 1)), O.mult, 17.5 / 32, O.add)
+    tr(b3(X("fUT")), b3(X("fUX")))
+    us = sums(b3(X("fUS")), b3(X("fUT")), 32)
+    for d in range(4):
+        cp(blk(X("UOo"), d), us)
     pick("MV", 32, 32, "UO", 0, 36, ("UOo", 0))
-    red(X("fG2", 1, 2), ("fNM", 0, 32, 0, 128, 4))
+    total(X("fG2", 1, 2), ("fNM", 0, 32, 0, 128, 4), X("fJK", 8, 16))
     for a in range(4):
         for d in (a, a ^ 1):
             cp(blk(X("fGA", 2 * a, 2 * a + 2), d), blk(X("fG2"), a))
     cp(bot(X("fGA", 0, 4)), top(X("fGA", 0, 4)))
     cp(top(X("fGA", 4, 8)), bot(X("fGA", 4, 8)))
-    _, c2k, z1, c2g, _, o2k, _, o2g = (X("fGA", i, i + 1) for i in range(8))
-    D1g, L2g, H2g = (X("fG4", i, i + 1) for i in range(3))
-    ts(X("fDQ", 1, 2), DQ, 1024.0, O.is_ge, -1024.0, O.mult)
-    ts(D1g, DQ, X("fDQ", 1, 2), O.add)
+    c2k, c2g, o2k, o2g = (X("fGA", i, i + 1) for i in (1, 3, 5, 7))
+    L2g, H2g = (X("fG4", i, i + 1) for i in range(2))
     dma("y", T.sw[0:1, :], ap(blk(D1g, 0)), [blk(D1g, 0)], [])
     dma("y", T.lw[0:1, :], ap(blk(L1g, 0)), [blk(L1g, 0)], [])
     ts(X("fOW", 0, 1), L1g, float(P * me), O.max, float(P * me + P - 1), O.min)
@@ -731,7 +738,8 @@ def rank_program(g, core, T, topo):
     mm("p6", 128, "UQ", 0, "QT", 320)
     tt(X("fSC"), X("p6", 0, 32), X("fIDW"), O.mult)
     red(X("fNK", 4 * me, 4 * me + 1), X("fSC"), O.add, True, True)
-    send1(3, "QT", 320, lambda: send_scores(2, X("fNK", 4 * me, 4 * me + 1), "fNK"))
+    send1(3, "QT", 320)
+    send_scores(2, X("fNK", 4 * me, 4 * me + 1), "fNK")
     if own2:
         pick("MG2", 0, 16 * -(-own2[0][2] // 16), "LD2", 0, 8 * own2[0][2], ("Mo", 2))
     send2(2)
@@ -750,7 +758,8 @@ def rank_program(g, core, T, topo):
         t, u, o = "fMT" + w, "fMU" + w, O.is_gt if w else O.is_ge
         ts(X(t, 0, 32), X("fMG" + w, 32, 64), 1.0, O.add, bk, O.mult)
         ts(X(t, 32, 64), X("fMK" + w), bk, o)
-        tr(X(u), X(t, 0, 64))
+        for c0, c1 in ((0, 64),) if w else ((0, 32), (32, 64)):
+            tr(X(u, c0, c1), X(t, c0, c1))
         ts(X(t, 64, 96), X(u, 0, 32), bk, o)
         total(X("fML" + w, 0, 1), X(u, 32, 64))
         total(X("fML" + w, 1, 2), X(t, 32, 96))
@@ -769,6 +778,10 @@ def rank_program(g, core, T, topo):
             return sums(X("fMJ" + w), X(ht, at, at + n), 64)
         total(out, X(ht, at, at + n))
 
+    def match(out, tmp, t, x, v, nv):
+        act(tmp, t, AF.Abs, x, -1.0)
+        act(out, tmp, AF.Relu, v, nv)
+
     def final(i):
         tr(X("fFT%d" % i), X("fFH%d" % i))
         tt(X("fFL"), sums(X("fFS%d" % i), X("fFT%d" % i), 32), X("fFL") if i else X("fJB"), O.max)
@@ -783,9 +796,9 @@ def rank_program(g, core, T, topo):
     for v, t, b in ((G1, L1g, D1g), (VA, o2g, a128), (VB, L1g, a192)):
         cp(top(v), top(t))
         cp(bot(v), bot(b))
-    ts(X("fFH0"), X("fPT"), G1, O.is_equal, a320, O.mult)
+    match(X("fFH0"), X("fFS1"), X("fPT"), G1, a320, n320)
     final(0)
-    ts(bot(X("fFH2")), bot(X("fPT")), bot(H2g), O.is_equal)
+    match(bot(X("fFH2")), bot(X("fFT1")), bot(X("fPT")), bot(H2g), 1.0, -1.0)
     pick("MV", 0, 32, "DW", 96, 192, ("B2o", 0))
     for b in range(4):
         mm("p%d" % (2 + b), 128, "EQ", 128 * b, "MV", 0)
@@ -806,21 +819,19 @@ def rank_program(g, core, T, topo):
     times(bot(X("fFH1")), bot(X("fFH2")), bot(L2g))
     final(1)
     for h in (top, bot):
-        cp(h(X("FLo", 0, 6)), top(X("fFL")))
-    pick("LF", 0, 128, "QT", 0, 576, ("FLo", 0))
+        cp(h(X("FLo")), top(X("fFL")))
+    pick("LF", 32, 96, "QT", 0, 576, ("FLo", 0))
     mm("p7", 128, "WQ", 0, "LF", 0)
-    dma("y", T.oc[:, 0:384], _view(T, "LF", 0, 96), [X("LF", 0, 96)], [])
-    for k in range(4):
-        dma("y", T.osc[4 * k:4 * k + 4, 0:96], T.LFs[32 * k:32 * k + 4, 0:96], [X("LFs", 0, 96)], [])
-    cp(X("fY"), X("p7", 0, 96))
+    cp(X("fY"), X("p7", 32, 128))
     dma("a", T.y[:], T.fY[:], [X("fY")], [])
-    dma("a", T.lw[1:2, :], ap(blk(L2g, 0)), [blk(L2g, 0)], [])
+    dma("y", T.lw[1:2, :], ap(blk(L2g, 0)), [blk(L2g, 0)], [])
     for h in (top, bot):
         cp(h(X("FDo")), bot(X("fFL")))
-    pick("DF", 0, 96, "DW", 0, 224, ("FDo", 0))
-    dma("y", T.oc[:, 384:768], _view(T, "DF", 0, 96), [X("DF", 0, 96)], [])
+    pick("LF", 128, 96, "DW", 0, 224, ("FDo", 0))
+    for h in range(2):
+        dma("y", T.oc[:, 384 * h:384 * h + 384], _view(T, "LF", 32 + 96 * h, 128 + 96 * h), [X("LF", 32 + 96 * h, 128 + 96 * h)], [])
     for k in range(4):
-        dma("a" if k % 2 else "y", T.osc[4 * k:4 * k + 4, 96:192], T.DFs[32 * k:32 * k + 4, 0:96], [X("DFs", 0, 96)], [])
+        dma("y", T.osc[4 * k:4 * k + 4, :], T.LFs[32 * k:32 * k + 4, 32:224], [X("LFs", 32, 224)], [])
     schedule()
     cnt["ls"] = ls[0]
     for s in sorted(cnt):

import numpy as np
from concourse.bass import DstId, RemoteDMATransfer
from concourse.mybir import dt, AluOpType, AxisListType, ActivationFunctionType

O = AluOpType
AF = ActivationFunctionType
P = 96
F32, BF, I32, U16 = "float32", "bfloat16", "int32", "uint16"
SCRATCH = {}
for _n, _w in {"BT": 1280, "WT": 512, "UZ": 8, "UT": 512, "ZT": 512, "ONB": 128, "HAF": 128, "DG": 128, "ET": 1056, "NT": 512, "HT": 512, "HU": 512,
               "MT": 528, "SG": 384, "MK": 128, "fTG": 128, "fTG2": 128, "fTG3": 128, "R32": 192, "R64": 128}.items():
    SCRATCH[_n] = ("sbuf", [128, _w], BF)
for _n, _w in {"PJ": 6, "MI": 4}.items():
    SCRATCH[_n] = ("sbuf", [128, _w], I32)
for _n, _w in {"LO": 4, "Mo": 4, "O1o": 2, "UOo": 2, "X2o": 6, "B2o": 2, "N2o": 2, "FLo": 6, "FDo": 6}.items():
    SCRATCH[_n] = ("sbuf", [128, _w], U16)
for _n, _w in {"QT": 576, "UQ": 128, "ZQ": 128, "EQ": 512, "WQ": 128, "HQ": 128, "HQ2": 128, "HQ3": 128, "MQ": 132, "SL1": 32, "LD1": 128, "MG1": 32,
               "UO": 36, "SL2": 96, "LD2": 160, "MG2": 32, "LD3": 96, "MG3": 16, "DW": 224, "MV": 192, "LF": 224,
               "RC1": 16, "RC2": 48, "RC3": 16, "RW1": 18, "RW2": 20, "RW3": 12}.items():
    SCRATCH[_n] = ("sbuf", [128, _w], "float8_e4m3fn_x4")
    SCRATCH[_n + "s"] = ("sbuf", [128, _w], "uint8")
for _n, _w in {"SL1s": 96, "RC1s": 64}.items():
    SCRATCH[_n] = ("sbuf", [128, _w], "uint8")
for _n, _w in {"RS1": 1, "RS2": 1, "RS3": 1, "RS4": 1, "SD": 32, "NL": 32, "NM": 32, "NK": 36, "Y": 96, "KT": 32}.items():
    SCRATCH["f" + _n] = ("sbuf", [128, _w], F32)
_V = {"UZ": 8, "PC": 16, "AD": 128, "AL": 96, "CD": 4, "CC": 192, "RK": 4, "OA": 128, "OC": 128, "DN": 384, "DB": 128}
_F = {"ON": 32, "ROW": 192, "R32": 32, "PT": 192, "JB": 6, "KR": 128, "PR": 128, "ZA": 128, "ZR": 128, "RO": 32, "GZ": 64, "GT": 64, "GV": 4,
      "CT": 64, "CTX": 128, "CT1": 32, "TH": 128, "RP": 96, "ID": 32, "SWA": 8, "CW": 256, "CV": 256, "CX": 256, "CY": 256, "NF": 4, "CF": 1,
      "HN": 96, "HM": 96, "H2": 128, "H2t": 128, "H2s": 128, "XT": 4, "XU": 4, "G2": 2, "DQ": 4, "GA": 8, "UX": 64, "UT": 64, "US": 64,
      "OW": 2, "IDW": 32, "MM": 160, "MW": 160, "MX": 160, "OM": 8, "SC": 32, "NB": 1, "JK": 16, "FM": 8, "G4": 4, "G5": 4, "FL": 6,
      "FH0": 192, "FH1": 192, "FH2": 192, "FT0": 192, "FT1": 192, "FS0": 192, "FS1": 192}
for _n, _w in (("ME", 64), ("MR", 32), ("MG", 64), ("MK", 32), ("MT", 96), ("MU", 64), ("ML", 4), ("MH", 192), ("MI", 192), ("MJ", 128)):
    _F[_n] = _F[_n + "b"] = _w
_AT = {}
for _b, _d in (("fV", _V), ("fW", _F)):
    _o = 0
    for _n, _w in _d.items():
        _AT["f" + _n] = (_b, _o, _w)
        _o += -(-_w // 32) * 32
    SCRATCH[_b] = ("sbuf", [128, _o], F32)
for _i in range(8):
    SCRATCH["p%d" % _i] = ("psum", [128, 512], F32)
SEMAPHORES = ["vs", "ac", "te", "gp", "ls"] + [_s + str(_k) for _k in (1, 2, 3, 4) for _s in ("sa", "sn", "sr")]
for _x in (1, 2, 3):
    SEMAPHORES += ["a%d" % _x, "b%d" % _x, "qc%d" % _x, "qs%d" % _x, "wc%d" % _x, "ws%d" % _x]
SEMAPHORES += ["d%d" % _i for _i in range(60)]
WAKE, PIPE, CYCLE, QUIET, GAP, BIAS = 0.1, 0.06, 0.00083, 1.8, 0.05, 0.05
LATE = {"n1": 2.0, "s1": 4.0, "a1": 4.2, "b1": 3.03, "n3": 1.9, "s3": 2.0, "n4": 1.9, "s4": 2.1, "n2": 2.14, "s2": 3.5, "a2": 3.2, "b2": 3.1,
        "a3": 3.7, "b3": 3.45, "small": 1.5, "big": 1.6, "dma": 2.0, "c0": 1.5, "c1": 0.3, "c2": 0.7, "c3": 0.3, "c": 0.1}
WHEN = {"sn1": [9.6, 9.8, 10.1, 10.1], "sa1": [11.9, 12.1, 12.1, 12.4], "a1": [11.6, 0.0, 0.0, 0.0], "b1": [17.8, 18.1, 17.9, 18.3],
        "sn3": [15.4, 15.6, 15.9, 15.8], "sa3": [16.8, 16.9, 16.9, 17.2], "sn4": [16.8, 18.1, 18.4, 18.6], "sa4": [18.6, 18.9, 18.9, 19.1],
        "a2": [0.0, 20.9, 20.4, 20.6], "sn2": [22.5, 22.8, 23.0, 22.9], "sa2": [23.8, 24.0, 24.1, 24.4], "b2": [25.1, 25.4, 25.4, 25.5],
        "a3": [23.8, 23.4, 0.0, 0.0], "b3": [27.4, 27.5, 27.6, 27.9]}
SHARE = {1: (16, 0, 0, 0), 2: (0, 8, 20, 20), 3: (4, 12, 0, 0)}
HALF = {_x: sum(_v) for _x, _v in SHARE.items()}
LAND = {1: ("UO", 0), 2: ("DW", 96), 3: ("DW", 192)}
PAIR = {1: (1, 2), 2: (0, 3), 3: (1, 2)}
OTHER = {1: (0, 3), 2: (1, 2), 3: (0, 3)}


def _layout(T, topo):
    ranks = T.cores
    a = [r for r in range(8) if r == 0 or topo.same_plane(ranks[0], ranks[r])]
    b = [r for r in range(8) if r not in a]
    return a, b


def _owners(x, order, step=1):
    out, at = [], 0
    for pl in (order[:4], order[4:]):
        for r, n in zip(pl, SHARE[x]):
            if n:
                n += 2 * (x == 1 and step == 2)
                out.append((r, at, n))
                at += n
    return out


def _helpers(home, far, topo):
    h = [c for c in topo.cores_of(home) if c != home and topo.may_write(c, far)]
    return sorted(h, key=lambda c: (topo.die(c) != topo.die(home), c))


def _remote(g, T, topo, core, moves):
    tr = []
    for src, dsts, eng, sem in moves:
        ids = []
        for c, _ in dsts:
            rid, pid = topo.addr(c, core)
            ids.append(DstId(rid=rid, pnc=pid))
        m = 0
        for e in eng:
            m |= 1 << e
        tr.append(RemoteDMATransfer(dst_ids=ids, dma_engine_mask=m, remote_sem=T.sem[sem], srcs=[src], dsts=[d for _, d in dsts]))
    g.remote_dma_fused(tr, local_sem=T.sem.ls)
    return sum(len(mv[2]) for mv in moves)


def _view(T, name, a, b, codes=True):
    return T[name][:, a:b].bitcast(dt.uint8) if codes else T[name + "s"][:, a:b]


def _hand_on(g, core, T, topo, rank, far):
    home = T.cores[rank]
    a, b = _layout(T, topo)
    hs = _helpers(home, T.cores[far[0]], topo)
    if core not in hs:
        return
    me = hs.index(core)
    near = [r for r in (a if rank in a else b) if r != rank]
    eng = topo.engines(core, T.cores[far[0]])
    n_on = len(topo.engines(home, core)) - len(eng)
    codes = me < 2

    def scores(k):
        g.wait_ge(T.sem["sr%d" % k], n_on)
        dst = ("fSD", "fNK", "fNL", "fNM")[k - 1]
        to = far[:len(far) // 2] if me < 2 else far[len(far) // 2:]
        return _remote(g, T, topo, core, [(T["fRS%d" % k][:], [(T.cores[r], T[dst][:, 4 * rank:4 * rank + 1]) for r in to], eng, "sa%d" % k)])

    def first(x, to):
        half = x == 1 or (x == 2 and rank in (a[0], b[0]))
        g.wait_ge(T.sem[("qc%d" if codes else "qs%d") % x], n_on // 2 if half else n_on)
        n = 0
        for r, s0, w in sorted(_owners(x, a + b), key=lambda o: -o[2]):
            if r in to:
                s0 %= HALF[x]
                n += _remote(g, T, topo, core, [(_view(T, "RC%d" % x, s0, s0 + w, codes), [(T.cores[r], _view(T, "LD%d" % x, w * rank, w * rank + w, codes))], eng, "a%d" % x)])
        return n

    def second(x):
        nm, base = LAND[x]
        h = 0 if me in PAIR[x] else 1
        to = far[2 * h:2 * h + 2] + (near[h:h + 1] if codes else [])
        for r, s0, n in _owners(x, a + b, 2):
            if r == rank:
                g.wait_ge(T.sem[("wc%d" if codes else "ws%d") % x], n_on)
                return _remote(g, T, topo, core, [(_view(T, "RW%d" % x, 0, n, codes), [(T.cores[r], _view(T, nm, base + s0, base + s0 + n, codes)) for r in to], eng, "b%d" % x)])
        return 0

    if me in PAIR[1]:
        ls = first(1, far) + second(1) + first(2, near) + first(3, far) + second(2) + second(3)
    else:
        ls = scores(1) + scores(3) + second(1) + scores(4) + first(2, far) + first(3, near) + scores(2) + second(2) + second(3)
    g.wait_ge(T.sem.ls, ls)


def rank_program(g, core, T, topo):
    rank = T.rank_of(core)
    pa, pb = _layout(T, topo)
    if rank is None:
        for r in range(8):
            if core in topo.cores_of(T.cores[r]):
                _hand_on(g, core, T, topo, r, pb if r in pa else pa)
        return
    far = pb if rank in pa else pa
    near = [r for r in (pa if rank in pa else pb) if r != rank]
    order = pa + pb
    m = order.index(rank)
    hs = _helpers(core, T.cores[far[0]], topo)
    e_off = topo.engines(core, T.cores[near[0]])
    e_on = [e for e in topo.engines(core, hs[0]) if e not in e_off]
    e_a, e_b = e_on[:len(e_on) // 2], e_on[len(e_on) // 2:]
    me = rank

    Q = {"v": g.vector, "a": g.scalar, "t": g.tensor, "g": g, "y": g.sync}
    SEM = {"v": "vs", "a": "ac", "t": "te", "g": "gp"}
    acc, waited, know, cnt = {}, {q: {} for q in Q}, {}, {}
    nd, ls, sent = [0], [0], []

    def X(name, c0=0, c1=None, r0=0, r1=128, st=1):
        b, o, w = _AT[name] if name in _AT else (name, 0, SCRATCH[name][1][1])
        return (b, o + c0, o + (w if c1 is None else c1), r0, r1, st)

    def ap(v):
        n, c0, c1, r0, r1, st = v
        if (r0, r1) == (0, 128):
            return T[n][:, c0:c1] if st == 1 else T[n][:, c0:c1:st]
        return T[n][r0:r1, c0:c1] if st == 1 else T[n][r0:r1, c0:c1:st]

    def rows(v, r0, r1):
        return (v[0], v[1], v[2], r0, r1, v[5])

    def blk(v, a):
        return rows(v, 32 * a, 32 * a + 32)

    def top(v):
        return rows(v, 0, 64)

    def bot(v):
        return rows(v, 64, 128)

    def width(v):
        return -(-(v[2] - v[1]) // v[5])

    def hit(a, b):
        if a[4] <= b[3] or b[4] <= a[3] or a[2] <= b[1] or b[2] <= a[1]:
            return False
        return not (a[5] == b[5] > 1 and (a[1] - b[1]) % a[5])

    def norm(v):
        return (v[0], 0, 512, 0, 128, 1) if SCRATCH[v[0]][0] == "psum" else v

    def enter(book, reads, writes, tag, q):
        for v in writes:
            nv = norm(v)
            book[v[0]] = [e for e in book.get(v[0], []) if not (nv[1] <= e[0][1] and e[0][2] <= nv[2] and nv[3] <= e[0][3] and e[0][4] <= nv[4] and nv[5] == 1)]
            book[v[0]].append((nv, True, tag, q))
        for v in reads:
            book.setdefault(v[0], []).append((norm(v), False, tag, q))

    def pre(q, reads, writes):
        need = {}
        for vs, w in ((reads, False), (writes, True)):
            for v in vs:
                ps = SCRATCH[v[0]][0] == "psum"
                for r, iw, ev, eq in acc.get(v[0], []):
                    if (iw or w or (ps and eq != q)) and hit(r, norm(v)):
                        if ps and q == "t" and eq == "t" and w:
                            continue
                        need[ev[0]] = max(need.get(ev[0], 0), ev[1])
        for s in sorted(need, key=lambda s: (s in ("vs", "ac", "te"), s)):
            if waited[q].get(s, 0) < need[s]:
                Q[q].wait_ge(T.sem[s], need[s])
                for s2, n2 in know.get((s, need[s]), {}).items():
                    waited[q][s2] = max(waited[q].get(s2, 0), n2)
                waited[q][s] = need[s]

    def post(q, reads, writes, ev):
        know[ev] = dict(waited[q])
        enter(acc, reads, writes, ev, q)

    nodes, seen, fill, floor = [], {}, set(), {}

    def note(ways, reads, writes, after=(), late=0.0):
        k = len(nodes)
        pr = set(after)
        q0 = list(ways)[0] if len(ways) == 1 else ""
        for vs, w in ((reads, False), (writes, True)):
            for v in vs:
                ps = SCRATCH[v[0]][0] == "psum"
                for r, iw, i, q in seen.get(v[0], []):
                    if i != k and (iw or w or (ps and (q != q0 or not q))) and hit(r, norm(v)):
                        pr.add(i)
        enter(seen, reads, writes, k, q0)
        nodes.append((ways, pr, late))
        return k

    def schedule():
        n = len(nodes)
        succ = [[] for _ in range(n)]
        for k, (_, pr, _) in enumerate(nodes):
            for p in pr:
                succ[p].append(k)
        dur = [min(c for _, c in w.values()) + late for w, _, late in nodes]
        path = [0.0] * n
        for k in range(n - 1, -1, -1):
            path[k] = dur[k] + max([path[x] + WAKE for x in succ[k]], default=0.0)
        busy, start, done = {q: [] for q in Q}, [None] * n, [0.0] * n
        for k in sorted(range(n), key=lambda k: (-path[k], k)):
            at = max([done[p] + WAKE for p in nodes[k][1]], default=0.0)
            best = None
            for q, (_, c) in nodes[k][0].items():
                t, d = at, c - (PIPE if q in SEM else 0.0)
                keep = []
                if k in fill and q in SEM:
                    keep = [(QUIET if q != "g" else done[sent[0]] - LATE["c0"] - 0.8, done[sent[0]])]
                for b0, b1 in sorted(busy.get(q, []) + keep):
                    if t + d + (GAP if k in fill else 0.0) <= b0:
                        break
                    t = max(t, b1)
                if best is None or t + c < best[0] + nodes[k][0][best[1]][1] + BIAS:
                    best = (t, q, d)
            t, q, d = best
            if q in busy:
                busy[q].append((t, t + d))
            start[k], done[k] = (t, -path[k], k, q), t + nodes[k][0][q][1] + nodes[k][2]
            if floor.get(k):
                done[k] = max(t, floor[k])
        for t, _, k, q in sorted(start):
            nodes[k][0][q][0]()

    def issue_op(q, call, reads, writes):
        pre(q, reads, writes)
        s = SEM[q]
        if q == "g" and waited[q].get(s, 0) < cnt.get(s, 0):
            g.wait_ge(T.sem[s], cnt[s])
            waited[q][s] = cnt[s]
        i = call()
        cnt[s] = cnt.get(s, 0) + 1
        i.then_inc(T.sem[s], 1)
        post(q, reads, writes, (s, cnt[s]))

    def el(n, f=1.0):
        return PIPE + max(64, n * f) * CYCLE

    def op(q, call, reads, writes, cost):
        note({q: (lambda: issue_op(q, call, reads, writes), cost)}, reads, writes)

    def either(v, a, reads, writes, c, more=0.02):
        note({"v": (lambda: issue_op("v", v, reads, writes), c), "a": (lambda: issue_op("a", a, reads, writes), c + more)}, reads, writes)

    def dma(q, out, in_, reads=(), writes=(), late="dma"):
        def issue():
            pre(q, reads, writes)
            s = "d%d" % nd[0]
            nd[0] += 1
            Q[q].dma_start(out, in_).then_inc(T.sem[s], 16)
            cnt[s] = 16
            post(q, reads, writes, (s, 16))
        note({q: (issue, 0.06)}, reads, writes, (), LATE[late])

    def send(moves, reads):
        def issue():
            pre("g", reads, [])
            ls[0] += _remote(g, T, topo, core, moves)
        sent.append(note({"g": (issue, LATE.get("c%d" % len(sent), LATE["c"]))}, reads, [], sent[-1:]))

    def arrive(views, sem, total, late):
        def issue():
            cnt[sem] = total
            for v in views:
                acc.setdefault(v[0], []).append((v, True, (sem, total), "r"))
        floor[note({"r": (issue, 0.0)}, [], views, sent[-1:], late)] = WHEN.get(sem, [0.0] * 4)[m % 4]

    def dcol(q, dst, d0, src, s0, n):
        dma(q, _view(T, dst, d0, d0 + n), _view(T, src, s0, s0 + n), [X(src, s0, s0 + n)], [X(dst, d0, d0 + n)])
        dma(q, T[dst + "s"][:, d0:d0 + n], T[src + "s"][:, s0:s0 + n], [X(src + "s", s0, s0 + n)], [X(dst + "s", d0, d0 + n)])

    def sc(s):
        return (ap(s), [s]) if isinstance(s, tuple) else (s, [])

    def ts(out, a, s1, op0, s2=None, op1=None):
        p1, r1 = sc(s1)
        p2, r2 = sc(s2)
        kinds = SCRATCH[out[0]][2], SCRATCH[a[0]][2]
        args = (p1, None, op0) if op1 is None else (p1, p2, op0, op1)
        v = lambda: g.vector.tensor_scalar(ap(out), ap(a), *args)
        other = None
        if kinds == (F32, F32):
            if op1 is None and op0 == O.add:
                other = {"bias": p1}
            elif op0 == O.mult and op1 == O.add:
                other = {"bias": p2, "scale": p1}
            elif op0 == O.add and s1 == 1.0 and op1 == O.mult:
                other = {"bias": p2, "scale": p2}
        if other:
            either(v, lambda: g.scalar.activation(ap(out), ap(a), AF.Identity, **other), [a] + r1 + r2, [out], el(width(out)))
        else:
            op("v", v, [a] + r1 + r2, [out], el(width(out), 0.5 if kinds == (BF, BF) and op1 is not None else 1.0))

    def tt(out, a, b, o):
        op("v", lambda: g.vector.tensor_tensor(ap(out), ap(a), ap(b), o), [a, b], [out], el(width(out), 2.0))

    def cp(out, a):
        v = lambda: g.vector.tensor_copy(ap(out), ap(a))
        if SCRATCH[out[0]][2] in (F32, BF) and SCRATCH[a[0]][2] in (F32, BF):
            either(v, lambda: g.scalar.activation(ap(out), ap(a), AF.Copy), [a], [out], el(width(out)))
        else:
            op("v", v, [a], [out], el(width(out)))

    def times(out, a, col):
        either(lambda: g.vector.tensor_scalar(ap(out), ap(a), ap(col), None, O.mult), lambda: g.scalar.activation(ap(out), ap(a), AF.Copy, scale=ap(col)), [a, col], [out], el(width(out)))

    def red(out, a, o=O.add, neg=False, ab=False):
        op("v", lambda: g.vector.tensor_reduce(ap(out), ap(a), AxisListType.X, o, negate=neg, apply_absolute_value=ab), [a], [out], el(width(a)))

    def total(out, a, b=None):
        b = b or a
        either(lambda: g.vector.tensor_reduce(ap(out), ap(a), AxisListType.X, O.add),
               lambda: g.scalar.activation(ap(b), ap(a), AF.Copy, accum_out=ap(out)), [a], [b, out], el(width(a)))

    def sums(out, a, n):
        r = X("R%d" % n, 0, width(a), a[3], a[4])
        op("v", lambda: g.vector.tensor_tensor_scan(ap(out), ap(r), ap(a), 0.0, O.mult, O.add), [r, a], [out], el(width(a)))
        return (out[0], out[1] + n - 1, out[2], out[3], out[4], n)

    def tr(out, a):
        op("v", lambda: g.vector.transpose(ap(out), ap(a)), [a], [out], el(width(a)))

    def ms(out, c):
        op("v", lambda: g.vector.memset(ap(out), c), [], [out], el(width(out), 0.5 if SCRATCH[out[0]][2] == BF else 1.0))

    def zero(out):
        src, n = X("MT", 32, 32 + width(out)), width(out)
        either(lambda: g.vector.memset(ap(out), 0.0), lambda: g.scalar.activation(ap(out), ap(src), AF.Copy), [src], [out], el(n, 0.5), el(n) - el(n, 0.5) + 0.02)

    def act(out, a, func, bias=None, scale=1.0):
        if bias is None:
            op("a", lambda: g.scalar.activation(ap(out), ap(a), func), [a], [out], el(width(out)) + 0.02)
        else:
            op("a", lambda: g.scalar.activation(ap(out), ap(a), func, bias=sc(bias)[0], scale=sc(scale)[0]), [a] + sc(bias)[1] + sc(scale)[1], [out], el(width(out)) + 0.02)

    def iota(out, pat, base, cm=0):
        kw = {} if SCRATCH[out[0]][2] == I32 else {"allow_small_or_imprecise_dtypes": True}
        op("g", lambda: g.iota(ap(out), pat, base, cm, **kw), [], [out], 0.3 + 2 * CYCLE * width(out))

    def quant(dst, d0, d1, src, s0, s1):
        op("v", lambda: g.vector.quantize_mx(T[dst][:, d0:d1], T[dst + "s"][:, d0:d1], T[src][:, s0:s1]), [X(src, s0, s1)], [X(dst, d0, d1), X(dst + "s", d0, d1)], 0.07 + 0.00022 * (s1 - s0))

    def mm(bank, n, l, l0, r, r0, start=True, stop=True):
        op("t", lambda: g.tensor.matmul_mx(T[bank][:, 0:n], T[l][:, l0:l0 + 128], T[l + "s"][:, l0:l0 + 128], T[r][:, r0:r0 + n], T[r + "s"][:, r0:r0 + n], start, stop),
           [X(l, l0, l0 + 128), X(l + "s", l0, l0 + 128), X(r, r0, r0 + n), X(r + "s", r0, r0 + n)], [X(bank, 0, n)], PIPE + 0.0008 * (n + 16))

    def pick(dst, d0, n, win, a, b, off):
        ov = X(off[0], off[1], off[1] + n // 16)
        op("a", lambda: g.scalar.activation(T[dst + "s"][:, d0:d0 + n], T[win + "s"][:, a:b].indirect(ap(ov)), AF.Copy), [X(win + "s", a, b), ov], [X(dst + "s", d0, d0 + n)], el(40 + 1.5 * n) + 0.02)
        op("v", lambda: g.vector.tensor_copy(T[dst][:, d0:d0 + n].bitcast(dt.uint32), T[win][:, a:b].bitcast(dt.uint32).indirect(ap(ov))), [X(win, a, b), ov], [X(dst, d0, d0 + n)], el(40 + 1.5 * n))

    def gather(out, win, ov):
        either(lambda: g.vector.tensor_copy(ap(out), ap(win).indirect(ap(ov))), lambda: g.scalar.activation(ap(out), ap(win).indirect(ap(ov)), AF.Copy),
               [win, ov], [out], el(40 + 1.5 * width(out)))

    def send1(x, src, s0, between=lambda: None):
        own, w = _owners(x, order), HALF[x]
        p, p2 = (s0 + w, s0) if me in pa else (s0, s0 + w)
        if x == 1:
            send([(_view(T, src, p, p + w), [(hs[PAIR[x][0]], _view(T, "RC1", 0, w))], e_a, "qc1"),
                  (_view(T, src, p, p + 4 * w, False), [(hs[PAIR[x][1]], _view(T, "RC1", 0, 4 * w, False))], e_b, "qs1")], [X(src, p, p + w), X(src + "s", p, p + 4 * w)])
        else:
            ea, eb = (e_a, e_b) if x == 2 and me in e1 else (e_on, e_off)
            for h, k in enumerate(("qc%d" % x, "qs%d" % x)):
                send([(_view(T, src, p, p + w, not h), [(hs[PAIR[x][h]], _view(T, "RC%d" % x, 0, w, not h))], ea, k),
                      (_view(T, src, p2, p2 + w, not h), [(hs[OTHER[x][h]], _view(T, "RC%d" % x, 0, w, not h))], eb, k)], [X(src + "s" * h, s0, s0 + 2 * w)])
        between()
        for r, c, n in own:
            if r in near and x == 1:
                for h in range(2):
                    send([(_view(T, src, s0 + c, s0 + c + n, not h), [(T.cores[r], _view(T, "LD%d" % x, n * me, n * me + n, not h))], e_off, "a%d" % x)], [X(src + "s" * h, s0 + c, s0 + c + n)])
            if r == me:
                dcol("y", "LD%d" % x, n * me, src, s0 + c, n)
                oth = [X(k, n * r, n * r + n) for k in ("LD%d" % x, "LD%ds" % x) for r in range(8) if r != me]
                arrive(oth, "a%d" % x, 7 * 2 * len(e_off), LATE["a%d" % x])

    def send2(x):
        own = _owners(x, order, 2)
        nm, base = LAND[x]
        src = "MG%d" % x
        for r, c, n in own:
            if r == me:
                for h, k in enumerate(("wc%d" % x, "ws%d" % x)):
                    sap, hap = _view(T, src, 0, n, not h), _view(T, "RW%d" % x, 0, n, not h)
                    send([(sap, [(hs[PAIR[x][h]], hap)], e_on, k), (sap, [(hs[OTHER[x][h]], hap)], e_off, k)], [X(src + "s" * h, 0, n)])
                for h in (1, 0):
                    send([(_view(T, src, 0, n, not h), [(T.cores[r], _view(T, nm, base + c, base + c + n, not h)) for r in (near if h else near[2:])], e_off, "b%d" % x)], [X(src + "s" * h, 0, n)])
                dcol("y", nm, base + c, src, 0, n)
        oth = [(base + c, n) for r, c, n in own if r != me]
        arrive([X(k, c, c + n) for k in (nm, nm + "s") for c, n in oth], "b%d" % x, len(oth) * 2 * len(e_off), LATE["b%d" % x])

    def send_scores(k, src, dst):
        fm = (ap(src), [(hs[h], T["fRS%d" % k][:]) for h in PAIR[2]], e_on, "sr%d" % k)
        nm = (ap(src), [(T.cores[r], T[dst][:, 4 * me:4 * me + 1]) for r in near], e_off, "sn%d" % k)
        for mv in ([fm], [nm]) if k == 1 else ([fm, nm],):
            send(mv, [src])
        arrive([X(dst, 4 * r, 4 * r + 1) for r in near], "sn%d" % k, len(near) * len(e_off), LATE["n%d" % k])
        arrive([X(dst, 4 * r, 4 * r + 1) for r in far], "sa%d" % k, len(far) * len(e_off), LATE["s%d" % k])

    def load(q, buf, c0, c1, ext, late):
        dma(q, T[buf][:, c0:c1], ext, [], [X(buf, c0, c1)], late)

    load("y", "UZ", 4, 8, T.z[:, 0:4], "small")
    load("a", "UZ", 0, 4, T.u[:, 0:4], "small")
    load("y", "BT", 384, 768, T.dm[:], "big")
    load("a", "BT", 0, 384, T.lv[:], "big")
    load("y", "BT", 768, 1152, T.nz[:], "big")
    load("a", "WT", 0, 512, T.w[:], "big")
    e1 = [o[0] for o in _owners(1, order)]
    own2, own3 = ([o for o in _owners(x, order) if o[0] == me] for x in (2, 3))
    cl = m % 2
    iota(X("PJ", 5, 6), [[1, 1]], 0, 1)
    iota(X("fTG", 0, 64), [[32, 2], [0, 2], [1, 16]], 0)
    iota(X("fTG2"), [[0, 8], [2, 16]], 0)
    iota(top(X("fPR")), [[1, 128]], P * me - 32)
    iota(bot(X("fPR")), [[1, 128]], P * me)
    ms(X("ONB"), 1.0)
    ms(X("HAF"), 0.5)
    op("g", lambda: g.affine_select(T.MK[:], T.HAF[:], [[1, 128]], O.is_ge, -0.5, 0, -1), [X("HAF")], [X("MK")], 0.55)
    for i, k in enumerate((31, 15, 3, 1, 63)):
        if i != 2:
            op("v", lambda k=k, i=i: g.vector.tensor_scalar(T.PJ[:, i:i + 1], T.PJ[:, 5:6], k, None, O.bitwise_and), [X("PJ", 5, 6)], [X("PJ", i, i + 1)], el(1))
    cp(X("fPC", 0, 2), X("PJ", 0, 2))
    cp(X("fPC", 3, 6), X("PJ", 3, 6))
    PC = lambda i: X("fPC", i, i + 1)
    P32, P16, _, PAR, LC, PF = (PC(i) for i in range(6))
    cp(X("fTG", 64, 128), X("fTG", 0, 64))
    ms(blk(X("fTG", 0, 64), 0), -1000.0)
    ms(blk(X("fTG", 64, 128), 3), -1000.0)
    ms(blk(X("fTG2"), 0), -1000.0)
    ms(X("MT"), 0.0)
    ts(PC(6), PF, P16, O.subtract)
    times(X("MT", 0, 16, 0, 128, 5), X("ONB", 0, 4), PC(6))
    times(X("MT", 16, 32, 0, 128, 5), X("ONB", 0, 4), P16)
    quant("MQ", 0, 132, "MT", 0, 528)
    for h in ("HT", "HU"):
        for t in (2, 3):
            ms(X(h, t, 512, 0, 128, 4), 0.0)
    ms(top(X("fKR", 0, 32)), 0.0)
    ms(bot(X("fKR", 96, 128)), 0.0)
    cp(X("fUZ", 0, 4), X("UZ", 0, 4))
    for t in range(4):
        ts(X("ZT", t, 512, 0, 128, 4), X("ONB"), X("UZ", 4 + t, 5 + t), O.mult)
        times(X("UT", t, 512, 0, 128, 4), X("ONB"), X("fUZ", t, t + 1))
    quant("ZQ", 0, 128, "ZT", 0, 512)
    quant("UQ", 0, 128, "UT", 0, 512)
    quant("QT", 0, 192, "BT", 0, 768)

    def ahead(i, row, col, sign, c0, n, out):
        red(X("fCD", i, i + 1), X(col, 0, 1), O.add, sign > 0, True)
        s = X("SG", 128 * i, 128 * i + n)
        act(s, row, AF.Sign, X("fCD", i, i + 1), float(sign))
        tt(out, s, X("MK", c0, c0 + n), O.is_gt)
        total(X("fRK", i, i + 1), out)

    def places(q, h, bank, out, c0):
        quant(q, 0, 128, h, 0, 512)
        mm(bank, 128, q, 0, "MQ", 0)
        for t in range(2):
            ts(X(out, c0 + t, c0 + t + 1), X(bank, t, t + 1), X(bank, 4 + t, 5 + t), O.add)

    mm("p0", 128, "ZQ", 0, "QT", 64)
    mm("p1", 128, "QT", 64, "ZQ", 0)
    mm("p6", 128, "UQ", 0, "QT", 0)
    mm("p7", 128, "QT", 0, "UQ", 0)
    mm("p2", 128, "ZQ", 0, "QT", 0)
    act(X("fAD", 32, 128), X("p0", 32, 128), AF.Abs)
    act(X("fAL"), X("p6", 0, 96), AF.Abs)
    ahead(0, X("fAD", 32, 128), "p1", 1, 32, 96, X("fCC", 0, 96))
    for t in range(2):
        ts(X("HU", t, 512, 0, 128, 4), X("fTG2"), X("fRK", 0, 1), O.subtract, -float((t - cl) % 2), O.is_equal)
    places("HQ3", "HU", "p3", "LO", 2)
    ahead(1, X("fAL"), "p7", -1, 0, 96, X("fCC", 96, 192))
    for t in range(2):
        ts(X("HT", t, 256, 0, 128, 4), X("fTG", 0, 64), X("fRK", 0, 1), O.subtract, -16.0 * t, O.is_equal)
        ts(X("HT", 256 + t, 512, 0, 128, 4), X("fTG", 64, 128), X("fRK", 1, 2), O.subtract, -16.0 * t, O.is_equal)
    places("HQ", "HT", "p1", "LO", 0)
    low = 2.0 ** -110
    ts(top(X("fKR", 32, 128)), top(X("fAD", 32, 128)), low, O.max)
    ts(bot(X("fKR", 0, 96)), bot(X("fAL")), -1.0, O.mult, -low, O.min)
    gather(X("fRO"), X("fKR"), X("LO", 0, 2))
    tr(X("fKT"), X("fRO"))
    KEY = X("fKT", 0, 1)
    dma("y", T.SL1s[:, 32:96], T.QTs[:, 0:64], [X("QTs", 0, 64)], [X("SL1s", 32, 96)], "small")
    pick("SL1", 0, 32, "QT", 64, 192, ("LO", 2))
    send1(1, "SL1", 0, lambda: send_scores(1, KEY, "fSD"))
    cp(X("fSD", 4 * me, 4 * me + 1), KEY)
    act(X("fZA"), X("p2", 0, 128), AF.Abs)
    ts(X("fZR"), X("fZA"), low, O.max)
    gather(X("fGZ", 0, 32), X("fPR"), X("LO", 0, 2))
    gather(X("fGZ", 32, 64), X("fZR"), X("LO", 0, 2))
    tr(X("fGT"), X("fGZ"))
    GN, ZL = X("fGT", 0, 1), X("fGT", 32, 33)

    f0 = len(nodes)
    iota(X("fROW"), [[16, 6], [0, 2], [1, 16]], 0)
    iota(X("fR32"), [[1, 32]], 0)
    iota(X("fJB"), [[16, 6]], 0)
    ms(X("BT", 1152, 1280), 0.0)
    quant("QT", 192, 320, "BT", 768, 1280)
    ms(X("fON"), 1.0)
    for n in (32, 64):
        ms(X("R%d" % n), 1.0)
        ms(X("R%d" % n, 0, None, 0, 128, n), 0.0)
    CT = lambda a, b: X("fCT", a, b)
    ts(CT(0, 32), X("fR32"), LC, O.subtract)
    ts(CT(32, 64), CT(0, 32), 32.0, O.add)
    ms(top(X("fCTX", 64, 128)), -1000.0)
    ts(top(X("fCTX", 0, 64)), top(X("fROW", 0, 64)), top(LC), O.subtract, 32.0, O.add)
    ts(bot(X("fCTX")), bot(X("fROW", 0, 128)), bot(LC), O.subtract)
    cols, parts = [], []
    for own, col in ((own3, 0), (own2, 2)):
        for _, s0, n in own:
            for c in range(-(-n // 16)):
                lo = s0 + 16 * c
                for lst in sorted({lo // 32, (min(lo + 16, s0 + n) - 1) // 32}):
                    at = 32 * len(parts)
                    ts(X("fMM", at, at + 32), X("fROW", 0, 32), float(lo - 32 * lst), O.add, P32, O.is_equal)
                    for h in (0, 16):
                        if s0 + n - lo < 16:
                            ms(X("fMM", at + h + s0 + n - lo, at + h + 16), 0.0)
                    parts.append((len(cols), lst))
                cols.append((n, col + c))
    ts(PC(14), P16, 16.0, O.add)
    if me in e1:
        iota(X("fTG3"), [[0, 8], [1, 16]], 0)
    VO, VK = (X("fGV", i, i + 1) for i in range(2))
    ts(blk(PC(7), 0), blk(PAR, 0), 2.0 - 4.0 * cl, O.mult, 2.0 * cl - 1.0, O.add)
    ts(top(VO), top(GN), float(P - P * me), O.add)
    ts(bot(VO), bot(GN), -float(P * me), O.add)
    ts(PC(8), LC, 32.0, O.is_lt)
    ts(PC(9), LC, 32.0, O.is_ge)
    times(X("fGV", 3, 4), KEY, PC(8))
    ts(VK, GN, PC(9), O.mult, X("fGV", 3, 4), O.add)
    b3 = lambda v: blk(v, 3)
    ts(b3(PC(10)), b3(P32), 0.5, O.mult, 0.5, O.add)
    ts(b3(X("fTH", 0, 64)), b3(X("fROW", 0, 64)), b3(P32), O.is_gt, 0.5, O.mult)
    ts(b3(X("fTH", 64, 128)), b3(X("fROW", 0, 64)), b3(P32), O.is_equal, b3(PC(10)), O.mult)
    tt(b3(X("fTH", 0, 64)), b3(X("fTH", 0, 64)), b3(X("fTH", 64, 128)), O.add)
    ts(PC(13), P32, 32.0, O.add)
    ts(X("fRP", 0, 64), X("fROW", 0, 64), -1.0, O.mult, PC(13), O.add)
    ts(X("fRP", 64, 96), X("fR32"), -1.0, O.mult, PC(13), O.add)
    ts(X("fID"), X("fR32"), P32, O.is_equal)
    ts(X("fPT"), X("fROW"), float(P * me), O.add)
    ts(X("fJB"), X("fJB"), P16, O.add)
    op("g", lambda: g.affine_select(T.DG[:], T.HAF[:], [[-1, 128]], O.is_equal, 0.0, 0, 1), [X("HAF")], [X("DG")], 0.55)
    for i in range(2):
        for j in range(2):
            zero(X("ET", 528 * i + 264 * j, 528 * i + 264 * j + 264))
        cp(X("ET", 528 * i + 2 + i, 528 * i + 514, 0, 128, 4), X("DG"))
        for j in range(2):
            quant("EQ", 128 * (i + 2 * j), 128 * (i + 2 * j) + 128, "ET", 528 * i + 2 - 2 * j, 528 * i + 514 - 2 * j)
    quant("WQ", 0, 128, "WT", 0, 512)
    dcol("y", "LF", 0, "QT", 0, 32)
    zero(X("NT", 128, 320))
    zero(X("NT", 320, 512))
    ms(X("fNK", 32, 33), -low)
    dcol("y", "MV", 96, "QT", 0, 96)
    dcol("y", "DW", 0, "QT", 96, 96)
    for b in range(4):
        mm("p%d" % (2 + b), 128, "EQ", 128 * b, "QT", 192)
        act(X("fDN", 96 * b, 96 * b + 96), X("p%d" % (2 + b), 0, 96), AF.Copy)
    a64, a320, a448, a128, a192, n320 = (X("fFM", i, i + 1) for i in range(6))
    for v, c in ((a64, 64), (top(a320), 320), (bot(a320), 96), (top(a448), 448), (bot(a128), 128), (bot(a192), 192)):
        ts(v, rows(P32, v[3], v[4]), float(c), O.add)
    ts(n320, a320, -1.0, O.mult, 0.0, O.add)
    fill.update(range(f0, len(nodes)))

    def key(s):
        return X("fSD", 4 * s, 4 * s + 1)

    if me in e1:
        mm("p0", 128, "ZQ", 0, "LD1", 0)
        mm("p7", 128, "LD1", 0, "ZQ", 0)
        act(X("fOA"), X("p0", 0, 128), AF.Abs)
        ahead(2, X("fOA"), "p7", 1, 0, 128, X("fOC"))
        for t in range(2):
            if e1.index(me):
                ts(X("HT", t, 512, 0, 128, 4), X("fTG3"), X("fRK", 2, 3), O.subtract, -16.0 * t, O.is_equal)
            else:
                ts(X("HT", t, 512, 0, 128, 4), X("fTG3"), X("fRK", 2, 3), O.add, 17.0 - 16 * t, O.is_equal)
        places("HQ2", "HT", "p1", "O1o", 0)
        pick("MG1", 0, 32, "LD1", 0, 128, ("O1o", 0))

    planes = (pa, pb) if rank in pa else (pb, pa)
    RO = X("fRO")
    for i, grp in enumerate((near, far)):
        n, pl = 32 * len(grp), planes[i]
        below = 2 * sum(s < me for s in grp) > len(grp)
        for a in range(4):
            cp(blk(X("fSWA", 4 * i, 4 * i + 4), a), ("fSD", 4 * pl[0], 4 * pl[-1] + 1, 32 * (a ^ 1), 32 * (a ^ 1) + 32, 4 * (pl[1] - pl[0])))
        for j, s in enumerate(grp):
            w, at = 4 * i + pl.index(s), 128 * i + 32 * j
            for out, kk in ((X("fCW", at, at + 32), key(s)), (X("fCX", at, at + 32), X("fSWA", w, w + 1))):
                args = (O.is_lt if s > me else O.is_le,) + ((O.subtract,) if below else ())
                v = lambda out=out, kk=kk, args=args: g.vector.tensor_scalar(ap(out), ap(RO), ap(kk), 1.0 if len(args) > 1 else None, *args)
                if (s < me) == below:
                    either(v, lambda out=out, kk=kk: g.scalar.activation(ap(out), ap(RO), AF.Sign, bias=ap(kk), scale=-1.0), [RO, kk], [out], el(32))
                else:
                    op("v", v, [RO, kk], [out], el(32))
        for k, (w, v) in enumerate((("fCW", "fCV"), ("fCX", "fCY"))):
            vv, oo = X(v, 128 * i, 128 * i + n), X("fNF", 2 * k + i, 2 * k + i + 1)
            tr(vv, X(w, 128 * i, 128 * i + n))
            f, b = (AF.Sign, 1.0) if below else (AF.Relu, 0.0)
            op("a", lambda vv=vv, oo=oo, f=f, b=b: g.scalar.activation(ap(vv), ap(vv), f, bias=b, accum_out=ap(oo)), [vv], [vv, oo], el(n) + 0.02)
        if i == 0:
            ts(X("fCT1"), CT(0, 32), X("fNF", 0, 1), O.subtract)
            ts(X("fNF", 2, 3), X("fNF", 2, 3), X("fNF", 0, 1), O.add)
    CF = X("fCF")
    ts(CF, X("fNF", 2, 3), X("fNF", 1, 2), O.add, X("fNF", 3, 4), O.add)
    NF1 = X("fNF", 1, 2)
    for d, a, v in ((0, 0, GN), (3, 0, PC(7)), (2, 2, GN), (1, 2, ZL)):
        ts(blk(X("fHN", 0, 32), d), blk(X("fCT1"), a), blk(NF1, a), O.is_equal, blk(v, a), O.mult)
    tr(X("fHM", 0, 32), X("fHN", 0, 32))
    total(X("fNL", 4 * me, 4 * me + 1), X("fHM", 0, 32))
    send_scores(3, X("fNL", 4 * me, 4 * me + 1), "fNL")
    send2(1)
    ts(X("fHN", 32, 64), CT(32, 64), CF, O.is_equal, VK, O.mult)
    for a in range(4):
        ts(blk(X("fHN", 64, 96), a), blk(CT(32, 64), a ^ 1), blk(CF, a ^ 1), O.is_equal, blk(GN if a % 2 else KEY, a ^ 1), O.mult)
    tr(X("fHM", 32, 96), X("fHN", 32, 96))
    total(X("fNM", 4 * me, 4 * me + 1), X("fHM", 32, 96))
    send_scores(4, X("fNM", 4 * me, 4 * me + 1), "fNM")

    ts(X("fH2"), X("fCTX"), CF, O.is_equal, VO, O.mult)
    tr(X("fH2t"), X("fH2"))
    s4 = sums(X("fH2s"), X("fH2t"), 32)
    for a in range(4):
        cp(blk(X("fXT"), a), blk(s4, a ^ 1))
    tt(X("fXU"), s4, X("fXT"), O.add)
    for h in (top, bot):
        cp(h(X("X2o", 0, 4)), bot(X("fXU")))
        cp(h(X("X2o", 4, 6)), top(X("fXU", 0, 2)))
    pick("SL2", 0, 96, "QT", 0, 192, ("X2o", 0))
    send1(2, "SL2", 0)
    pick("MV", 64, 32, "QT", 192, 288, ("X2o", 0))
    for b in range(4):
        mm("p%d" % (2 + b), 128, "EQ", 128 * b, "MV", 64, True, False)

    total(X("fG2", 0, 1), ("fNL", 0, 32, 0, 128, 4), X("fJK", 0, 8))
    D1g, z1, L1g = (X("fDQ", i, i + 1) for i in range(3))
    for d in range(4):
        for v, a in ((L1g, 2), (D1g, 0), (z1, 1)):
            cp(blk(v, d), blk(X("fG2", 0, 1), a))
    ts(b3(X("fUX")), b3(X("fTH", 0, 64)), b3(X("fG2", 0, 1)), O.mult, 17.5 / 32, O.add)
    tr(b3(X("fUT")), b3(X("fUX")))
    us = sums(b3(X("fUS")), b3(X("fUT")), 32)
    for d in range(4):
        cp(blk(X("UOo"), d), us)
    pick("MV", 32, 32, "UO", 0, 36, ("UOo", 0))
    total(X("fG2", 1, 2), ("fNM", 0, 32, 0, 128, 4), X("fJK", 8, 16))
    for a in range(4):
        for d in (a, a ^ 1):
            cp(blk(X("fGA", 2 * a, 2 * a + 2), d), blk(X("fG2"), a))
    cp(bot(X("fGA", 0, 4)), top(X("fGA", 0, 4)))
    cp(top(X("fGA", 4, 8)), bot(X("fGA", 4, 8)))
    c2k, c2g, o2k, o2g = (X("fGA", i, i + 1) for i in (1, 3, 5, 7))
    L2g, H2g = (X("fG4", i, i + 1) for i in range(2))
    dma("y", T.sw[0:1, :], ap(blk(D1g, 0)), [blk(D1g, 0)], [])
    dma("y", T.lw[0:1, :], ap(blk(L1g, 0)), [blk(L1g, 0)], [])
    ts(X("fOW", 0, 1), L1g, float(P * me), O.max, float(P * me + P - 1), O.min)
    ts(X("fOW", 1, 2), X("fOW", 0, 1), L1g, O.is_equal)
    times(X("fIDW"), X("fID"), X("fOW", 1, 2))
    for i, (c, lst) in enumerate(parts):
        times(X("fMW", 32 * i, 32 * i + 32), X("fMM", 32 * i, 32 * i + 32), (L1g, o2g, c2g)[lst])
    tr(X("fMX", 0, 32 * len(parts)), X("fMW", 0, 32 * len(parts)))
    for j in range(len(cols)):
        at = [i for i, (c, _) in enumerate(parts) if c == j]
        total(X("fOM", 4 + j, 5 + j), X("fMX", 32 * at[0], 32 * at[-1] + 32))
    ts(X("fOM", 0, len(cols)), X("fOM", 4, 4 + len(cols)), (P - 1) / 2, O.subtract, 1.0 / P, O.mult)
    cp(X("MI", 0, len(cols)), X("fOM", 0, len(cols)))
    for j, (n, col) in enumerate(cols):
        ts(X("Mo", col, col + 1), X("MI", j, j + 1), float(n), O.mult, PC(14) if col == 3 else P16, O.add)

    for b in range(4):
        mm("p%d" % (2 + b), 128, "EQ", 128 * b, "MV", 32, False, True)
    for b in range(4):
        cp(X("NT", b, 128, 0, 128, 4), X("p%d" % (2 + b), 0, 32))
    quant("QT", 320, 448, "NT", 0, 512)
    mm("p6", 128, "UQ", 0, "QT", 320)
    tt(X("fSC"), X("p6", 0, 32), X("fIDW"), O.mult)
    red(X("fNK", 4 * me, 4 * me + 1), X("fSC"), O.add, True, True)
    send1(3, "QT", 320)
    send_scores(2, X("fNK", 4 * me, 4 * me + 1), "fNK")
    if own2:
        pick("MG2", 0, 16 * -(-own2[0][2] // 16), "LD2", 0, 8 * own2[0][2], ("Mo", 2))
    send2(2)

    step = 2.0 ** -24

    def prep(w, ak, ag, bg):
        times(X("fME" + w, 0, 32), X("fON"), bg)
        tr(X("fMR" + w), X("fME" + w, 0, 32))
        for i, c in enumerate((ag, bg)):
            ts(X("fMG" + w, 32 * i, 32 * i + 32), X("fMR" + w), c, O.is_gt if w else O.is_le, -step, O.mult)
        ts(X("fME" + w, 32, 64), X("fMG" + w, 0, 32), 1.0, O.add, ak, O.mult)
        tr(X("fMK" + w), X("fME" + w, 32, 64))

    def ranks(w, bk):
        t, u, o = "fMT" + w, "fMU" + w, O.is_gt if w else O.is_ge
        ts(X(t, 0, 32), X("fMG" + w, 32, 64), 1.0, O.add, bk, O.mult)
        ts(X(t, 32, 64), X("fMK" + w), bk, o)
        for c0, c1 in ((0, 64),) if w else ((0, 32), (32, 64)):
            tr(X(u, c0, c1), X(t, c0, c1))
        ts(X(t, 64, 96), X(u, 0, 32), bk, o)
        total(X("fML" + w, 0, 1), X(u, 32, 64))
        total(X("fML" + w, 1, 2), X(t, 32, 96))

    def hot(w, at, wide, va, vb, out=None):
        h, ht = "fMH" + w, "fMI" + w
        n = 128 if wide else 64
        for i in range(n // 64):
            ra = X("fRP", 32 * i, 32 * i + 32) if wide else X("fRP", 64, 96)
            rb = X("fROW", 32 * i, 32 * i + 32) if wide else X("fR32")
            o = at + 64 * i
            ts(X(h, o, o + 32), ra, X("fML" + w, 0, 1), O.is_equal, va, O.mult)
            ts(X(h, o + 32, o + 64), rb, X("fML" + w, 1, 2), O.is_equal, vb, O.mult)
        tr(X(ht, at, at + n), X(h, at, at + n))
        if wide:
            return sums(X("fMJ" + w), X(ht, at, at + n), 64)
        total(out, X(ht, at, at + n))

    def match(out, tmp, t, x, v, nv):
        act(tmp, t, AF.Abs, x, -1.0)
        act(out, tmp, AF.Relu, v, nv)

    def final(i):
        tr(X("fFT%d" % i), X("fFH%d" % i))
        tt(X("fFL"), sums(X("fFS%d" % i), X("fFT%d" % i), 32), X("fFL") if i else X("fJB"), O.max)

    prep("", c2k, c2g, D1g)
    ranks("", z1)
    cp(X("B2o"), hot("", 0, True, a64, P32))
    prep("b", o2k, o2g, L1g)
    hot("", 128, False, c2g, D1g, H2g)
    dma("y", T.sw[1:2, :], ap(blk(H2g, 0)), [blk(H2g, 0)], [])
    G1, VA, VB = (X("fG5", i, i + 1) for i in range(3))
    for v, t, b in ((G1, L1g, D1g), (VA, o2g, a128), (VB, L1g, a192)):
        cp(top(v), top(t))
        cp(bot(v), bot(b))
    match(X("fFH0"), X("fFS1"), X("fPT"), G1, a320, n320)
    final(0)
    match(bot(X("fFH2")), bot(X("fFT1")), bot(X("fPT")), bot(H2g), 1.0, -1.0)
    pick("MV", 0, 32, "DW", 96, 192, ("B2o", 0))
    for b in range(4):
        mm("p%d" % (2 + b), 128, "EQ", 128 * b, "MV", 0)
        cp(X("fDB", 32 * b, 32 * b + 32), X("p%d" % (2 + b), 0, 32))

    red(X("fNB"), ("fNK", 0, 36, 0, 128, 4), O.min)
    ranks("b", X("fNB"))
    ts(X("N2o"), hot("b", 0, True, o2g, L1g), float(P * me), O.subtract, P - 1.0, O.min)
    for b in range(4):
        o, w, d = X("NT", b, 128, 0, 128, 4), X("fDN", 96 * b, 96 * b + 96), X("fDB", 32 * b, 32 * b + 32)
        op("v", lambda o=o, w=w, d=d: g.vector.tensor_tensor(ap(o), ap(w).indirect(T.N2o[:]), ap(d), O.add), [w, d, X("N2o")], [o], el(110))
    quant("QT", 448, 576, "NT", 0, 512)
    if own3:
        pick("MG3", 0, 16, "LD3", 0, 8 * own3[0][2], ("Mo", 0))
    send2(3)
    hot("b", 128, False, VA, VB, L2g)
    ts(top(X("fFH1")), top(X("fPT")), top(L2g), O.is_equal, top(a448), O.mult)
    times(bot(X("fFH1")), bot(X("fFH2")), bot(L2g))
    final(1)
    for h in (top, bot):
        cp(h(X("FLo")), top(X("fFL")))
    pick("LF", 32, 96, "QT", 0, 576, ("FLo", 0))
    mm("p7", 128, "WQ", 0, "LF", 0)
    cp(X("fY"), X("p7", 32, 128))
    dma("a", T.y[:], T.fY[:], [X("fY")], [])
    dma("y", T.lw[1:2, :], ap(blk(L2g, 0)), [blk(L2g, 0)], [])
    for h in (top, bot):
        cp(h(X("FDo")), bot(X("fFL")))
    pick("LF", 128, 96, "DW", 0, 224, ("FDo", 0))
    for h in range(2):
        dma("y", T.oc[:, 384 * h:384 * h + 384], _view(T, "LF", 32 + 96 * h, 128 + 96 * h), [X("LF", 32 + 96 * h, 128 + 96 * h)], [])
    for k in range(4):
        dma("y", T.osc[4 * k:4 * k + 4, :], T.LFs[32 * k:32 * k + 4, 32:224], [X("LFs", 32, 224)], [])
    schedule()
    cnt["ls"] = ls[0]
    for s in sorted(cnt):
        if waited["g"].get(s, 0) < cnt[s]:
            g.wait_ge(T.sem[s], cnt[s])
